import numpy as np, ml_dtypes
CORES = [35,38,43,46]
N = 4
BF = ml_dtypes.bfloat16
def f(rng, *shape):
    return (rng.standard_normal(shape, dtype=np.float32) * np.exp2(rng.integers(-2, 3, shape[:-1] + (1,)))).astype(BF)
def wide(rng, *shape):
    v = f(rng, *shape).astype(np.float32); k = shape[:-2] + (1, shape[-1])
    return (v * np.exp2(rng.integers(-6, 7, k)) * (rng.random(k) > 0.0625)).astype(BF)
def entries(a):
    return np.ascontiguousarray(a.T).reshape(-1)
def table(e):
    return np.ascontiguousarray(np.reshape(e, (-1, 16)).T).astype(np.int32)
def gentries(a):
    return np.ascontiguousarray(a.reshape(8, 16, -1).transpose(0, 2, 1)).reshape(8, -1)
def gtable(e):
    e = np.asarray(e); return np.ascontiguousarray(e.reshape(8, -1, 16).transpose(0, 2, 1)).reshape(128, -1).astype(np.int32)
GX, GY, GZ, P, S, CAP = 32, 32, 32, 8192, 4096, 256
B, NB, CELLS = P // 8, N * P // 8, (GX - 1) * (GY - 1) * (GZ - 1)
def coords(a):
    return np.ascontiguousarray(a.reshape(3, 16, -1).transpose(0, 2, 1)).reshape(3, -1)
def uncoords(v):
    return np.ascontiguousarray(v.reshape(3, -1, 16).transpose(0, 2, 1)).reshape(48, -1)
def corners(bm, c):
    g = np.arange(8)[:, None]; cx, cy, cz = c[0] + (g & 1), c[1] + (g >> 1 & 1), c[2] + (g >> 2)
    return bm[(cx >> 1) + (GX // 2) * ((cy >> 1) + (GY // 2) * (cz >> 1))] * 8 + (cx & 1) + 2 * (cy & 1) + 4 * (cz & 1)
def touch(bm, c):
    rk = corners(bm, c) // P
    return np.stack([(rk == q).any(axis=0) for q in range(N)])
def draw_map(rng):
    own = rng.permutation(np.repeat(np.arange(N), P // 512)).reshape(GZ // 8, GY // 8, GX // 8)
    own = np.repeat(np.repeat(np.repeat(own, 4, axis=0), 4, axis=1), 4, axis=2).reshape(-1); bm = np.zeros(NB, np.int64)
    for q in range(N): bm[own == q] = q * B + rng.permutation(B)
    return bm
def draw_cells(rng, t, r, first):
    c = rng.choice(np.flatnonzero(t[r] & (np.sum(t, axis=0) == 1)), S)
    m = np.concatenate([first, rng.integers(0, CELLS, rng.integers(N * CAP // 4, N * CAP // 2 + 1))]).astype(np.int64)
    far = t[:, m].copy(); far[r] = False
    m = m[((np.add.accumulate(far.astype(np.int64), axis=1) <= CAP) | ~far).all(axis=0)]; c[:len(m)] = m
    return rng.permutation(c)
def draw_go(rng, tc, r):
    e = []
    for q in range(N):
        a = np.flatnonzero(tc[q]) if q != r else np.zeros(0, np.int64); free = np.ones(S, bool); free[a] = False
        e.append(rng.permutation(np.concatenate([a, rng.permutation(np.flatnonzero(free))[:CAP - len(a)]])))
    return table(np.concatenate(e))
def draw_hit(rng, r, shape):
    q = (r + rng.integers(1, N, shape)) % N
    return np.where(rng.random(shape) < 0.5, rng.integers(0, S, shape), S + q * CAP + rng.integers(0, CAP, shape))
def draw(rng, kind):
    bm = draw_map(rng); cells = np.stack([a.reshape(-1) for a in np.meshgrid(np.arange(GX - 1), np.arange(GY - 1), np.arange(GZ - 1), indexing="ij")])
    t = touch(bm, cells); nt = np.sum(t, axis=0); pos, go, hit = [], [], []; z = rng.integers(0, N)
    for r in range(N):
        first = np.zeros(0, np.int64)
        if kind == "full":
            q = (r + 1) % N; first = rng.choice(np.flatnonzero(t[q] & (nt - t[q] - t[r] == 0)), CAP)
        if kind == "ends": first = np.array([0, CELLS - 1, (7 * (GY - 1) + 7) * (GZ - 1) + 7])
        c = draw_cells(rng, t, r, first); fr = rng.integers(0, 65536, (3, S)); h = draw_hit(rng, r, (8, P))
        if kind == "ends":
            fr = rng.choice(np.array([0, 1, 32768, 65535]), (3, S)); a, b = (1 if r == 0 else 0), (N - 2 if r == N - 1 else N - 1)
            edge = np.array([0, S - 1, S + a * CAP, S + a * CAP + CAP - 1, S + b * CAP, S + b * CAP + CAP - 1])
            for g in range(8): h[g, :6] = np.roll(edge, g); h[g, P - 6:] = np.roll(edge, -g)
        if kind == "alike":
            h[:, :P // 2] = draw_hit(rng, r, (1, P // 2)); h[:, P // 2:] = draw_hit(rng, r, (8, 1))
            if r == z: c = np.full(S, rng.choice(np.flatnonzero(t[r] & (nt == 1))))
        pos.append(uncoords((cells[:, c] + fr * 2.0 ** -16).astype(np.float32))); go.append(draw_go(rng, t[:, c], r)); hit.append(gtable(h))
    return {"pro": f(rng, N, 16, P), "bas": f(rng, N, 16, S), "pos": np.stack(pos), "alb": rng.random((N, 1, S), dtype=np.float32),
            "bmap": np.repeat(bm.reshape(1, 1, NB), N, axis=0).astype(np.int32), "go": np.stack(go), "hit": np.stack(hit)}
def setup_inputs(rng):
    return draw(rng, "")
def setup_inputs_full(rng):
    return draw(rng, "full")
def setup_inputs_ends(rng):
    d = draw(rng, "ends"); d["alb"] = np.where(rng.random((N, 1, S)) < 0.25, rng.integers(0, 2, (N, 1, S)), d["alb"]).astype(np.float32); return d
def setup_inputs_alike(rng):
    return draw(rng, "alike")
def setup_inputs_spread(rng):
    d = draw(rng, ""); d["pro"] = wide(rng, N, 16, P); d["bas"] = wide(rng, N, 16, S); return d
def check_inputs(d):
    bad = []
    try:
        x = np.stack([coords(a) for a in d["pos"]]); bm = d["bmap"].reshape(N, NB).astype(np.int64); e = np.stack([entries(a) for a in d["go"]]).reshape(N, N, CAP); h = np.stack([gentries(a) for a in d["hit"]])
        if not (np.isfinite(x).all() and (x >= 0).all() and (x < np.array([GX - 1, GY - 1, GZ - 1])[:, None]).all()): bad.append("pos")
        if not ((bm == bm[:1]).all() and np.array_equal(np.sort(bm[0]), np.arange(NB))): bad.append("bmap")
        if e.min() < 0 or e.max() >= S or (np.diff(np.sort(e, axis=2), axis=2) == 0).any(): bad.append("go")
        if h.min() < 0 or h.max() >= S + N * CAP or any(((h[r] >= S + r * CAP) & (h[r] < S + r * CAP + CAP)).any() for r in range(N)): bad.append("hit")
        if not all(np.isfinite(d[a].astype(np.float32)).all() for a in ("pro", "bas")): bad.append("finite")
        if not ((d["alb"] >= 0).all() and (d["alb"] <= 1).all()): bad.append("alb")
        if not bad:
            for r in range(N):
                t = touch(bm[0], np.floor(x[r]).astype(np.int64))
                for q in range(N):
                    if q != r and np.sum(t[q]) != np.sum(t[q, e[r, q]]) and "go_touch" not in bad: bad.append("go_touch")
    except Exception:
        bad.append("shape")
    return bad
def reference(pro, bas, pos, alb, bmap, go, hit):
    bm = bmap[0].reshape(-1).astype(np.int64); every = np.concatenate([a.astype(np.float64) for a in pro], axis=1); lit = np.zeros((N, 16, S), np.float64)
    for r in range(N):
        x = coords(pos[r]); c = np.floor(x).astype(np.int64); fr = (x - c.astype(np.float32)).astype(np.float64)
        num = corners(bm, c); b = bas[r].astype(np.float64); rad = np.zeros(S, np.float64)
        for g in range(8):
            w = (fr[0] if g & 1 else 1 - fr[0]) * (fr[1] if g & 2 else 1 - fr[1]) * (fr[2] if g & 4 else 1 - fr[2])
            rad += w * np.sum(every[:, num[g]] * b, axis=0)
        lit[r] = rad * alb[r, 0].astype(np.float64) * b
    y = np.zeros((N, 16, P), np.float64)
    for r in range(N):
        seen = np.concatenate([lit[r]] + [lit[q][:, entries(go[q])[r * CAP:(r + 1) * CAP]] for q in range(N)], axis=1); h = gentries(hit[r])
        for g in range(8): y[r] += seen[:, h[g]]
        y[r] = pro[r].astype(np.float64) + 0.125 * y[r]
    return {"y": y.astype(np.float32)}

@@ -1,0 +1,410 @@
+from concourse.bass import DstId, RemoteDMATransfer
+from concourse.mybir import AluOpType, ActivationFunctionType
+
+F32, BF, I32, U16 = "float32", "bfloat16", "int32", "uint16"
+N, S, P, CAP = 4, 4096, 8192, 256
+NG = (N - 1) * CAP
+MAGIC = 25165824.0
+PAR = {
+    "dense_v": 128,
+    "na": 24,
+    "v1": 24,
+    "order": "G012F3w4a5d6s7",
+    "deint_v": 4,
+}
+NAMAX = 32
+
+SB = {
+    "X": ([64, 2048], BF), "X2": ([64, 2048], BF), "W": ([128, 1056], BF), "WD": ([128, 4096], BF),
+    "BAS": ([128, S], BF), "BG": ([128, NG], BF), "BFO": ([128, NG], BF), "OG": ([128, 48], U16), "OF": ([128, 48], U16),
+    "POS": ([128, 256], F32), "P3": ([16, 1024], F32), "GBI": ([16, 304], I32), "GBF": ([16, 304], F32),
+    "DU": ([128, 256], U16), "GI": ([128, 48], I32), "GU": ([128, 48], U16), "CR": ([128, 96], I32), "CRU": ([128, 96], U16),
+    "ZL": ([128, 16], U16), "BT": ([128, 256], F32), "B2": ([128, 256], BF), "OU": ([128, 256], U16),
+    "MASK": ([128, NG], BF), "MX": ([128, NG], F32), "MB": ([128, NG], BF),
+    "T1": ([128, S + 2 * NG], F32), "DF": ([128, 48], F32), "RET": ([128, 3, 32], F32), "WG": ([128, 3, 32], F32),
+    "XS": ([128, 152], F32), "XT": ([128, 114], F32), "XY": ([128, 114], F32), "XD": ([128, 114], F32),
+    "FF": ([128, 228], F32), "FZ": ([128, 76], F32), "WXY": ([128, 152], F32), "WT": ([128, 304], F32),
+    "DG": ([128, 96], F32), "SG": ([128, 96], F32), "RG": ([128, 12], F32), "PG": ([128, 6, 32], BF),
+    "DW": ([128, 256], F32), "SC": ([128, 256], F32), "R1": ([128, 32], F32), "PC": ([128, 192], BF), "R": ([48, 1024], BF),
+    "ZIN": ([128, 256], BF), "Z": ([128, S], BF), "ZG": ([128, NG], BF), "ZF": ([128, NG], BF), "LIT": ([128, S + N * CAP], F32),
+    "HA": ([128, 512], I32), "HB": ([128, 512], I32), "HU": ([128, 512], U16),
+    "PRG": ([128, 1024], BF), "ACC": ([128, 1024], F32), "GA": ([128, 8 * 16 * NAMAX], F32),
+    "ONE": ([128, 256], F32), "SL": ([16, 240], F32), "REP": ([16, 128], F32), "I16": ([128, 16], I32), "I16B": ([128, 16], I32),
+    "ID16": ([128, 16], F32), "GS0": ([128, 8], F32), "GS": ([128, 8], F32), "EC": ([128, 16], F32),
+    "C0": ([128, 2, 4], F32), "C1": ([128, 8], F32), "C2": ([128, 8], F32), "FGO": ([128, 144], BF), "WB": ([128, 128], BF),
+    "IDF": ([128, 128], F32), "IDB": ([128, 128], BF), "SEL8": ([48, 1024], BF), "SELO": ([128, 512], BF), "KEEP": ([128, 128], F32),
+}
+SCRATCH = {k: ("sbuf", v[0], v[1]) for k, v in SB.items()}
+for _b in ("psA", "psB", "psC", "psD", "ps0", "ps1", "ps2", "ps3"):
+    SCRATCH[_b] = ("psum", [128, 512], F32)
+SEMAPHORES = ["V", "A", "P", "G", "dpro", "dgo", "dgb", "dpos", "dbas", "dp3", "dw", "dha", "dhb", "dprg", "dy",
+              "hop1", "hop2", "hop3", "sent1", "sent2", "sent3"]
+
+
+def split_engines(topo, core, dsts):
+    free = {d: list(topo.engines(core, d)) for d in dsts}
+    fewest = min(len(v) for v in free.values())
+    tight = [d for d in dsts if len(free[d]) == fewest]
+    n = 1
+    while 2 * n * len(tight) <= fewest:
+        n *= 2
+    used, masks = set(), {}
+    for d in sorted(dsts, key=lambda d: len(free[d])):
+        mine = [e for e in free[d] if e not in used][:n]
+        used.update(mine)
+        masks[d] = sum(1 << e for e in mine)
+    return masks, n
+
+
+def rank_program(g, core, T, topo):
+    r = T.rank_of(core)
+    if r is None:
+        return
+    others = [q for q in range(N) if q != r]
+    there = [[x for x in range(N) if x != q].index(r) for q in others]
+    cores = list(T.cores)
+    masks, neng = split_engines(topo, core, [cores[q] for q in others])
+    Q = {"V": g.vector, "A": g.scalar, "P": g.tensor, "G": g, "S": g.sync}
+    OP, FN = AluOpType, ActivationFunctionType
+    cnt, seen, state = {s: 0 for s in SEMAPHORES}, {}, {}
+
+    def wait(q, tok):
+        sem, val, src = tok
+        if q == "P" and src == "P":
+            return
+        val = cnt[sem] if val is None else val
+        if seen.get((q, sem), 0) < val:
+            Q[q].wait_ge(T.sem[sem], val)
+            seen[(q, sem)] = val
+
+    def before(q, reads, writes):
+        toks = []
+        for k in reads:
+            st = state.setdefault(k, {"w": [], "base": [], "r": []})
+            toks += st["w"]
+            if k.startswith("ps"):
+                toks += [t for t in st["r"] if t[2] != q]
+        for k in writes:
+            st = state.setdefault(k.lstrip("+"), {"w": [], "base": [], "r": []})
+            toks += (st["base"] if k[0] == "+" else st["w"]) + st["r"]
+        for t in sorted(toks, key=lambda t: -(t[1] or 0)):
+            wait(q, t)
+
+    def after(tok, reads, writes):
+        for k in reads:
+            state[k]["r"].append(tok)
+        for k in writes:
+            st = state[k.lstrip("+")]
+            if k[0] == "+":
+                st["w"].append(tok)
+            else:
+                st["w"], st["base"], st["r"] = [tok], [tok], []
+
+    def op(q, call, reads, writes):
+        before(q, reads, writes)
+        call().then_inc(T.sem[q], 1)
+        cnt[q] += 1
+        after((q, cnt[q], q), reads, writes)
+
+    def dma(q, sem, out, in_, reads, writes):
+        before(q, reads, writes)
+        Q[q].dma_start(out, in_).then_inc(T.sem[sem], 16)
+        cnt[sem] += 16
+        after((sem, None, "D"), reads, writes)
+
+    def send(hop, src, dst, width):
+        before("G", [src], [])
+
+        def dst_ap(j):
+            return T[dst][:, j, 0:width] if len(SB[dst][0]) == 3 else T[dst][:, width * j:width * j + width]
+        tr = []
+        for j, q in enumerate(others):
+            rid, pid, _ = topo.addr(cores[q])
+            tr.append(RemoteDMATransfer(dst_ids=[DstId(rid=rid, pnc=pid)], dma_engine_mask=masks[cores[q]], remote_sem=T.sem["hop" + hop],
+                                        src=T[src][:, width * j:width * j + width], dst=dst_ap(there[j])))
+        g.remote_dma_fused(tr, local_sem=T.sem["sent" + hop])
+        cnt["sent" + hop] += neng * len(others)
+        cnt["hop" + hop] += neng * len(others)
+        state.setdefault(dst, {"w": [], "base": [], "r": []})["w"].append(("hop" + hop, None, "D"))
+
+    V, A, PE = g.vector, g.scalar, g.tensor
+
+    def memset(ap, c, w):
+        op("V", lambda: V.memset(ap, c), [], w)
+
+    def copy(out, in_, rd, w):
+        op("V", lambda: V.tensor_copy(out, in_), rd, w)
+
+    def tt(out, a, b, o, rd, w):
+        op("V", lambda: V.tensor_tensor(out, a, b, o), rd, w)
+
+    def ts(out, a, s1, o0, rd, w, s2=None, o1=None):
+        if o1 is None:
+            op("V", lambda: V.tensor_scalar(out, a, s1, None, o0), rd, w)
+        else:
+            op("V", lambda: V.tensor_scalar(out, a, s1, s2, o0, o1), rd, w)
+
+    def scan(out, keep, data, rd, w):
+        op("V", lambda: V.tensor_tensor_scan(out, keep, data, 0.0, OP.mult, OP.add), rd, w)
+
+    def act(out, in_, rd, w, func=None, **kw):
+        plain = FN.Identity if kw else FN.Copy
+        op("A", lambda: A.activation(out, in_, plain if func is None else func, **kw), rd, w)
+
+    def mm(out, lhsT, rhs, rd, w, start=True, stop=True):
+        op("P", lambda: PE.matmul(out, lhsT, rhs, start, stop), rd, w)
+
+    def sel(out, in_, pat, cmp, base, cm, rd, w):
+        op("G", lambda: g.affine_select(out, in_, pat, cmp, 0.0, base, cm), rd, w)
+
+    def zero(out, n, w):
+        op("G", lambda: g.iota(out, [[0, n]], 0, 0, allow_small_or_imprecise_dtypes=True), [], w)
+
+    if r > 0:
+        dma("A", "dgo", T.GBI[:, 256:256 + 16 * r], T.go[:, 0:16 * r], [], ["+GOI"])
+    if r < N - 1:
+        dma("A", "dgo", T.GBI[:, 256 + 16 * r:304], T.go[:, 16 * r + 16:64], [], ["+GOI"])
+    dma("S", "dpro", T.X[:], T.pro[:], [], ["X"])
+    dma("S", "dgb", T.GBI[:, 0:256], T.bmap[:], [], ["+GBI"])
+    for e in range(2):
+        dma("AS"[e], "dpos", T.POS[48 * e:48 * e + 48, :], T.pos[:], [], ["+POS"])
+    for e in range(2):
+        dma("AS"[e], "dpos", T.POS[96 + 16 * e:112 + 16 * e, :], T.alb[:], [], ["+POS"])
+    for p in range(8):
+        dma("AS"[p % 2], "dbas", T.BAS[16 * p:16 * p + 16, :], T.bas[:], [], ["+BAS"])
+
+    memset(T.ONE[:], 1.0, ["ONE"])
+    op("G", lambda: g.iota(T.I16[:], [[-1, 16]], 16, 1), [], ["I16"])
+    sel(T.GS0[:], T.ONE[:, 0:8], [[-16, 8]], OP.is_ge, 0, 1, ["ONE"], ["GS0"])
+    sel(T.EC[:, 0:1], T.ONE[:, 0:1], [[0, 1]], OP.is_ge, -48, 1, ["ONE"], ["E1"])
+    sel(T.GS[:], T.GS0[:], [[16, 8]], OP.is_ge, 15, -1, ["GS0"], ["GS"])
+    sel(T.REP[:], T.ONE[0:16, 0:128], [[0, 8], [-1, 16]], OP.is_equal, 0, 1, ["ONE"], ["REP"])
+    sel(T.SL[:], T.ONE[0:16, 0:240], [[-1, 240]], OP.is_equal, 112, 1, ["ONE"], ["SL"])
+    zero(T.Z[:, 0:2048], 2048, ["+Z"])
+    memset(T.W[:, 0:16], 0.0, ["+W"])
+    memset(T.W[:, 1040:1056], 0.0, ["+W"])
+    memset(T.FGO[:], 0.0, ["FGO"])
+    ts(T.I16B[:], T.I16[:], 15, OP.bitwise_and, ["I16"], ["I16B"])
+    memset(T.PG[:], 0.0, ["PG"])
+    ts(T.ID16[:], T.I16B[:], 0.0, OP.is_equal, ["I16B"], ["ID16"])
+    memset(T.PC[:], 0.0, ["PC"])
+    for b in range(2):
+        ts(T.C0[:, :, 2 * b:2 * b + 2], T.ONE[:, 0:4], T.GS[:, 3 * b + 1:3 * b + 2], OP.mult, ["GS", "ONE"], ["+C0"])
+    memset(T.ZIN[96:128, :], 0.0, ["+ZIN"])
+    for b in range(2):
+        ts(T.C1[:, b:8:2], T.C0[:, :, b:4:2], 16.0, OP.mult, ["GS", "C0"], ["+C1"], T.GS[:, 3 * b:3 * b + 1], OP.add)
+    memset(T.LIT[:, S + CAP * r:S + CAP * r + CAP], 0.0, ["+LIT"])
+    for b in range(2):
+        ts(T.C2[:, 4 * b:4 * b + 4], T.C1[:, 4 * b:4 * b + 4], 16.0, OP.mult, ["GS", "C1"], ["+C2"], T.GS[:, 3 * b + 2:3 * b + 3], OP.add)
+    act(T.FGO[:, 15:128:16], T.C2[:], ["C2"], ["+FGO"])
+    for p in range(8):
+        act(T.WB[:, 16 * p:16 * p + 16], T.ID16[:], ["C2", "ID16"], ["+WB"], scale=T.C2[:, p:p + 1])
+
+    nv = PAR["deint_v"]
+
+    def apart(p):
+        (copy if p < nv else act)(T.X2[:, 256 * p:256 * p + 256], T.X[:, p:2048:8], ["X"], ["X2%d" % p])
+
+    copy(T.GBF[:, 256:304], T.GBI[:, 256:304], ["GOI"], ["GBG"])
+    mm(T.psD[:, 0:48], T.REP[:], T.GBF[:, 256:304], ["REP", "GBG"], ["+psD"])
+    for p in range(8):
+        apart(p)
+    for p in range(8):
+        dma("S" if p < nv else "A", "dw", T.W[16 * p:16 * p + 16, 16:1040], T.X2[:, 256 * p:256 * p + 256], ["X2%d" % p], ["+W"])
+    for a in range(3):
+        dma("S", "dp3", T.P3[:, 256 * a:256 * a + 256], T.pos[16 * a:16 * a + 16, :], [], ["+P3"])
+    dma("S", "dp3", T.P3[:, 768:1024], T.alb[:], [], ["+P3"])
+
+    copy(T.GI[:], T.psD[:, 0:48], ["psD"], ["GI"])
+    ts(T.BT[:], T.POS[:], T.EC[:, 0:1], OP.subtract, ["POS", "E1"], ["BT"], MAGIC, OP.add)
+    ts(T.CR[0:96, 48:96], T.GI[0:96, :], 15, OP.bitwise_and, ["GI"], ["+CR"])
+    ts(T.CR[96:128, 48:96], T.GI[96:128, :], 8, OP.arith_shift_right, ["GI"], ["+CR"])
+    ts(T.CR[0:96, 0:48], T.GI[0:96, :], 4, OP.arith_shift_right, ["GI"], ["+CR"])
+    ts(T.CR[96:128, 0:48], T.GI[96:128, :], 255, OP.bitwise_and, ["GI"], ["+CR"])
+    ts(T.B2[:], T.BT[:], MAGIC, OP.subtract, ["BT"], ["B2"], 0.5, OP.mult)
+    copy(T.CRU[:], T.CR[:], ["CR"], ["CRU"])
+    copy(T.GU[:], T.GI[:], ["GI"], ["GU"])
+    act(T.MASK[:], T.ID16[:, 0:16].indirect(T.CRU[:, 48:96]), ["ID16", "CRU"], ["MASK"])
+    act(T.BG[:], T.BAS[:, 0:S].indirect(T.GU[:, 0:48]), ["BAS", "GU"], ["BG"])
+    mm(T.psB[:, 0:256], T.WB[:], T.B2[:], ["WB", "B2"], ["+psB"])
+    ts(T.GBF[:, 0:256], T.GBI[:, 0:256], float(16 - 1024 * r), OP.add, ["GBI"], ["GBF"], 0.0, OP.max)
+    mm(T.psA[:, 0:256], T.REP[:], T.GBF[:, 0:256], ["REP", "GBF"], ["+psA"])
+    copy(T.OU[:], T.psB[:, 0:256], ["psB"], ["OU"])
+    for j, (lo, hi) in enumerate(((0, 32), (32, 64), (64, 128))):
+        copy(T.ZL[lo:hi, :], T.GI[lo:hi, 16 * j:16 * j + 16], ["GI"], ["+ZL"])
+    tt(T.MB[:], T.B2[:, 0:256].indirect(T.CRU[:, 0:48]), T.MASK[:], OP.mult, ["B2", "CRU", "MASK"], ["MB"])
+    for rho in range(16):
+        mm(T.psB[:, 256:304], T.FGO[:, 15 - rho:143 - rho], T.MB[:, rho:NG:16], ["FGO", "MB"], ["+psB"], rho == 0, rho == 15)
+    ts(T.DU[:], T.psA[:, 0:256], 1040.0, OP.min, ["psA"], ["DU"])
+    tt(T.MX[:, 0:256], T.POS[:, 0:256].indirect(T.CRU[:, 0:16]), T.MASK[:, 0:256], OP.mult, ["POS", "CRU", "MASK"], ["+MX"])
+    copy(T.OG[:], T.psB[:, 256:304], ["psB"], ["OG"])
+    tt(T.MX[:, 256:NG], T.POS[:, 0:256].indirect(T.CRU[:, 16:48]), T.MASK[:, 256:NG], OP.mult, ["POS", "CRU", "MASK"], ["+MX"])
+    for c8 in range(8):
+        mm(T.psC[:, 0:96], T.SL[:, 112 - 16 * c8:240 - 16 * c8], T.P3[:, c8:768:8], ["SL", "P3"], ["+psC"], c8 == 0, c8 == 7)
+    for h in range(2):
+        mm(T.psC[:, 96 + 16 * h:112 + 16 * h], T.P3[:, 768 + 128 * h:896 + 128 * h], T.SL[:, 112:128], ["SL", "P3"], ["+psC"])
+    for c in range(6):
+        mm(T.psC[:, 128 + 8 * c:136 + 8 * c], T.MX[:, 128 * c:128 * c + 128], T.GS[:], ["MX", "GS"], ["+psC"])
+
+    send("1", "BG", "BFO", CAP)
+    send("1", "OG", "OF", 16)
+    zero(T.Z[:, 2048:4096], 2048, ["+Z"])
+    sel(T.KEEP[:], T.ONE[:, 0:128], [[0, 16], [1, 8]], OP.not_equal, 0, 0, ["ONE"], ["KEEP"])
+    sel(T.IDB[:], T.ONE[:, 0:128], [[-1, 128]], OP.is_equal, 0, 1, ["ONE"], ["IDB"])
+
+    d = PAR["dense_v"]
+    copy(T.WD[:, 0:16 * d], T.W[:, 0:1056].indirect(T.DU[:, 0:d]), ["W", "DU"], ["+WD"])
+    act(T.WD[:, 16 * d:4096], T.W[:, 0:1056].indirect(T.DU[:, d:256]), ["W", "DU"], ["+WD"])
+
+    wait("S", ("sent1", None, "D"))
+    for k in range(8):
+        dma("S", "dha", T.HA[:, 64 * k:64 * k + 64], T.hit[16 * k:16 * k + 16, :], [], ["+HA"])
+    for k in range(8):
+        dma("S", "dhb", T.HB[16 * k:16 * k + 16, :], T.HA[k:128:8, :], ["HA"], ["+HB"])
+    wait("S", ("dhb", None, "D"))
+    for k in range(8):
+        dma("S", "dprg", T.PRG[16 * k:16 * k + 16, :], T.pro[:, 1024 * k:1024 * k + 1024], [], ["+PRG"])
+
+    def dots(col, n, off, bas, rd, bank, pcol):
+        key = "T1%d" % col
+        tt(T.T1[:, col:col + n], T.WD[:, 0:4096].indirect(off), bas, OP.mult, ["WD"] + rd, [key])
+        for c in range(n // 128):
+            mm(T[bank][:, pcol + 8 * c:pcol + 8 * c + 8], T.T1[:, col + 128 * c:col + 128 * c + 128], T.GS[:], [key, "GS"], ["+" + bank])
+
+    def pieces(v, hi, mid, lo, rest, src, dst, tmp, fill):
+        copy(hi, v, [src], ["+" + dst])
+        fill()
+        tt(rest, v, hi, OP.subtract, [src, dst], [tmp])
+        fill()
+        copy(mid, rest, [tmp], ["+" + dst + "m"])
+        fill()
+        tt(lo, rest, mid, OP.subtract, [tmp, dst + "m"], ["+" + dst + "l"])
+
+    for a in range(3):
+        act(T.XS[:, 38 * a:38 * a + 32], T.psC[:, 32 * a:32 * a + 32], ["psC"], ["+XS"])
+        act(T.XS[:, 38 * a + 32:38 * a + 38], T.psC[:, 128 + a:176:8], ["psC"], ["+XS"])
+    act(T.XT[:], T.XS[:, 0:114], ["XS", "EM"], ["XT"], bias=MAGIC)
+    for h in range(2):
+        act(T.XS[:, 114 + h:146:2], T.psC[:, 96 + 16 * h:112 + 16 * h], ["psC"], ["+AL"], scale=0.125)
+    act(T.XY[:], T.XT[:], ["XT", "EM"], ["XY"], bias=-MAGIC)
+    act(T.XS[:, 146:152], T.psC[:, 134:176:8], ["psC"], ["+AL"], scale=0.125)
+    selr = T.SELO[:, 384:512]
+    ring = ["ps0", "ps1", "ps2", "psD", "psA", "ps0", "ps1", "ps2"]
+
+    def f(a, e):
+        return T.FF[:, 114 * e + 38 * a:114 * e + 38 * a + 38]
+
+    def rad(h, fill):
+        bank, n = ("psA", "ps3")[h], "%d" % h
+        tt(T.DW[:, 128 * h:128 * h + 128], T[bank][:, 0:128], T.WT[:, 128 * h:128 * h + 128], OP.mult, [bank, "WT"], ["DW" + n])
+        fill()
+        scan(T.SC[:, 128 * h:128 * h + 128], T.KEEP[:], T.DW[:, 128 * h:128 * h + 128], ["KEEP", "DW" + n], ["SC" + n])
+        fill()
+        c = 16 * h
+        pieces(T.SC[:, 128 * h + 7:128 * h + 128:8], T.PC[:, c:c + 16], T.PC[:, 64 + c:80 + c], T.PC[:, 128 + c:144 + c], T.R1[:, c:c + 16],
+               "SC" + n, "PC", "R1" + n, fill)
+        for u in range(4):
+            mm(T.psC[0:48, 128 * u:128 * u + 128], T.PC[:, u:192:4], T.IDB[:], ["PC", "PCm", "PCl", "IDB"], ["+psC"])
+        act(T.R[:, 512 * h:512 * h + 512], T.psC[0:48, :], ["psC"], ["R" + n])
+
+    def spread(t):
+        h = t // 4
+        mm(T[ring[t]][:], selr, T.Z[:, 512 * t:512 * t + 512], ["SELO", "Z"], ["+" + ring[t]], True, False)
+        mm(T[ring[t]][:], T.SEL8[:, 128 * t:128 * t + 128], T.R[:, 512 * h:512 * h + 512], ["SEL8", "R%d" % h], ["+" + ring[t]], False, True)
+
+    def lit(c0, n):
+        bank = ring[c0 // 512]
+        tt(T.LIT[:, c0:c0 + n], T[bank][:, c0 % 512:c0 % 512 + n], T.BAS[:, c0:c0 + n], OP.mult, [bank, "BAS"], ["+LIT"])
+
+    def step(c):
+        if c.isdigit():
+            k = int(c)
+            dots(512 * k, 512, T.OU[:, 32 * k:32 * k + 32], T.BAS[:, 512 * k:512 * k + 512], ["OU", "BAS"], ("psA", "ps3")[k // 4], 32 * (k % 4))
+        if c == "G":
+            dots(S, NG, T.OG[:, 0:48], T.BG[:], ["OG", "BG"], "psD", 256)
+            tt(T.XD[:], T.XS[:, 0:114], T.XY[:], OP.subtract, ["XS", "XY"], ["XD"])
+            act(T.FF[:, 114:228], T.XD[:], ["XD"], ["F1"], FN.Abs)
+            act(T.FF[:, 0:114], T.FF[:, 114:228], ["F1"], ["F0"], bias=1.0, scale=-1.0)
+            act(T.RET[:, :, 16:32], T.psD[:, 256:304], ["psD"], ["+RET"])
+            act(T.EC[:, 4:5], T.GS[:, 0:1], ["GS"], ["Ea"], bias=T.GS[:, 2:3])
+            for t in range(8):
+                act(T.SEL8[:, 128 * t:128 * t + 128], T.ONE[0:48, 0:128], ["ONE", "ID16"], ["+SEL8"], scale=T.ID16[0:48, t:t + 1])
+            act(T.EC[:, 8:9], T.GS[:, 4:5], ["GS", "Ea"], ["Eb"], bias=T.EC[:, 4:5])
+        if c == "F":
+            dots(S + NG, NG, T.OF[:, 0:48], T.BFO[:], ["OF", "BFO"], "psB", 0)
+            act(T.DF[:], T.psB[:, 0:48], ["psB"], ["DF"])
+            send("2", "DF", "RET", 16)
+            sel(T.IDF[:], T.ONE[:, 0:128], [[-1, 128]], OP.is_equal, 0, 1, ["ONE"], ["IDF"])
+            act(selr, T.ONE[:, 0:128], ["ONE", "Eb"], ["+SELO"], scale=T.EC[:, 8:9])
+            for j in range(3):
+                act(T.SELO[:, 128 * j:128 * j + 128], T.ONE[:, 0:128], ["ONE", "GS", "Eb"], ["+SELO"],
+                    scale=T.GS[:, 2 * there[j] + 1:2 * there[j] + 2], bias=T.EC[:, 8:9])
+        if c == "w":
+            for e in range(2):
+                tt(T.FZ[:, 38 * e:38 * e + 38], f(2, e), T.XS[:, 114:152], OP.mult, ["F0", "F1", "AL"], ["+FZ"])
+            for x in range(4):
+                tt(T.WXY[:, 38 * x:38 * x + 38], f(0, x & 1), f(1, x >> 1), OP.mult, ["F0", "F1"], ["+WXY"])
+            for p in range(8):
+                tt(T.WT[:, p:304:8], T.WXY[:, 38 * (p & 3):38 * (p & 3) + 38], T.FZ[:, 38 * (p >> 2):38 * (p >> 2) + 38], OP.mult,
+                   ["WXY", "FZ"], ["+WT"])
+            for x in range(2):
+                act(T.WG[:, :, 16 * x:16 * x + 16], T.WT[:, 256:304], ["WT"], ["+WG"])
+        if c == "a":
+            rad(0, lambda: None)
+        if c == "d":
+            tt(T.DG[:], T.RET[:], T.WG[:], OP.mult, ["RET", "WG"], ["DG"])
+            scan(T.SG[:], T.KEEP[:, 0:96], T.DG[:], ["KEEP", "DG"], ["SG"])
+            pieces(T.SG[:, 7:96:8], T.PG[:, :, 0:2], T.PG[:, :, 2:4], T.PG[:, :, 4:6], T.RG[:], "SG", "PG", "RG", lambda: None)
+            for t2 in range(2):
+                mm(T.psD[0:96, 128 * t2:128 * t2 + 128], T.PG[:, :, t2:32:2], T.IDB[:], ["PG", "PGm", "PGl", "IDB"], ["+psD"])
+            act(T.ZIN[0:96, :], T.psD[0:96, 0:256], ["psD"], ["+ZIN"])
+        if c == "s":
+            copy(T.Z[:, 0:S].indirect(T.ZL[:, 0:16]), T.ZIN[:], ["ZL", "ZIN"], ["Z"])
+            act(T.ZG[:], T.Z[:, 0:S].indirect(T.GU[:, 0:48]), ["Z", "GU"], ["ZG"])
+            send("3", "ZG", "ZF", CAP)
+            for t in range(2):
+                spread(t)
+
+    for c in PAR["order"]:
+        step(c)
+    for t in range(2, 4):
+        spread(t)
+    todo = [(0, 512), (512, 256), (768, 256), (1024, 256), (1280, 256), (1536, 256)]
+    lit(*todo.pop(0))
+    rad(1, lambda: lit(*todo.pop(0)))
+    copy(T.HU[:], T.HB[:], ["HB"], ["HU"])
+    lit(1792, 256)
+    for t in range(4, 8):
+        spread(t)
+        lit(512 * t, 512)
+    for j, q in enumerate(others):
+        bank = ("psD", "ps3", "psC")[j]
+        mm(T[bank][:, 0:256], T.SELO[:, 128 * j:128 * j + 128], T.ZF[:, 256 * j:256 * j + 256], ["SELO", "ZF"], ["+" + bank])
+        tt(T.LIT[:, S + CAP * q:S + CAP * q + CAP], T[bank][:, 0:256], T.BFO[:, 256 * j:256 * j + 256], OP.mult, [bank, "BFO"], ["+LIT"])
+
+    win = T.LIT[:, 0:S + N * CAP]
+    nc, v1 = PAR["na"], PAR["v1"]
+    na, c0 = 16 * nc, 1024 - 16 * nc
+    mm(T.psB[:, 0:na], T.IDB[:], T.PRG[:, c0:1024], ["IDB", "PRG"], ["+psB"], True, False)
+
+    def vpart(a, b, key):
+        for k in range(8):
+            src = T.PRG if k == 0 else T.ACC
+            tt(T.ACC[:, 16 * a:16 * b], win.indirect(T.HU[:, 64 * k + a:64 * k + b]), src[:, 16 * a:16 * b], OP.add,
+               ["LIT", "HU", "PRG"] + ([key] if k else []), [key])
+
+    def store(lo, hi, keys, queues):
+        for k in range(8):
+            dma(queues[k % len(queues)], "dy", T.y[:, 1024 * k + lo:1024 * k + hi], T.ACC[16 * k:16 * k + 16, lo:hi], keys, [])
+
+    for k in range(8):
+        act(T.GA[:, na * k:na * k + na], win.indirect(T.HU[:, 64 * k + 64 - nc:64 * k + 64]), ["LIT", "HU"], ["GA%d" % k])
+        mm(T.psB[:, 0:na], T.IDF[:], T.GA[:, na * k:na * k + na], ["IDF", "GA%d" % k], ["+psB"], False, k == 7)
+    vpart(0, v1, "ACCa")
+    store(0, 16 * v1, ["ACCa"], "S")
+    act(T.ACC[:, c0:1024], T.psB[:, 0:na], ["psB"], ["ACCc"])
+    vpart(v1, 64 - nc, "ACCb")
+    store(16 * v1, 1024, ["ACCb", "ACCc"], "SA")
+
+    for s in SEMAPHORES:
+        wait("G" if s.startswith("sent") else "S", (s, None, "D"))

@@ -5,13 +5,7 @@ F32, BF, I32, U16 = "float32", "bfloat16", "int32", "uint16"
 N, S, P, CAP = 4, 4096, 8192, 256
 NG = (N - 1) * CAP
 MAGIC = 25165824.0
-PAR = {
-    "dense_v": 128,
-    "na": 24,
-    "v1": 24,
-    "order": "G012F3w4a5d6s7",
-    "deint_v": 4,
-}
+PAR = {"dense_v": 120, "na": 26, "v1": 28, "n2": 8, "ev": 4, "order": "G4x4wF44W44b4s4", "deint_v": 5}
 NAMAX = 32
 
 SB = {
@@ -19,8 +13,8 @@ SB = {
     "BAS": ([128, S], BF), "BG": ([128, NG], BF), "BFO": ([128, NG], BF), "OG": ([128, 48], U16), "OF": ([128, 48], U16),
     "POS": ([128, 256], F32), "P3": ([16, 1024], F32), "GBI": ([16, 304], I32), "GBF": ([16, 304], F32),
     "DU": ([128, 256], U16), "GI": ([128, 48], I32), "GU": ([128, 48], U16), "CR": ([128, 96], I32), "CRU": ([128, 96], U16),
-    "ZL": ([128, 16], U16), "BT": ([128, 256], F32), "B2": ([128, 256], BF), "OU": ([128, 256], U16),
-    "MASK": ([128, NG], BF), "MX": ([128, NG], F32), "MB": ([128, NG], BF),
+    "ZL": ([128, 16], U16), "BT": ([128, 256], F32), "BU": ([128, 256], F32), "B2": ([128, 256], BF), "OU": ([128, 256], U16),
+    "MASK": ([128, NG], BF), "MX": ([128, NG], F32), "MB": ([128, NG], BF), "EA": ([128, 304], F32), "EB": ([128, 304], F32),
     "T1": ([128, S + 2 * NG], F32), "DF": ([128, 48], F32), "RET": ([128, 3, 32], F32), "WG": ([128, 3, 32], F32),
     "XS": ([128, 152], F32), "XT": ([128, 114], F32), "XY": ([128, 114], F32), "XD": ([128, 114], F32),
     "FF": ([128, 228], F32), "FZ": ([128, 76], F32), "WXY": ([128, 152], F32), "WT": ([128, 304], F32),
@@ -37,7 +31,7 @@ SB = {
 SCRATCH = {k: ("sbuf", v[0], v[1]) for k, v in SB.items()}
 for _b in ("psA", "psB", "psC", "psD", "ps0", "ps1", "ps2", "ps3"):
     SCRATCH[_b] = ("psum", [128, 512], F32)
-SEMAPHORES = ["V", "A", "P", "G", "dpro", "dgo", "dgb", "dpos", "dbas", "dp3", "dw", "dha", "dhb", "dprg", "dy",
+SEMAPHORES = ["V", "A", "P", "G", "dpro", "dgo", "dgb", "dpos", "dbas", "dp3", "dw", "dha", "dhb", "dprg", "dzl", "dy",
               "hop1", "hop2", "hop3", "sent1", "sent2", "sent3"]
 
 
@@ -172,6 +166,9 @@ def rank_program(g, core, T, topo):
         dma("AS"[e], "dpos", T.POS[96 + 16 * e:112 + 16 * e, :], T.alb[:], [], ["+POS"])
     for p in range(8):
         dma("AS"[p % 2], "dbas", T.BAS[16 * p:16 * p + 16, :], T.bas[:], [], ["+BAS"])
+    for a in range(3):
+        dma("S", "dp3", T.P3[:, 256 * a:256 * a + 256], T.pos[16 * a:16 * a + 16, :], [], ["+P3"])
+    dma("S", "dp3", T.P3[:, 768:1024], T.alb[:], [], ["+P3"])
 
     memset(T.ONE[:], 1.0, ["ONE"])
     op("G", lambda: g.iota(T.I16[:], [[-1, 16]], 16, 1), [], ["I16"])
@@ -197,41 +194,33 @@ def rank_program(g, core, T, topo):
     for b in range(2):
         ts(T.C2[:, 4 * b:4 * b + 4], T.C1[:, 4 * b:4 * b + 4], 16.0, OP.mult, ["GS", "C1"], ["+C2"], T.GS[:, 3 * b + 2:3 * b + 3], OP.add)
     act(T.FGO[:, 15:128:16], T.C2[:], ["C2"], ["+FGO"])
-    for p in range(8):
-        act(T.WB[:, 16 * p:16 * p + 16], T.ID16[:], ["C2", "ID16"], ["+WB"], scale=T.C2[:, p:p + 1])
 
     nv = PAR["deint_v"]
-
-    def apart(p):
-        (copy if p < nv else act)(T.X2[:, 256 * p:256 * p + 256], T.X[:, p:2048:8], ["X"], ["X2%d" % p])
-
     copy(T.GBF[:, 256:304], T.GBI[:, 256:304], ["GOI"], ["GBG"])
     mm(T.psD[:, 0:48], T.REP[:], T.GBF[:, 256:304], ["REP", "GBG"], ["+psD"])
     for p in range(8):
-        apart(p)
+        (copy if p < nv else act)(T.X2[:, 256 * p:256 * p + 256], T.X[:, p:2048:8], ["X"], ["X2%d" % p])
     for p in range(8):
         dma("S" if p < nv else "A", "dw", T.W[16 * p:16 * p + 16, 16:1040], T.X2[:, 256 * p:256 * p + 256], ["X2%d" % p], ["+W"])
-    for a in range(3):
-        dma("S", "dp3", T.P3[:, 256 * a:256 * a + 256], T.pos[16 * a:16 * a + 16, :], [], ["+P3"])
-    dma("S", "dp3", T.P3[:, 768:1024], T.alb[:], [], ["+P3"])
 
     copy(T.GI[:], T.psD[:, 0:48], ["psD"], ["GI"])
-    ts(T.BT[:], T.POS[:], T.EC[:, 0:1], OP.subtract, ["POS", "E1"], ["BT"], MAGIC, OP.add)
+    act(T.BT[:], T.POS[:], ["POS", "E1"], ["BT"], scale=-1.0, bias=T.EC[:, 0:1])
+    act(T.BU[:], T.BT[:], ["BT"], ["BU"], scale=-1.0, bias=MAGIC)
+    act(T.B2[:], T.BU[:], ["BU"], ["B2"], scale=0.5, bias=-0.5 * MAGIC)
     ts(T.CR[0:96, 48:96], T.GI[0:96, :], 15, OP.bitwise_and, ["GI"], ["+CR"])
     ts(T.CR[96:128, 48:96], T.GI[96:128, :], 8, OP.arith_shift_right, ["GI"], ["+CR"])
     ts(T.CR[0:96, 0:48], T.GI[0:96, :], 4, OP.arith_shift_right, ["GI"], ["+CR"])
     ts(T.CR[96:128, 0:48], T.GI[96:128, :], 255, OP.bitwise_and, ["GI"], ["+CR"])
-    ts(T.B2[:], T.BT[:], MAGIC, OP.subtract, ["BT"], ["B2"], 0.5, OP.mult)
     copy(T.CRU[:], T.CR[:], ["CR"], ["CRU"])
     copy(T.GU[:], T.GI[:], ["GI"], ["GU"])
-    act(T.MASK[:], T.ID16[:, 0:16].indirect(T.CRU[:, 48:96]), ["ID16", "CRU"], ["MASK"])
+    copy(T.MASK[:], T.ID16[:, 0:16].indirect(T.CRU[:, 48:96]), ["ID16", "CRU"], ["MASK"])
+    for p in range(8):
+        act(T.WB[:, 16 * p:16 * p + 16], T.ID16[:], ["C2", "ID16"], ["+WB"], scale=T.C2[:, p:p + 1])
     act(T.BG[:], T.BAS[:, 0:S].indirect(T.GU[:, 0:48]), ["BAS", "GU"], ["BG"])
-    mm(T.psB[:, 0:256], T.WB[:], T.B2[:], ["WB", "B2"], ["+psB"])
     ts(T.GBF[:, 0:256], T.GBI[:, 0:256], float(16 - 1024 * r), OP.add, ["GBI"], ["GBF"], 0.0, OP.max)
     mm(T.psA[:, 0:256], T.REP[:], T.GBF[:, 0:256], ["REP", "GBF"], ["+psA"])
-    copy(T.OU[:], T.psB[:, 0:256], ["psB"], ["OU"])
     for j, (lo, hi) in enumerate(((0, 32), (32, 64), (64, 128))):
-        copy(T.ZL[lo:hi, :], T.GI[lo:hi, 16 * j:16 * j + 16], ["GI"], ["+ZL"])
+        dma("S", "dzl", T.ZL[lo:hi, :], T.GU[lo:hi, 16 * j:16 * j + 16], ["GU"], ["+ZL"])
     tt(T.MB[:], T.B2[:, 0:256].indirect(T.CRU[:, 0:48]), T.MASK[:], OP.mult, ["B2", "CRU", "MASK"], ["MB"])
     for rho in range(16):
         mm(T.psB[:, 256:304], T.FGO[:, 15 - rho:143 - rho], T.MB[:, rho:NG:16], ["FGO", "MB"], ["+psB"], rho == 0, rho == 15)
@@ -239,6 +228,7 @@ def rank_program(g, core, T, topo):
     tt(T.MX[:, 0:256], T.POS[:, 0:256].indirect(T.CRU[:, 0:16]), T.MASK[:, 0:256], OP.mult, ["POS", "CRU", "MASK"], ["+MX"])
     copy(T.OG[:], T.psB[:, 256:304], ["psB"], ["OG"])
     tt(T.MX[:, 256:NG], T.POS[:, 0:256].indirect(T.CRU[:, 16:48]), T.MASK[:, 256:NG], OP.mult, ["POS", "CRU", "MASK"], ["+MX"])
+    mm(T.ps0[:, 0:256], T.WB[:], T.B2[:], ["WB", "B2"], ["+ps0"])
     for c8 in range(8):
         mm(T.psC[:, 0:96], T.SL[:, 112 - 16 * c8:240 - 16 * c8], T.P3[:, c8:768:8], ["SL", "P3"], ["+psC"], c8 == 0, c8 == 7)
     for h in range(2):
@@ -254,6 +244,7 @@ def rank_program(g, core, T, topo):
 
     d = PAR["dense_v"]
     copy(T.WD[:, 0:16 * d], T.W[:, 0:1056].indirect(T.DU[:, 0:d]), ["W", "DU"], ["+WD"])
+    copy(T.OU[:], T.ps0[:, 0:256], ["ps0"], ["OU"])
     act(T.WD[:, 16 * d:4096], T.W[:, 0:1056].indirect(T.DU[:, d:256]), ["W", "DU"], ["+WD"])
 
     wait("S", ("sent1", None, "D"))
@@ -271,22 +262,13 @@ def rank_program(g, core, T, topo):
         for c in range(n // 128):
             mm(T[bank][:, pcol + 8 * c:pcol + 8 * c + 8], T.T1[:, col + 128 * c:col + 128 * c + 128], T.GS[:], [key, "GS"], ["+" + bank])
 
-    def pieces(v, hi, mid, lo, rest, src, dst, tmp, fill):
-        copy(hi, v, [src], ["+" + dst])
-        fill()
-        tt(rest, v, hi, OP.subtract, [src, dst], [tmp])
-        fill()
-        copy(mid, rest, [tmp], ["+" + dst + "m"])
-        fill()
-        tt(lo, rest, mid, OP.subtract, [tmp, dst + "m"], ["+" + dst + "l"])
-
     for a in range(3):
         act(T.XS[:, 38 * a:38 * a + 32], T.psC[:, 32 * a:32 * a + 32], ["psC"], ["+XS"])
         act(T.XS[:, 38 * a + 32:38 * a + 38], T.psC[:, 128 + a:176:8], ["psC"], ["+XS"])
-    act(T.XT[:], T.XS[:, 0:114], ["XS", "EM"], ["XT"], bias=MAGIC)
+    act(T.XT[:], T.XS[:, 0:114], ["XS"], ["XT"], bias=MAGIC)
     for h in range(2):
         act(T.XS[:, 114 + h:146:2], T.psC[:, 96 + 16 * h:112 + 16 * h], ["psC"], ["+AL"], scale=0.125)
-    act(T.XY[:], T.XT[:], ["XT", "EM"], ["XY"], bias=-MAGIC)
+    act(T.XY[:], T.XT[:], ["XT"], ["XY"], bias=-MAGIC)
     act(T.XS[:, 146:152], T.psC[:, 134:176:8], ["psC"], ["+AL"], scale=0.125)
     selr = T.SELO[:, 384:512]
     ring = ["ps0", "ps1", "ps2", "psD", "psA", "ps0", "ps1", "ps2"]
@@ -295,14 +277,20 @@ def rank_program(g, core, T, topo):
         return T.FF[:, 114 * e + 38 * a:114 * e + 38 * a + 38]
 
     def rad(h, fill):
-        bank, n = ("psA", "ps3")[h], "%d" % h
+        bank, n, c = ("psA", "ps3")[h], "%d" % h, 16 * h
         tt(T.DW[:, 128 * h:128 * h + 128], T[bank][:, 0:128], T.WT[:, 128 * h:128 * h + 128], OP.mult, [bank, "WT"], ["DW" + n])
         fill()
         scan(T.SC[:, 128 * h:128 * h + 128], T.KEEP[:], T.DW[:, 128 * h:128 * h + 128], ["KEEP", "DW" + n], ["SC" + n])
         fill()
-        c = 16 * h
-        pieces(T.SC[:, 128 * h + 7:128 * h + 128:8], T.PC[:, c:c + 16], T.PC[:, 64 + c:80 + c], T.PC[:, 128 + c:144 + c], T.R1[:, c:c + 16],
-               "SC" + n, "PC", "R1" + n, fill)
+        v, rest = T.SC[:, 128 * h + 7:128 * h + 128:8], T.R1[:, c:c + 16]
+        hi, mid, lo = T.PC[:, c:c + 16], T.PC[:, 64 + c:80 + c], T.PC[:, 128 + c:144 + c]
+        copy(hi, v, ["SC" + n], ["+PC"])
+        fill()
+        tt(rest, v, hi, OP.subtract, ["SC" + n, "PC"], ["R1" + n])
+        fill()
+        copy(mid, rest, ["R1" + n], ["+PCm"])
+        fill()
+        tt(lo, rest, mid, OP.subtract, ["R1" + n, "PCm"], ["+PCl"])
         for u in range(4):
             mm(T.psC[0:48, 128 * u:128 * u + 128], T.PC[:, u:192:4], T.IDB[:], ["PC", "PCm", "PCl", "IDB"], ["+psC"])
         act(T.R[:, 512 * h:512 * h + 512], T.psC[0:48, :], ["psC"], ["R" + n])
@@ -316,22 +304,26 @@ def rank_program(g, core, T, topo):
         bank = ring[c0 // 512]
         tt(T.LIT[:, c0:c0 + n], T[bank][:, c0 % 512:c0 % 512 + n], T.BAS[:, c0:c0 + n], OP.mult, [bank, "BAS"], ["+LIT"])
 
+    done = [0]
+
     def step(c):
         if c.isdigit():
-            k = int(c)
-            dots(512 * k, 512, T.OU[:, 32 * k:32 * k + 32], T.BAS[:, 512 * k:512 * k + 512], ["OU", "BAS"], ("psA", "ps3")[k // 4], 32 * (k % 4))
+            t, n = done[0], int(c)
+            dots(128 * t, 128 * n, T.OU[:, 8 * t:8 * t + 8 * n], T.BAS[:, 128 * t:128 * t + 128 * n], ["OU", "BAS"],
+                 ("psA", "ps3")[t // 16], 8 * (t % 16))
+            done[0] = t + n
         if c == "G":
             dots(S, NG, T.OG[:, 0:48], T.BG[:], ["OG", "BG"], "psD", 256)
+        if c == "x":
             tt(T.XD[:], T.XS[:, 0:114], T.XY[:], OP.subtract, ["XS", "XY"], ["XD"])
             act(T.FF[:, 114:228], T.XD[:], ["XD"], ["F1"], FN.Abs)
             act(T.FF[:, 0:114], T.FF[:, 114:228], ["F1"], ["F0"], bias=1.0, scale=-1.0)
             act(T.RET[:, :, 16:32], T.psD[:, 256:304], ["psD"], ["+RET"])
             act(T.EC[:, 4:5], T.GS[:, 0:1], ["GS"], ["Ea"], bias=T.GS[:, 2:3])
-            for t in range(8):
-                act(T.SEL8[:, 128 * t:128 * t + 128], T.ONE[0:48, 0:128], ["ONE", "ID16"], ["+SEL8"], scale=T.ID16[0:48, t:t + 1])
             act(T.EC[:, 8:9], T.GS[:, 4:5], ["GS", "Ea"], ["Eb"], bias=T.EC[:, 4:5])
         if c == "F":
-            dots(S + NG, NG, T.OF[:, 0:48], T.BFO[:], ["OF", "BFO"], "psB", 0)
+            for lo, hi in ((0, 4), (4, 6)):
+                dots(S + NG + 128 * lo, 128 * (hi - lo), T.OF[:, 8 * lo:8 * hi], T.BFO[:, 128 * lo:128 * hi], ["OF", "BFO"], "psB", 8 * lo)
             act(T.DF[:], T.psB[:, 0:48], ["psB"], ["DF"])
             send("2", "DF", "RET", 16)
             sel(T.IDF[:], T.ONE[:, 0:128], [[-1, 128]], OP.is_equal, 0, 1, ["ONE"], ["IDF"])
@@ -345,16 +337,25 @@ def rank_program(g, core, T, topo):
             for x in range(4):
                 tt(T.WXY[:, 38 * x:38 * x + 38], f(0, x & 1), f(1, x >> 1), OP.mult, ["F0", "F1"], ["+WXY"])
             for p in range(8):
-                tt(T.WT[:, p:304:8], T.WXY[:, 38 * (p & 3):38 * (p & 3) + 38], T.FZ[:, 38 * (p >> 2):38 * (p >> 2) + 38], OP.mult,
-                   ["WXY", "FZ"], ["+WT"])
+                act(T.EA[:, p:304:8], T.FZ[:, 38 * (p >> 2):38 * (p >> 2) + 38], ["FZ"], ["+EA"])
+            for p in range(8):
+                act(T.EB[:, p:304:8], T.WXY[:, 38 * (p & 3):38 * (p & 3) + 38], ["WXY"], ["+EB"])
+        if c == "W":
+            tt(T.WT[:], T.EA[:], T.EB[:], OP.mult, ["EA", "EB"], ["WT"])
             for x in range(2):
                 act(T.WG[:, :, 16 * x:16 * x + 16], T.WT[:, 256:304], ["WT"], ["+WG"])
-        if c == "a":
-            rad(0, lambda: None)
-        if c == "d":
+            for t in range(8):
+                act(T.SEL8[:, 128 * t:128 * t + 128], T.ONE[0:48, 0:128], ["ONE", "ID16"], ["+SEL8"], scale=T.ID16[0:48, t:t + 1])
+        if c == "b":
+            v, hi, mid, lo = T.SG[:, 7:96:8], T.PG[:, :, 0:2], T.PG[:, :, 2:4], T.PG[:, :, 4:6]
+            steps = [lambda: scan(T.SG[:], T.KEEP[:, 0:96], T.DG[:], ["KEEP", "DG"], ["SG"]),
+                     lambda: copy(hi, v, ["SG"], ["+PG"]),
+                     lambda: tt(T.RG[:], v, hi, OP.subtract, ["SG", "PG"], ["RG"]),
+                     lambda: copy(mid, T.RG[:], ["RG"], ["+PGm"]),
+                     lambda: (tt(lo, T.RG[:], mid, OP.subtract, ["RG", "PGm"], ["+PGl"]), step("z"))]
             tt(T.DG[:], T.RET[:], T.WG[:], OP.mult, ["RET", "WG"], ["DG"])
-            scan(T.SG[:], T.KEEP[:, 0:96], T.DG[:], ["KEEP", "DG"], ["SG"])
-            pieces(T.SG[:, 7:96:8], T.PG[:, :, 0:2], T.PG[:, :, 2:4], T.PG[:, :, 4:6], T.RG[:], "SG", "PG", "RG", lambda: None)
+            rad(0, lambda: steps.pop(0)())
+        if c == "z":
             for t2 in range(2):
                 mm(T.psD[0:96, 128 * t2:128 * t2 + 128], T.PG[:, :, t2:32:2], T.IDB[:], ["PG", "PGm", "PGl", "IDB"], ["+psD"])
             act(T.ZIN[0:96, :], T.psD[0:96, 0:256], ["psD"], ["+ZIN"])
@@ -372,8 +373,8 @@ def rank_program(g, core, T, topo):
     todo = [(0, 512), (512, 256), (768, 256), (1024, 256), (1280, 256), (1536, 256)]
     lit(*todo.pop(0))
     rad(1, lambda: lit(*todo.pop(0)))
-    copy(T.HU[:], T.HB[:], ["HB"], ["HU"])
     lit(1792, 256)
+    copy(T.HU[:], T.HB[:], ["HB"], ["HU"])
     for t in range(4, 8):
         spread(t)
         lit(512 * t, 512)
@@ -384,27 +385,37 @@ def rank_program(g, core, T, topo):
 
     win = T.LIT[:, 0:S + N * CAP]
     nc, v1 = PAR["na"], PAR["v1"]
-    na, c0 = 16 * nc, 1024 - 16 * nc
-    mm(T.psB[:, 0:na], T.IDB[:], T.PRG[:, c0:1024], ["IDB", "PRG"], ["+psB"], True, False)
+    c0, m, half = 1024 - 16 * nc, 64 - nc + PAR["n2"], 2 * (v1 // 4)
 
-    def vpart(a, b, key):
+    def on_vector(parts):
         for k in range(8):
             src = T.PRG if k == 0 else T.ACC
-            tt(T.ACC[:, 16 * a:16 * b], win.indirect(T.HU[:, 64 * k + a:64 * k + b]), src[:, 16 * a:16 * b], OP.add,
-               ["LIT", "HU", "PRG"] + ([key] if k else []), [key])
+            for a, b, key in parts:
+                tt(T.ACC[:, 16 * a:16 * b], win.indirect(T.HU[:, 64 * k + a:64 * k + b]), src[:, 16 * a:16 * b], OP.add,
+                   ["LIT", "HU", "PRG"] + ([key] if k else []), [key])
+
+    def on_scalar(a, b, bank, key):
+        n, g0 = 16 * (b - a), 128 * (a - 64 + nc)
+        mm(T[bank][:, 0:n], T.IDB[:], T.PRG[:, 16 * a:16 * b], ["IDB", "PRG"], ["+" + bank], True, False)
+        for k in range(8):
+            out = T.GA[:, g0 + n * k:g0 + n * k + n]
+            act(out, win.indirect(T.HU[:, 64 * k + a:64 * k + b]), ["LIT", "HU"], ["GA%d%s" % (k, key)])
+            mm(T[bank][:, 0:n], T.IDF[:], out, ["IDF", "GA%d%s" % (k, key)], ["+" + bank], False, k == 7)
+            if k == PAR["ev"] and key == "d":
+                act(T.ACC[:, 16 * b:1024], T.psB[:, 0:1024 - 16 * b], ["psB"], ["ACCc"])
 
     def store(lo, hi, keys, queues):
         for k in range(8):
             dma(queues[k % len(queues)], "dy", T.y[:, 1024 * k + lo:1024 * k + hi], T.ACC[16 * k:16 * k + 16, lo:hi], keys, [])
 
-    for k in range(8):
-        act(T.GA[:, na * k:na * k + na], win.indirect(T.HU[:, 64 * k + 64 - nc:64 * k + 64]), ["LIT", "HU"], ["GA%d" % k])
-        mm(T.psB[:, 0:na], T.IDF[:], T.GA[:, na * k:na * k + na], ["IDF", "GA%d" % k], ["+psB"], False, k == 7)
-    vpart(0, v1, "ACCa")
-    store(0, 16 * v1, ["ACCa"], "S")
-    act(T.ACC[:, c0:1024], T.psB[:, 0:na], ["psB"], ["ACCc"])
-    vpart(v1, 64 - nc, "ACCb")
-    store(16 * v1, 1024, ["ACCb", "ACCc"], "SA")
+    on_scalar(m, 64, "psB", "c")
+    on_scalar(64 - nc, m, "ps0", "d")
+    act(T.ACC[:, c0:16 * m], T.ps0[:, 0:16 * m - c0], ["ps0"], ["ACCd"])
+    on_vector([(0, half, "ACCz"), (half, v1, "ACCa")])
+    on_vector([(v1, 64 - nc, "ACCb")])
+    store(16 * m, 1024, ["ACCc"], "S")
+    store(0, 16 * v1, ["ACCa", "ACCz"], "S")
+    store(16 * v1, 16 * m, ["ACCb", "ACCd"], "SA")
 
     for s in SEMAPHORES:
         wait("G" if s.startswith("sent") else "S", (s, None, "D"))

@@ -5,7 +5,7 @@ F32, BF, I32, U16 = "float32", "bfloat16", "int32", "uint16"
 N, S, P, CAP = 4, 4096, 8192, 256
 NG = (N - 1) * CAP
 MAGIC = 25165824.0
-PAR = {"dense_v": 120, "na": 26, "v1": 28, "n2": 8, "ev": 4, "order": "G4x4wF44W44b4s4", "deint_v": 5}
+PAR = {"dense_v": 100, "na": 24, "v1": 18, "v2": 30, "n2": 8, "order": "G4x4wF44W444b4s", "deint_v": 5}
 NAMAX = 32
 
 SB = {
@@ -190,44 +190,49 @@ def rank_program(g, core, T, topo):
     memset(T.ZIN[96:128, :], 0.0, ["+ZIN"])
     for b in range(2):
         ts(T.C1[:, b:8:2], T.C0[:, :, b:4:2], 16.0, OP.mult, ["GS", "C0"], ["+C1"], T.GS[:, 3 * b:3 * b + 1], OP.add)
-    memset(T.LIT[:, S + CAP * r:S + CAP * r + CAP], 0.0, ["+LIT"])
-    for b in range(2):
-        ts(T.C2[:, 4 * b:4 * b + 4], T.C1[:, 4 * b:4 * b + 4], 16.0, OP.mult, ["GS", "C1"], ["+C2"], T.GS[:, 3 * b + 2:3 * b + 3], OP.add)
-    act(T.FGO[:, 15:128:16], T.C2[:], ["C2"], ["+FGO"])
-
-    nv = PAR["deint_v"]
     copy(T.GBF[:, 256:304], T.GBI[:, 256:304], ["GOI"], ["GBG"])
     mm(T.psD[:, 0:48], T.REP[:], T.GBF[:, 256:304], ["REP", "GBG"], ["+psD"])
+    for b in range(2):
+        ts(T.C2[:, 4 * b:4 * b + 4], T.C1[:, 4 * b:4 * b + 4], 16.0, OP.mult, ["GS", "C1"], ["+C2"], T.GS[:, 3 * b + 2:3 * b + 3], OP.add)
+
+    def weights_b(lo, hi):
+        for p in range(lo, hi):
+            act(T.WB[:, 16 * p:16 * p + 16], T.ID16[:], ["C2", "ID16"], ["+WB"], scale=T.C2[:, p:p + 1])
+
+    nv = PAR["deint_v"]
     for p in range(8):
+        if p == nv - 1:
+            copy(T.GI[:], T.psD[:, 0:48], ["psD"], ["GI"])
         (copy if p < nv else act)(T.X2[:, 256 * p:256 * p + 256], T.X[:, p:2048:8], ["X"], ["X2%d" % p])
     for p in range(8):
         dma("S" if p < nv else "A", "dw", T.W[16 * p:16 * p + 16, 16:1040], T.X2[:, 256 * p:256 * p + 256], ["X2%d" % p], ["+W"])
 
-    copy(T.GI[:], T.psD[:, 0:48], ["psD"], ["GI"])
+    act(T.FGO[:, 15:128:16], T.C2[:], ["C2"], ["+FGO"])
     act(T.BT[:], T.POS[:], ["POS", "E1"], ["BT"], scale=-1.0, bias=T.EC[:, 0:1])
+    weights_b(0, 2)
     act(T.BU[:], T.BT[:], ["BT"], ["BU"], scale=-1.0, bias=MAGIC)
+    weights_b(2, 4)
     act(T.B2[:], T.BU[:], ["BU"], ["B2"], scale=0.5, bias=-0.5 * MAGIC)
     ts(T.CR[0:96, 48:96], T.GI[0:96, :], 15, OP.bitwise_and, ["GI"], ["+CR"])
     ts(T.CR[96:128, 48:96], T.GI[96:128, :], 8, OP.arith_shift_right, ["GI"], ["+CR"])
     ts(T.CR[0:96, 0:48], T.GI[0:96, :], 4, OP.arith_shift_right, ["GI"], ["+CR"])
     ts(T.CR[96:128, 0:48], T.GI[96:128, :], 255, OP.bitwise_and, ["GI"], ["+CR"])
-    copy(T.CRU[:], T.CR[:], ["CR"], ["CRU"])
     copy(T.GU[:], T.GI[:], ["GI"], ["GU"])
-    copy(T.MASK[:], T.ID16[:, 0:16].indirect(T.CRU[:, 48:96]), ["ID16", "CRU"], ["MASK"])
-    for p in range(8):
-        act(T.WB[:, 16 * p:16 * p + 16], T.ID16[:], ["C2", "ID16"], ["+WB"], scale=T.C2[:, p:p + 1])
-    act(T.BG[:], T.BAS[:, 0:S].indirect(T.GU[:, 0:48]), ["BAS", "GU"], ["BG"])
+    copy(T.CRU[:], T.CR[:], ["CR"], ["CRU"])
     ts(T.GBF[:, 0:256], T.GBI[:, 0:256], float(16 - 1024 * r), OP.add, ["GBI"], ["GBF"], 0.0, OP.max)
     mm(T.psA[:, 0:256], T.REP[:], T.GBF[:, 0:256], ["REP", "GBF"], ["+psA"])
+    copy(T.MASK[:], T.ID16[:, 0:16].indirect(T.CRU[:, 48:96]), ["ID16", "CRU"], ["MASK"])
+    weights_b(4, 8)
+    act(T.BG[:], T.BAS[:, 0:S].indirect(T.GU[:, 0:48]), ["BAS", "GU"], ["BG"])
     for j, (lo, hi) in enumerate(((0, 32), (32, 64), (64, 128))):
         dma("S", "dzl", T.ZL[lo:hi, :], T.GU[lo:hi, 16 * j:16 * j + 16], ["GU"], ["+ZL"])
+    ts(T.DU[:], T.psA[:, 0:256], 1040.0, OP.min, ["psA"], ["DU"])
     tt(T.MB[:], T.B2[:, 0:256].indirect(T.CRU[:, 0:48]), T.MASK[:], OP.mult, ["B2", "CRU", "MASK"], ["MB"])
     for rho in range(16):
         mm(T.psB[:, 256:304], T.FGO[:, 15 - rho:143 - rho], T.MB[:, rho:NG:16], ["FGO", "MB"], ["+psB"], rho == 0, rho == 15)
-    ts(T.DU[:], T.psA[:, 0:256], 1040.0, OP.min, ["psA"], ["DU"])
-    tt(T.MX[:, 0:256], T.POS[:, 0:256].indirect(T.CRU[:, 0:16]), T.MASK[:, 0:256], OP.mult, ["POS", "CRU", "MASK"], ["+MX"])
+    tt(T.MX[:, 0:512], T.POS[:, 0:256].indirect(T.CRU[:, 0:32]), T.MASK[:, 0:512], OP.mult, ["POS", "CRU", "MASK"], ["+MX"])
     copy(T.OG[:], T.psB[:, 256:304], ["psB"], ["OG"])
-    tt(T.MX[:, 256:NG], T.POS[:, 0:256].indirect(T.CRU[:, 16:48]), T.MASK[:, 256:NG], OP.mult, ["POS", "CRU", "MASK"], ["+MX"])
+    tt(T.MX[:, 512:NG], T.POS[:, 0:256].indirect(T.CRU[:, 32:48]), T.MASK[:, 512:NG], OP.mult, ["POS", "CRU", "MASK"], ["+MX"])
     mm(T.ps0[:, 0:256], T.WB[:], T.B2[:], ["WB", "B2"], ["+ps0"])
     for c8 in range(8):
         mm(T.psC[:, 0:96], T.SL[:, 112 - 16 * c8:240 - 16 * c8], T.P3[:, c8:768:8], ["SL", "P3"], ["+psC"], c8 == 0, c8 == 7)
@@ -265,11 +270,11 @@ def rank_program(g, core, T, topo):
     for a in range(3):
         act(T.XS[:, 38 * a:38 * a + 32], T.psC[:, 32 * a:32 * a + 32], ["psC"], ["+XS"])
         act(T.XS[:, 38 * a + 32:38 * a + 38], T.psC[:, 128 + a:176:8], ["psC"], ["+XS"])
+    act(T.XS[:, 146:152], T.psC[:, 134:176:8], ["psC"], ["+AL"], scale=0.125)
     act(T.XT[:], T.XS[:, 0:114], ["XS"], ["XT"], bias=MAGIC)
     for h in range(2):
         act(T.XS[:, 114 + h:146:2], T.psC[:, 96 + 16 * h:112 + 16 * h], ["psC"], ["+AL"], scale=0.125)
     act(T.XY[:], T.XT[:], ["XT"], ["XY"], bias=-MAGIC)
-    act(T.XS[:, 146:152], T.psC[:, 134:176:8], ["psC"], ["+AL"], scale=0.125)
     selr = T.SELO[:, 384:512]
     ring = ["ps0", "ps1", "ps2", "psD", "psA", "ps0", "ps1", "ps2"]
 
@@ -317,9 +322,9 @@ def rank_program(g, core, T, topo):
         if c == "x":
             tt(T.XD[:], T.XS[:, 0:114], T.XY[:], OP.subtract, ["XS", "XY"], ["XD"])
             act(T.FF[:, 114:228], T.XD[:], ["XD"], ["F1"], FN.Abs)
+            act(T.EC[:, 4:5], T.GS[:, 0:1], ["GS"], ["Ea"], bias=T.GS[:, 2:3])
             act(T.FF[:, 0:114], T.FF[:, 114:228], ["F1"], ["F0"], bias=1.0, scale=-1.0)
             act(T.RET[:, :, 16:32], T.psD[:, 256:304], ["psD"], ["+RET"])
-            act(T.EC[:, 4:5], T.GS[:, 0:1], ["GS"], ["Ea"], bias=T.GS[:, 2:3])
             act(T.EC[:, 8:9], T.GS[:, 4:5], ["GS", "Ea"], ["Eb"], bias=T.EC[:, 4:5])
         if c == "F":
             for lo, hi in ((0, 4), (4, 6)):
@@ -327,19 +332,20 @@ def rank_program(g, core, T, topo):
             act(T.DF[:], T.psB[:, 0:48], ["psB"], ["DF"])
             send("2", "DF", "RET", 16)
             sel(T.IDF[:], T.ONE[:, 0:128], [[-1, 128]], OP.is_equal, 0, 1, ["ONE"], ["IDF"])
+            zero(T.LIT[:, S + CAP * r:S + CAP * r + CAP], CAP, ["+LIT"])
             act(selr, T.ONE[:, 0:128], ["ONE", "Eb"], ["+SELO"], scale=T.EC[:, 8:9])
             for j in range(3):
                 act(T.SELO[:, 128 * j:128 * j + 128], T.ONE[:, 0:128], ["ONE", "GS", "Eb"], ["+SELO"],
                     scale=T.GS[:, 2 * there[j] + 1:2 * there[j] + 2], bias=T.EC[:, 8:9])
         if c == "w":
-            for e in range(2):
-                tt(T.FZ[:, 38 * e:38 * e + 38], f(2, e), T.XS[:, 114:152], OP.mult, ["F0", "F1", "AL"], ["+FZ"])
             for x in range(4):
                 tt(T.WXY[:, 38 * x:38 * x + 38], f(0, x & 1), f(1, x >> 1), OP.mult, ["F0", "F1"], ["+WXY"])
-            for p in range(8):
-                act(T.EA[:, p:304:8], T.FZ[:, 38 * (p >> 2):38 * (p >> 2) + 38], ["FZ"], ["+EA"])
+            for e in range(2):
+                tt(T.FZ[:, 38 * e:38 * e + 38], f(2, e), T.XS[:, 114:152], OP.mult, ["F0", "F1", "AL"], ["+FZ"])
             for p in range(8):
                 act(T.EB[:, p:304:8], T.WXY[:, 38 * (p & 3):38 * (p & 3) + 38], ["WXY"], ["+EB"])
+            for p in range(8):
+                act(T.EA[:, p:304:8], T.FZ[:, 38 * (p >> 2):38 * (p >> 2) + 38], ["FZ"], ["+EA"])
         if c == "W":
             tt(T.WT[:], T.EA[:], T.EB[:], OP.mult, ["EA", "EB"], ["WT"])
             for x in range(2):
@@ -363,17 +369,15 @@ def rank_program(g, core, T, topo):
             copy(T.Z[:, 0:S].indirect(T.ZL[:, 0:16]), T.ZIN[:], ["ZL", "ZIN"], ["Z"])
             act(T.ZG[:], T.Z[:, 0:S].indirect(T.GU[:, 0:48]), ["Z", "GU"], ["ZG"])
             send("3", "ZG", "ZF", CAP)
-            for t in range(2):
-                spread(t)
 
     for c in PAR["order"]:
         step(c)
-    for t in range(2, 4):
+    for t in range(4):
         spread(t)
-    todo = [(0, 512), (512, 256), (768, 256), (1024, 256), (1280, 256), (1536, 256)]
-    lit(*todo.pop(0))
-    rad(1, lambda: lit(*todo.pop(0)))
-    lit(1792, 256)
+    todo = [None, None, (0, 256), (256, 256), (512, 256), (768, 256), (1024, 512), (1536, 512)]
+    rad(1, lambda: lit(*todo.pop(0)) if todo[0] else todo.pop(0))
+    for x in todo:
+        lit(*x)
     copy(T.HU[:], T.HB[:], ["HB"], ["HU"])
     for t in range(4, 8):
         spread(t)
@@ -384,15 +388,13 @@ def rank_program(g, core, T, topo):
         tt(T.LIT[:, S + CAP * q:S + CAP * q + CAP], T[bank][:, 0:256], T.BFO[:, 256 * j:256 * j + 256], OP.mult, [bank, "BFO"], ["+LIT"])
 
     win = T.LIT[:, 0:S + N * CAP]
-    nc, v1 = PAR["na"], PAR["v1"]
-    c0, m, half = 1024 - 16 * nc, 64 - nc + PAR["n2"], 2 * (v1 // 4)
+    nc, v1, v2 = PAR["na"], PAR["v1"], PAR["v2"]
+    c0, m = 1024 - 16 * nc, 64 - nc + PAR["n2"]
 
-    def on_vector(parts):
-        for k in range(8):
-            src = T.PRG if k == 0 else T.ACC
-            for a, b, key in parts:
-                tt(T.ACC[:, 16 * a:16 * b], win.indirect(T.HU[:, 64 * k + a:64 * k + b]), src[:, 16 * a:16 * b], OP.add,
-                   ["LIT", "HU", "PRG"] + ([key] if k else []), [key])
+    def on_vector(k, a, b, key):
+        src = T.PRG if k == 0 else T.ACC
+        tt(T.ACC[:, 16 * a:16 * b], win.indirect(T.HU[:, 64 * k + a:64 * k + b]), src[:, 16 * a:16 * b], OP.add,
+           ["LIT", "HU", "PRG"] + ([key] if k else []), [key])
 
     def on_scalar(a, b, bank, key):
         n, g0 = 16 * (b - a), 128 * (a - 64 + nc)
@@ -401,7 +403,7 @@ def rank_program(g, core, T, topo):
             out = T.GA[:, g0 + n * k:g0 + n * k + n]
             act(out, win.indirect(T.HU[:, 64 * k + a:64 * k + b]), ["LIT", "HU"], ["GA%d%s" % (k, key)])
             mm(T[bank][:, 0:n], T.IDF[:], out, ["IDF", "GA%d%s" % (k, key)], ["+" + bank], False, k == 7)
-            if k == PAR["ev"] and key == "d":
+            if k == 7 and key == "d":
                 act(T.ACC[:, 16 * b:1024], T.psB[:, 0:1024 - 16 * b], ["psB"], ["ACCc"])
 
     def store(lo, hi, keys, queues):
@@ -411,11 +413,19 @@ def rank_program(g, core, T, topo):
     on_scalar(m, 64, "psB", "c")
     on_scalar(64 - nc, m, "ps0", "d")
     act(T.ACC[:, c0:16 * m], T.ps0[:, 0:16 * m - c0], ["ps0"], ["ACCd"])
-    on_vector([(0, half, "ACCz"), (half, v1, "ACCa")])
-    on_vector([(v1, 64 - nc, "ACCb")])
+    x, y, z = (0, v1, "ACCa"), (v1, v2, "ACCz"), (v2, 64 - nc, "ACCb")
+    for k in range(4):
+        on_vector(k, *x)
+        on_vector(k, *y)
+    for k in range(4):
+        on_vector(k + 4, *x)
+        on_vector(k, *z)
+    for k in range(4, 8):
+        on_vector(k, *y)
+        on_vector(k, *z)
+    store(0, 16 * v1, ["ACCa"], "S")
     store(16 * m, 1024, ["ACCc"], "S")
-    store(0, 16 * v1, ["ACCa", "ACCz"], "S")
-    store(16 * v1, 16 * m, ["ACCb", "ACCd"], "SA")
+    store(16 * v1, 16 * m, ["ACCz", "ACCb", "ACCd"], "SA")
 
     for s in SEMAPHORES:
         wait("G" if s.startswith("sent") else "S", (s, None, "D"))

@@ -5,34 +5,39 @@ F32, BF, I32, U16 = "float32", "bfloat16", "int32", "uint16"
 N, S, P, CAP = 4, 4096, 8192, 256
 NG = (N - 1) * CAP
 MAGIC = 25165824.0
-PAR = {"dense_v": 100, "na": 24, "v1": 18, "v2": 30, "n2": 8, "order": "G4x4wF44W444b4s", "deint_v": 5}
-NAMAX = 32
+PAR = {"dense_v": 112, "sets": (((4,), (4,), (4,), (4,)),), "n2": 10, "lag": ((2, 5),), "v1": 22, "v2": 32,
+       "pre": "bkBlLyQYmfnFwdVOHMDogxeEpX", "mid": "P", "order": "C6xOBAS43w3t5nW(4ukU)4da1a1a1aarDybszhbibLbLb", "early": 6, "zp": 2048, "zq": 768, "zv": 1, "fcv": 0,
+       "us": (384, 384), "pairs": 0, "lits": ((0, 0, 256), (0, 256, 512), (1, 0, 512), (2, 0, 512), (3, 0, 512))}
 
 SB = {
-    "X": ([64, 2048], BF), "X2": ([64, 2048], BF), "W": ([128, 1056], BF), "WD": ([128, 4096], BF),
+    "X": ([128, 1024], BF), "Y": ([128, 1024], BF), "W": ([128, 1056], BF), "WD": ([128, 4096], BF),
     "BAS": ([128, S], BF), "BG": ([128, NG], BF), "BFO": ([128, NG], BF), "OG": ([128, 48], U16), "OF": ([128, 48], U16),
-    "POS": ([128, 256], F32), "P3": ([16, 1024], F32), "GBI": ([16, 304], I32), "GBF": ([16, 304], F32),
-    "DU": ([128, 256], U16), "GI": ([128, 48], I32), "GU": ([128, 48], U16), "CR": ([128, 96], I32), "CRU": ([128, 96], U16),
-    "ZL": ([128, 16], U16), "BT": ([128, 256], F32), "BU": ([128, 256], F32), "B2": ([128, 256], BF), "OU": ([128, 256], U16),
-    "MASK": ([128, NG], BF), "MX": ([128, NG], F32), "MB": ([128, NG], BF), "EA": ([128, 304], F32), "EB": ([128, 304], F32),
-    "T1": ([128, S + 2 * NG], F32), "DF": ([128, 48], F32), "RET": ([128, 3, 32], F32), "WG": ([128, 3, 32], F32),
-    "XS": ([128, 152], F32), "XT": ([128, 114], F32), "XY": ([128, 114], F32), "XD": ([128, 114], F32),
-    "FF": ([128, 228], F32), "FZ": ([128, 76], F32), "WXY": ([128, 152], F32), "WT": ([128, 304], F32),
-    "DG": ([128, 96], F32), "SG": ([128, 96], F32), "RG": ([128, 12], F32), "PG": ([128, 6, 32], BF),
-    "DW": ([128, 256], F32), "SC": ([128, 256], F32), "R1": ([128, 32], F32), "PC": ([128, 192], BF), "R": ([48, 1024], BF),
+    "FC": ([128, NG], BF), "RC": ([128, NG], BF), "GO": ([128, NG], BF), "GOA": ([128, NG], BF),
+    "POS": ([128, 256], F32), "P3": ([16, 1024], F32), "GBI": ([16, 48], I32), "GBF": ([16, 72], F32), "BM": ([128, 256], I32),
+    "DU": ([128, 256], U16), "CR": ([128, 216], I32), "CU": ([128, 216], U16),
+    "ZL": ([128, 16], U16), "BU": ([128, 256], F32), "B2": ([128, 256], BF), "OU": ([128, 256], U16),
+    "MASK": ([128, NG + 384], BF), "MX": ([128, 384], F32), "MB": ([128, NG], BF),
+    "T1": ([128, S + NG], F32), "XS": ([128, 4, 38], F32), "XT": ([128, 114], F32), "XD": ([128, 114], F32),
+    "FS": ([128, 76], F32), "FY": ([128, 76], F32), "WXZ": ([128, 152], F32), "WT": ([128, 304], F32),
+    "FL": ([128, 48], F32), "WO": ([128, 48], F32),
+    "DW": ([128, 352], F32), "SC": ([128, 352], F32), "R1": ([128, 44], F32), "PU": ([128, 22, 32], BF), "R": ([128, 512], BF),
     "ZIN": ([128, 256], BF), "Z": ([128, S], BF), "ZG": ([128, NG], BF), "ZF": ([128, NG], BF), "LIT": ([128, S + N * CAP], F32),
     "HA": ([128, 512], I32), "HB": ([128, 512], I32), "HU": ([128, 512], U16),
-    "PRG": ([128, 1024], BF), "ACC": ([128, 1024], F32), "GA": ([128, 8 * 16 * NAMAX], F32),
-    "ONE": ([128, 256], F32), "SL": ([16, 240], F32), "REP": ([16, 128], F32), "I16": ([128, 16], I32), "I16B": ([128, 16], I32),
-    "ID16": ([128, 16], F32), "GS0": ([128, 8], F32), "GS": ([128, 8], F32), "EC": ([128, 16], F32),
-    "C0": ([128, 2, 4], F32), "C1": ([128, 8], F32), "C2": ([128, 8], F32), "FGO": ([128, 144], BF), "WB": ([128, 128], BF),
-    "IDF": ([128, 128], F32), "IDB": ([128, 128], BF), "SEL8": ([48, 1024], BF), "SELO": ([128, 512], BF), "KEEP": ([128, 128], F32),
+    "PRG": ([128, 1024], BF), "ACC": ([128, 1024], F32), "GA": ([128, 5120], F32),
+    "PRA": ([128, 768], BF), "SUM": ([128, 768], F32), "OUT": ([128, 768], F32), "E4": ([128, 68], F32),
+    "ONE": ([128, 256], F32), "SL": ([16, 240], F32), "SL2": ([16, 34], F32),
+    "REP": ([16, 128], F32), "REPB": ([16, 128], F32), "I16": ([128, 32], I32), "I16B": ([128, 32], I32),
+    "ID16": ([128, 16], F32), "GS": ([128, 8], F32), "GSB": ([128, 8], BF), "GS3": ([128, 26], F32), "EC": ([128, 24], F32),
+    "FGO": ([128, 144], BF), "WB": ([128, 128], BF), "IDF": ([128, 128], F32), "IDB": ([128, 128], BF),
+    "SEL2": ([128, 256], BF), "SELO": ([128, 512], BF), "KEEP": ([128, 224], F32),
+    "TMP": ([128, 1536], F32), "BAS2": ([128, 1536], BF),
 }
 SCRATCH = {k: ("sbuf", v[0], v[1]) for k, v in SB.items()}
-for _b in ("psA", "psB", "psC", "psD", "ps0", "ps1", "ps2", "ps3"):
-    SCRATCH[_b] = ("psum", [128, 512], F32)
-SEMAPHORES = ["V", "A", "P", "G", "dpro", "dgo", "dgb", "dpos", "dbas", "dp3", "dw", "dha", "dhb", "dprg", "dzl", "dy",
-              "hop1", "hop2", "hop3", "sent1", "sent2", "sent3"]
+SCRATCH["PS"] = ("psum", [128, 6 * 512], F32)
+for _b in ("psT0", "psT1"):
+    SCRATCH[_b] = ("psum", [128, 1024], BF)
+SEMAPHORES = ["V", "A", "P", "G", "dpro", "dgo", "dgb", "dpos", "dalb", "dbas", "dp3", "dha", "dhb", "dprg", "dzl", "db2", "dsw", "dy",
+              "hop1", "hop2", "hop3", "hopb", "sent1", "sent2", "sent3", "sentb"]
 
 
 def split_engines(topo, core, dsts):
@@ -81,6 +86,8 @@ def rank_program(g, core, T, topo):
         for k in writes:
             st = state.setdefault(k.lstrip("+"), {"w": [], "base": [], "r": []})
             toks += (st["base"] if k[0] == "+" else st["w"]) + st["r"]
+            if k.startswith("+ps"):
+                toks += [t for t in st["w"] if t[2] != q]
         for t in sorted(toks, key=lambda t: -(t[1] or 0)):
             wait(q, t)
 
@@ -108,14 +115,12 @@ def rank_program(g, core, T, topo):
 
     def send(hop, src, dst, width):
         before("G", [src], [])
-
-        def dst_ap(j):
-            return T[dst][:, j, 0:width] if len(SB[dst][0]) == 3 else T[dst][:, width * j:width * j + width]
         tr = []
         for j, q in enumerate(others):
             rid, pid, _ = topo.addr(cores[q])
             tr.append(RemoteDMATransfer(dst_ids=[DstId(rid=rid, pnc=pid)], dma_engine_mask=masks[cores[q]], remote_sem=T.sem["hop" + hop],
-                                        src=T[src][:, width * j:width * j + width], dst=dst_ap(there[j])))
+                                        src=T[src][:, width * j:width * j + width],
+                                        dst=T[dst][:, width * there[j]:width * there[j] + width]))
         g.remote_dma_fused(tr, local_sem=T.sem["sent" + hop])
         cnt["sent" + hop] += neng * len(others)
         cnt["hop" + hop] += neng * len(others)
@@ -123,8 +128,9 @@ def rank_program(g, core, T, topo):
 
     V, A, PE = g.vector, g.scalar, g.tensor
 
-    def memset(ap, c, w):
-        op("V", lambda: V.memset(ap, c), [], w)
+    def ps(bank, lo, hi, rows=128, row0=0):
+        at = 512 * "ABCDEF".index(bank[-1])
+        return T.PS[row0:rows, at + lo:at + hi]
 
     def copy(out, in_, rd, w):
         op("V", lambda: V.tensor_copy(out, in_), rd, w)
@@ -148,284 +154,490 @@ def rank_program(g, core, T, topo):
     def mm(out, lhsT, rhs, rd, w, start=True, stop=True):
         op("P", lambda: PE.matmul(out, lhsT, rhs, start, stop), rd, w)
 
-    def sel(out, in_, pat, cmp, base, cm, rd, w):
-        op("G", lambda: g.affine_select(out, in_, pat, cmp, 0.0, base, cm), rd, w)
+    def turn(out, in_, rd, w):
+        op("P", lambda: PE.transpose(out, in_, T.IDB[:]), rd + ["IDB"], w)
 
-    def zero(out, n, w):
-        op("G", lambda: g.iota(out, [[0, n]], 0, 0, allow_small_or_imprecise_dtypes=True), [], w)
+    start = [0]
+
+    def pool(call, p0, rd, w):
+        if p0 != start[0]:
+            wait("G", ("G", None, "G"))
+            start[0] = p0
+        op("G", call, rd, w)
+
+    def sel(out, in_, pat, cmp, base, cm, rd, w, p0=0):
+        pool(lambda: g.affine_select(out, in_, pat, cmp, 0.0, base, cm), p0, rd, w)
+
+    def iota(out, pat, base, cm, w, p0=0):
+        pool(lambda: g.iota(out, pat, base, cm), p0, [], w)
+
+    def fill(out, n, c, w, p0=0):
+        pool(lambda: g.iota(out, [[0, n]], c, 0, allow_small_or_imprecise_dtypes=True), p0, [], w)
+
+    def zero(out, n, w, lo=0, hi=128):
+        act(out, T.ONE[lo:hi, 0:n], ["ONE"], w, scale=0.0)
 
     if r > 0:
-        dma("A", "dgo", T.GBI[:, 256:256 + 16 * r], T.go[:, 0:16 * r], [], ["+GOI"])
+        dma("A", "dgo", T.GBI[:, 0:16 * r], T.go[:, 0:16 * r], [], ["+GOI"])
     if r < N - 1:
-        dma("A", "dgo", T.GBI[:, 256 + 16 * r:304], T.go[:, 16 * r + 16:64], [], ["+GOI"])
+        dma("A", "dgo", T.GBI[:, 16 * r:48], T.go[:, 16 * r + 16:64], [], ["+GOI"])
+    for k in range(6):
+        dma("SSA"[k % 3], "dpos", T.POS[16 * k:16 * k + 16, :], T.pos[16 * (k // 2):16 * (k // 2) + 16, :], [], ["+POS"])
     dma("S", "dpro", T.X[:], T.pro[:], [], ["X"])
-    dma("S", "dgb", T.GBI[:, 0:256], T.bmap[:], [], ["+GBI"])
-    for e in range(2):
-        dma("AS"[e], "dpos", T.POS[48 * e:48 * e + 48, :], T.pos[:], [], ["+POS"])
-    for e in range(2):
-        dma("AS"[e], "dpos", T.POS[96 + 16 * e:112 + 16 * e, :], T.alb[:], [], ["+POS"])
     for p in range(8):
-        dma("AS"[p % 2], "dbas", T.BAS[16 * p:16 * p + 16, :], T.bas[:], [], ["+BAS"])
+        dma("S", "dgb", T.BM[16 * p:16 * p + 16, :], T.bmap[:], [], ["+BM"])
+    for e in range(2):
+        dma("S", "dalb", T.POS[96 + 16 * e:112 + 16 * e, :], T.alb[:], [], ["+ALB"])
     for a in range(3):
         dma("S", "dp3", T.P3[:, 256 * a:256 * a + 256], T.pos[16 * a:16 * a + 16, :], [], ["+P3"])
     dma("S", "dp3", T.P3[:, 768:1024], T.alb[:], [], ["+P3"])
+    for p in range(8):
+        dma("S", "dbas", T.BAS[16 * p:16 * p + 16, :], T.bas[:], [], ["+BAS"])
 
-    memset(T.ONE[:], 1.0, ["ONE"])
-    op("G", lambda: g.iota(T.I16[:], [[-1, 16]], 16, 1), [], ["I16"])
-    sel(T.GS0[:], T.ONE[:, 0:8], [[-16, 8]], OP.is_ge, 0, 1, ["ONE"], ["GS0"])
-    sel(T.EC[:, 0:1], T.ONE[:, 0:1], [[0, 1]], OP.is_ge, -48, 1, ["ONE"], ["E1"])
-    sel(T.GS[:], T.GS0[:], [[16, 8]], OP.is_ge, 15, -1, ["GS0"], ["GS"])
+    op("V", lambda: V.memset(T.ONE[:], 1.0), [], ["ONE"])
+    iota(T.I16[:, 0:16], [[-1, 16]], 16, 1, ["I16"])
+    iota(T.I16[:, 16:24], [[-16, 8]], 0, 1, ["I8"])
     sel(T.REP[:], T.ONE[0:16, 0:128], [[0, 8], [-1, 16]], OP.is_equal, 0, 1, ["ONE"], ["REP"])
-    sel(T.SL[:], T.ONE[0:16, 0:240], [[-1, 240]], OP.is_equal, 112, 1, ["ONE"], ["SL"])
-    zero(T.Z[:, 0:2048], 2048, ["+Z"])
-    memset(T.W[:, 0:16], 0.0, ["+W"])
-    memset(T.W[:, 1040:1056], 0.0, ["+W"])
-    memset(T.FGO[:], 0.0, ["FGO"])
-    ts(T.I16B[:], T.I16[:], 15, OP.bitwise_and, ["I16"], ["I16B"])
-    memset(T.PG[:], 0.0, ["PG"])
-    ts(T.ID16[:], T.I16B[:], 0.0, OP.is_equal, ["I16B"], ["ID16"])
-    memset(T.PC[:], 0.0, ["PC"])
-    for b in range(2):
-        ts(T.C0[:, :, 2 * b:2 * b + 2], T.ONE[:, 0:4], T.GS[:, 3 * b + 1:3 * b + 2], OP.mult, ["GS", "ONE"], ["+C0"])
-    memset(T.ZIN[96:128, :], 0.0, ["+ZIN"])
-    for b in range(2):
-        ts(T.C1[:, b:8:2], T.C0[:, :, b:4:2], 16.0, OP.mult, ["GS", "C0"], ["+C1"], T.GS[:, 3 * b:3 * b + 1], OP.add)
-    copy(T.GBF[:, 256:304], T.GBI[:, 256:304], ["GOI"], ["GBG"])
-    mm(T.psD[:, 0:48], T.REP[:], T.GBF[:, 256:304], ["REP", "GBG"], ["+psD"])
-    for b in range(2):
-        ts(T.C2[:, 4 * b:4 * b + 4], T.C1[:, 4 * b:4 * b + 4], 16.0, OP.mult, ["GS", "C1"], ["+C2"], T.GS[:, 3 * b + 2:3 * b + 3], OP.add)
-
-    def weights_b(lo, hi):
-        for p in range(lo, hi):
-            act(T.WB[:, 16 * p:16 * p + 16], T.ID16[:], ["C2", "ID16"], ["+WB"], scale=T.C2[:, p:p + 1])
-
-    nv = PAR["deint_v"]
-    for p in range(8):
-        if p == nv - 1:
-            copy(T.GI[:], T.psD[:, 0:48], ["psD"], ["GI"])
-        (copy if p < nv else act)(T.X2[:, 256 * p:256 * p + 256], T.X[:, p:2048:8], ["X"], ["X2%d" % p])
-    for p in range(8):
-        dma("S" if p < nv else "A", "dw", T.W[16 * p:16 * p + 16, 16:1040], T.X2[:, 256 * p:256 * p + 256], ["X2%d" % p], ["+W"])
-
-    act(T.FGO[:, 15:128:16], T.C2[:], ["C2"], ["+FGO"])
-    act(T.BT[:], T.POS[:], ["POS", "E1"], ["BT"], scale=-1.0, bias=T.EC[:, 0:1])
-    weights_b(0, 2)
-    act(T.BU[:], T.BT[:], ["BT"], ["BU"], scale=-1.0, bias=MAGIC)
-    weights_b(2, 4)
-    act(T.B2[:], T.BU[:], ["BU"], ["B2"], scale=0.5, bias=-0.5 * MAGIC)
-    ts(T.CR[0:96, 48:96], T.GI[0:96, :], 15, OP.bitwise_and, ["GI"], ["+CR"])
-    ts(T.CR[96:128, 48:96], T.GI[96:128, :], 8, OP.arith_shift_right, ["GI"], ["+CR"])
-    ts(T.CR[0:96, 0:48], T.GI[0:96, :], 4, OP.arith_shift_right, ["GI"], ["+CR"])
-    ts(T.CR[96:128, 0:48], T.GI[96:128, :], 255, OP.bitwise_and, ["GI"], ["+CR"])
-    copy(T.GU[:], T.GI[:], ["GI"], ["GU"])
-    copy(T.CRU[:], T.CR[:], ["CR"], ["CRU"])
-    ts(T.GBF[:, 0:256], T.GBI[:, 0:256], float(16 - 1024 * r), OP.add, ["GBI"], ["GBF"], 0.0, OP.max)
-    mm(T.psA[:, 0:256], T.REP[:], T.GBF[:, 0:256], ["REP", "GBF"], ["+psA"])
-    copy(T.MASK[:], T.ID16[:, 0:16].indirect(T.CRU[:, 48:96]), ["ID16", "CRU"], ["MASK"])
-    weights_b(4, 8)
-    act(T.BG[:], T.BAS[:, 0:S].indirect(T.GU[:, 0:48]), ["BAS", "GU"], ["BG"])
-    for j, (lo, hi) in enumerate(((0, 32), (32, 64), (64, 128))):
-        dma("S", "dzl", T.ZL[lo:hi, :], T.GU[lo:hi, 16 * j:16 * j + 16], ["GU"], ["+ZL"])
-    ts(T.DU[:], T.psA[:, 0:256], 1040.0, OP.min, ["psA"], ["DU"])
-    tt(T.MB[:], T.B2[:, 0:256].indirect(T.CRU[:, 0:48]), T.MASK[:], OP.mult, ["B2", "CRU", "MASK"], ["MB"])
-    for rho in range(16):
-        mm(T.psB[:, 256:304], T.FGO[:, 15 - rho:143 - rho], T.MB[:, rho:NG:16], ["FGO", "MB"], ["+psB"], rho == 0, rho == 15)
-    tt(T.MX[:, 0:512], T.POS[:, 0:256].indirect(T.CRU[:, 0:32]), T.MASK[:, 0:512], OP.mult, ["POS", "CRU", "MASK"], ["+MX"])
-    copy(T.OG[:], T.psB[:, 256:304], ["psB"], ["OG"])
-    tt(T.MX[:, 512:NG], T.POS[:, 0:256].indirect(T.CRU[:, 32:48]), T.MASK[:, 512:NG], OP.mult, ["POS", "CRU", "MASK"], ["+MX"])
-    mm(T.ps0[:, 0:256], T.WB[:], T.B2[:], ["WB", "B2"], ["+ps0"])
-    for c8 in range(8):
-        mm(T.psC[:, 0:96], T.SL[:, 112 - 16 * c8:240 - 16 * c8], T.P3[:, c8:768:8], ["SL", "P3"], ["+psC"], c8 == 0, c8 == 7)
-    for h in range(2):
-        mm(T.psC[:, 96 + 16 * h:112 + 16 * h], T.P3[:, 768 + 128 * h:896 + 128 * h], T.SL[:, 112:128], ["SL", "P3"], ["+psC"])
-    for c in range(6):
-        mm(T.psC[:, 128 + 8 * c:136 + 8 * c], T.MX[:, 128 * c:128 * c + 128], T.GS[:], ["MX", "GS"], ["+psC"])
-
-    send("1", "BG", "BFO", CAP)
-    send("1", "OG", "OF", 16)
-    zero(T.Z[:, 2048:4096], 2048, ["+Z"])
-    sel(T.KEEP[:], T.ONE[:, 0:128], [[0, 16], [1, 8]], OP.not_equal, 0, 0, ["ONE"], ["KEEP"])
+    sel(T.REPB[:], T.ONE[0:16, 0:128], [[0, 4], [-1, 32]], OP.is_equal, 16, 1, ["ONE"], ["REPB"])
     sel(T.IDB[:], T.ONE[:, 0:128], [[-1, 128]], OP.is_equal, 0, 1, ["ONE"], ["IDB"])
+    ts(T.I16B[:, 16:24], T.I16[:, 16:24], 4, OP.arith_shift_right, ["I8"], ["I8B"])
+    ts(T.I16B[:, 0:16], T.I16[:, 0:16], 15, OP.bitwise_and, ["I16"], ["I16B"])
+    ts(T.GS[:], T.I16B[:, 16:24], 0.0, OP.is_equal, ["I8B"], ["GS"])
+    ts(T.ID16[:], T.I16B[:, 0:16], 0.0, OP.is_equal, ["I16B"], ["ID16"])
+    for a, factor in enumerate((16.0, 256.0, 1.0)):
+        act(T.EC[32 * a:32 * a + 32, 1:2], T.ONE[32 * a:32 * a + 32, 0:1], ["ONE"], ["+EF"], scale=0.5 * factor)
+    zero(T.FGO[0:96, :], 144, ["FGO"], 0, 96)
+    act(T.EC[:, 16:20], T.GS[:, 1:8:2], ["GS"], ["E1"], accum_out=T.EC[:, 0:1])
+    if "A" in PAR["pre"]:
+        act(T.EC[0:96, 2:3], T.EC[0:96, 1:2], ["EF"], ["EM"], scale=-MAGIC)
+    zero(T.B2[96:128, :], 256, ["+B2"], 96, 128)
+    zero(T.W[:, 0:16], 16, ["+W"])
+    zero(T.W[:, 1040:1056], 16, ["+W"])
+    zero(T.GS3[:], 26, ["GS3"])
+    act(T.GSB[:], T.GS[:], ["GS"], ["GSB"])
+    act(T.GS3[:, 2:26:3], T.GS[:], ["GS"], ["+GS3"])
+    for a, bit in enumerate(([[0, 4], [16, 2]], [[0, 2], [16, 2], [0, 2]], [[16, 2], [0, 4]])):
+        rows, p0 = slice(32 * a, 32 * a + 32), 32 * a
+        iota(T.I16[rows, 24:32], bit, 15, -1, ["+IP"], p0)
+        if a == 1:
+            for h in range(2):
+                sel(T.WB[rows, 64 * h:64 * h + 64], T.ONE[rows, 0:64], [[16, 2], [0, 2], [1, 16]], OP.is_equal, 0, -1, ["ONE"], ["+WB"], p0)
+        else:
+            sel(T.WB[rows, :], T.ONE[rows, 0:128], bit + [[1, 16]], OP.is_equal, 0, -1, ["ONE"], ["+WB"], p0)
+    sel(T.SL[:], T.ONE[0:16, 0:240], [[-1, 240]], OP.is_equal, 112, 1, ["ONE"], ["SL"])
+    sel(T.SL2[:], T.ONE[0:16, 0:34], [[-1, 34]], OP.is_equal, 1, 2, ["ONE"], ["SL2"])
 
-    d = PAR["dense_v"]
-    copy(T.WD[:, 0:16 * d], T.W[:, 0:1056].indirect(T.DU[:, 0:d]), ["W", "DU"], ["+WD"])
-    copy(T.OU[:], T.ps0[:, 0:256], ["ps0"], ["OU"])
-    act(T.WD[:, 16 * d:4096], T.W[:, 0:1056].indirect(T.DU[:, d:256]), ["W", "DU"], ["+WD"])
+    copy(T.GBF[:, 0:48], T.GBI[:], ["GOI"], ["GBG"])
+    tt(T.GBF[:, 48:72], T.GBI[:, 24:48], T.GBI[:, 0:24], OP.subtract, ["GOI"], ["GBD"])
+    mm(ps("D", 0, 48), T.REP[:], T.GBF[:, 0:48], ["REP", "GBG"], ["+psD"])
+    mm(ps("D", 48, 72), T.REP[:], T.GBF[:, 0:24], ["REP", "GBG"], ["+psD"], True, False)
+    mm(ps("D", 48, 72), T.REPB[:], T.GBF[:, 48:72], ["REPB", "GBD"], ["+psD"], False, True)
 
+    d, go_u = PAR["dense_v"], T.CU[:, 0:48]
+    halves = ((0, 24), (24, 48)) if "n" in PAR["pre"] else ((0, 48),)
+
+    def ready(c):
+        if c == "k":
+            copy(T.CR[:, 0:72], ps("D", 0, 72), ["psD"], ["GI"])
+        if c == "l":
+            ts(T.CR[0:96, 144:216], T.CR[0:96, 0:72], 15, OP.bitwise_and, ["GI"], ["+CR"])
+            ts(T.CR[96:128, 144:216], T.CR[96:128, 0:72], 8, OP.arith_shift_right, ["GI"], ["+CR"])
+            ts(T.CR[0:96, 72:144], T.CR[0:96, 0:72], 4, OP.arith_shift_right, ["GI"], ["+CR"])
+            ts(T.CR[96:128, 72:144], T.CR[96:128, 0:72], 255, OP.bitwise_and, ["GI"], ["+CR"])
+        if c == "L":
+            lo = 144 * ("Q" in PAR["pre"])
+            copy(T.CU[:, lo:216], T.CR[:, lo:216], ["CR", "GI"], ["CL", "+CU"])
+            for a, b in halves:
+                act(T.MASK[:, 16 * a:16 * b], T.ID16[:, 0:16].indirect(T.CU[:, 144 + a:144 + b]), ["ID16", "CL"], ["MASK%d" % a])
+        if c == "Q":
+            copy(T.CU[:, 0:144], T.CR[:, 0:144], ["CR", "GI"], ["+CU"])
+        if c == "H":
+            act(T.MASK[:, NG:NG + 384], T.ID16[:, 0:16].indirect(T.CU[:, 192:216]), ["ID16", "CL"], ["MASKH"])
+        if c == "b":
+            ts(T.BU[0:96, :], T.POS[0:96, :], T.EC[0:96, 0:1], OP.subtract, ["POS", "E1"], ["BU"], MAGIC, OP.add)
+        if c == "B":
+            ts(T.B2[0:96, :], T.BU[0:96, :], MAGIC, OP.subtract, ["BU", "EF"], ["+B2"], T.EC[0:96, 1:2], OP.mult)
+        if c == "A":
+            act(T.B2[0:96, :], T.BU[0:96, :], ["BU", "EF", "EM"], ["+B2"], scale=T.EC[0:96, 1:2], bias=T.EC[0:96, 2:3])
+        if c in "yz":
+            for p in range(8):
+                turn(T["psT%d" % (p // 4)][:, 128 * (p % 4):128 * (p % 4) + 128], T.X[:, p:1024:8], ["X"], ["+psT%d" % (p // 4)])
+            (copy if c == "y" else act)(T.Y[:, 0:512], T.psT0[:, 0:512], ["psT0"], ["+Y"])
+        if c == "Y":
+            copy(T.Y[:, 512:1024], T.psT1[:, 0:512], ["psT1"], ["+Y"])
+            for p in range(8):
+                turn(T["psT%d" % (p // 4)][:, 128 * (p % 4):128 * (p % 4) + 128], T.Y[:, p:1024:8], ["Y"], ["+psT%d" % (p // 4)])
+        if c in "wW":
+            (act if c == "w" else copy)(T.W[:, 16:528], T.psT0[:, 0:512], ["psT0"], ["+W"])
+        if c in "vV":
+            (act if c == "v" else copy)(T.W[:, 528:1040], T.psT1[:, 0:512], ["psT1"], ["+W"])
+        if c in "mn":
+            a, b = halves[c == "n"]
+            tt(T.MB[:, 16 * a:16 * b], T.B2[:, 0:256].indirect(T.CU[:, 72 + a:72 + b]), T.MASK[:, 16 * a:16 * b], OP.mult,
+               ["B2", "CU", "MASK%d" % a], ["+MB"])
+        if c == "f":
+            ts(T.I16B[0:96, 24:32], T.I16[0:96, 24:32], 4, OP.arith_shift_right, ["IP"], ["IPB"])
+        if c == "F":
+            ts(T.FGO[0:96, 15:128:16], T.I16B[0:96, 24:32], 0.0, OP.is_equal, ["IPB"], ["+FGO"])
+        if c == "M":
+            for rho in range(16):
+                mm(ps("E", 256, 304), T.FGO[0:96, 15 - rho:143 - rho], T.MB[0:96, rho:NG:16], ["FGO", "MB"], ["+psE"], rho == 0, rho == 15)
+        if c == "g":
+            copy(T.OG[:], ps("E", 256, 304), ["psE"], ["OG"])
+        if c == "O":
+            mm(ps("F", 0, 256), T.WB[0:96, :], T.B2[0:96, :], ["WB", "B2"], ["+psF"])
+        if c == "o":
+            copy(T.OU[:], ps("F", 0, 256), ["psF"], ["OU"])
+        if c == "d":
+            ts(T.DU[:], T.BM[:], float(16 - 1024 * r), OP.add, ["BM"], ["DU"], 1040.0, OP.min)
+        if c == "D":
+            act(T.WD[:, 16 * d:4096], T.W[:, 0:1056].indirect(T.DU[:, d:256]), ["W", "DU"], ["+WD"])
+        if c == "e":
+            copy(T.WD[:, 0:256], T.W[:, 0:1056].indirect(T.DU[:, 0:16]), ["W", "DU"], ["+WD"])
+        if c == "E":
+            lo = 16 * ("e" in PAR["pre"])
+            copy(T.WD[:, 16 * lo:16 * d], T.W[:, 0:1056].indirect(T.DU[:, lo:d]), ["W", "DU"], ["+WD"])
+        if c == "p":
+            for c8 in range(8):
+                mm(ps("C", 0, 96), T.SL[:, 112 - 16 * c8:240 - 16 * c8], T.P3[:, c8:768:8], ["SL", "P3"], ["+psC"], c8 == 0, c8 == 7)
+            for h in range(2):
+                mm(ps("C", 96, 128), T.P3[:, 768 + 128 * h:896 + 128 * h], T.SL2[:, 1 - h:33 - h], ["SL2", "P3"], ["+psC"], h == 0, h == 1)
+        if c == "x":
+            tt(T.MX[:], T.POS[:, 0:256].indirect(T.CU[:, 120:144]), T.MASK[:, NG:NG + 384], OP.mult, ["POS", "ALB", "CU", "MASKH"], ["MX"])
+        if c == "X":
+            for b in range(3):
+                mm(ps("C", 128, 152), T.MX[:, 128 * b:128 * b + 128], T.GS3[:, 2 - b:26 - b], ["MX", "GS3"], ["+psC"], b == 0, b == 2)
+
+    for c in PAR["pre"]:
+        ready(c)
+
+    zp, zq = PAR["zp"], PAR["zq"]
+    if PAR.get("probe") == 1:
+        before("G", ["OG"], [])
+        fill(T.GA[:, 0:448], 448, 0, [])
+    send("1", "OG", "OF", 16)
+    fill(T.PU[:], 704, 0, ["PU"])
+    sel(T.KEEP[:], T.ONE[:, 0:224], [[0, 28], [1, 8]], OP.not_equal, 0, 0, ["ONE"], ["KEEP"])
+    for c in PAR["mid"]:
+        if c == "P":
+            act(T.XS[:, :, 6:38], ps("C", 0, 128), ["psC"], ["+XS"])
+            act(T.XS[:, :, 0:6], ps("C", 128, 152), ["psC"], ["+XS"])
+            act(T.XT[:], T.XS[:, 0:3, :], ["XS"], ["XT"], bias=MAGIC)
+            act(ps("C", 200, 314), T.XT[:], ["XT"], ["+psC"], bias=-MAGIC)
+        if c == "B":
+            act(T.BG[:], T.BAS[:, 0:S].indirect(go_u), ["BAS", "CU"], ["BG"])
+
+    sets = PAR["sets"]
+    na = 128 * sum(sum(sum(c) for c in u) for u in sets)
+    cw = (P - na) // 128
+    nv = 16 * cw
+    early = PAR["early"]
+    for k, (lo, hi) in enumerate(((0, 16), (16, 32), (32, 48), (48, 64), (64, 80), (80, 128))):
+        dma("S", "dzl", T.ZL[lo:hi, :], T.CU[lo:hi, 16 * (k % 3):16 * (k % 3) + 16], ["CU"], ["+ZL"])
     wait("S", ("sent1", None, "D"))
-    for k in range(8):
-        dma("S", "dha", T.HA[:, 64 * k:64 * k + 64], T.hit[16 * k:16 * k + 16, :], [], ["+HA"])
-    for k in range(8):
-        dma("S", "dhb", T.HB[16 * k:16 * k + 16, :], T.HA[k:128:8, :], ["HA"], ["+HB"])
-    wait("S", ("dhb", None, "D"))
-    for k in range(8):
-        dma("S", "dprg", T.PRG[16 * k:16 * k + 16, :], T.pro[:, 1024 * k:1024 * k + 1024], [], ["+PRG"])
+    for e in range(2 if PAR["pairs"] else 0):
+        n = 512 * PAR["pairs"]
+        dma("S", "db2", T.BAS2[64 * e:64 * e + 64, 0:n], T.BAS[64 * e:64 * e + 64, n * e:n * e + n], ["BAS"], ["+BAS2"])
+    for k in range(early):
+        dma("S", "dha", T.HA[:, cw * k:cw * k + cw], T.hit[16 * k:16 * k + 16, 0:8 * cw], [], ["+HA"])
 
-    def dots(col, n, off, bas, rd, bank, pcol):
-        key = "T1%d" % col
-        tt(T.T1[:, col:col + n], T.WD[:, 0:4096].indirect(off), bas, OP.mult, ["WD"] + rd, [key])
+    def hop2():
+        n = PAR["fcv"]
+        act(T.FC[:, 16 * n:NG], T.WD[:, 0:4096].indirect(T.OF[:, n:48]), ["WD", "OF"], ["+FC"])
+        if n:
+            copy(T.FC[:, 0:16 * n], T.WD[:, 0:4096].indirect(T.OF[:, 0:n]), ["WD", "OF"], ["+FC"])
+        send("2", "FC", "RC", CAP)
+        fill(T.Z[:, 0:zq], zq, 0, ["+Z"])
+        wait("S", ("sent2", None, "D"))
+        for k in range(early, 8):
+            dma("S", "dha", T.HA[:, cw * k:cw * k + cw], T.hit[16 * k:16 * k + 16, 0:8 * cw], [], ["+HA"])
+        dma("S", "dhb", T.HB[:, 8 * cw:512], T.hit[:, 8 * cw:512], [], ["+HB"])
+        for k in range(8):
+            dma("S", "dhb", T.HB[16 * k:16 * k + 16, 0:8 * cw], T.HA[k:128:8, 0:8 * cw], ["HA"], ["+HB"])
+
+    def sums(col, n, bank, pcol):
         for c in range(n // 128):
-            mm(T[bank][:, pcol + 8 * c:pcol + 8 * c + 8], T.T1[:, col + 128 * c:col + 128 * c + 128], T.GS[:], [key, "GS"], ["+" + bank])
+            mm(ps(bank, pcol + 8 * c, pcol + 8 * c + 8), T.T1[:, col + 128 * c:col + 128 * c + 128], T.GS[:], ["T1%d" % col, "GS"], ["+" + bank])
 
-    for a in range(3):
-        act(T.XS[:, 38 * a:38 * a + 32], T.psC[:, 32 * a:32 * a + 32], ["psC"], ["+XS"])
-        act(T.XS[:, 38 * a + 32:38 * a + 38], T.psC[:, 128 + a:176:8], ["psC"], ["+XS"])
-    act(T.XS[:, 146:152], T.psC[:, 134:176:8], ["psC"], ["+AL"], scale=0.125)
-    act(T.XT[:], T.XS[:, 0:114], ["XS"], ["XT"], bias=MAGIC)
-    for h in range(2):
-        act(T.XS[:, 114 + h:146:2], T.psC[:, 96 + 16 * h:112 + 16 * h], ["psC"], ["+AL"], scale=0.125)
-    act(T.XY[:], T.XT[:], ["XT"], ["XY"], bias=-MAGIC)
     selr = T.SELO[:, 384:512]
-    ring = ["ps0", "ps1", "ps2", "psD", "psA", "ps0", "ps1", "ps2"]
+    ring, pairs = ["psE", "psF", "psC", "psD", "psA", "psB", "psE", "psF"], PAR["pairs"]
 
-    def f(a, e):
-        return T.FF[:, 114 * e + 38 * a:114 * e + 38 * a + 38]
+    def pieces(lo, hi, n):
+        v, rest = T.SC[:, lo + 7:hi:8], T.R1[:, lo // 8:hi // 8]
+        top, mid, low = (T.PU[:, lo // 16:hi // 16, 2 * x:2 * x + 2] for x in range(3))
+        return [lambda: scan(T.SC[:, lo:hi], T.KEEP[:, 0:hi - lo], T.DW[:, lo:hi], ["KEEP", "DW" + n], ["SC" + n]),
+                lambda: copy(top, v, ["SC" + n, "PU"], ["Pa" + n]),
+                lambda: tt(rest, v, top, OP.subtract, ["SC" + n, "Pa" + n], ["R1" + n]),
+                lambda: copy(mid, rest, ["R1" + n], ["Pb" + n]),
+                lambda: tt(low, rest, mid, OP.subtract, ["R1" + n, "Pb" + n], ["Pc" + n])]
 
-    def rad(h, fill):
-        bank, n, c = ("psA", "ps3")[h], "%d" % h, 16 * h
-        tt(T.DW[:, 128 * h:128 * h + 128], T[bank][:, 0:128], T.WT[:, 128 * h:128 * h + 128], OP.mult, [bank, "WT"], ["DW" + n])
-        fill()
-        scan(T.SC[:, 128 * h:128 * h + 128], T.KEEP[:], T.DW[:, 128 * h:128 * h + 128], ["KEEP", "DW" + n], ["SC" + n])
-        fill()
-        v, rest = T.SC[:, 128 * h + 7:128 * h + 128:8], T.R1[:, c:c + 16]
-        hi, mid, lo = T.PC[:, c:c + 16], T.PC[:, 64 + c:80 + c], T.PC[:, 128 + c:144 + c]
-        copy(hi, v, ["SC" + n], ["+PC"])
-        fill()
-        tt(rest, v, hi, OP.subtract, ["SC" + n, "PC"], ["R1" + n])
-        fill()
-        copy(mid, rest, ["R1" + n], ["+PCm"])
-        fill()
-        tt(lo, rest, mid, OP.subtract, ["R1" + n, "PCm"], ["+PCl"])
-        for u in range(4):
-            mm(T.psC[0:48, 128 * u:128 * u + 128], T.PC[:, u:192:4], T.IDB[:], ["PC", "PCm", "PCl", "IDB"], ["+psC"])
-        act(T.R[:, 512 * h:512 * h + 512], T.psC[0:48, :], ["psC"], ["R" + n])
+    def rows(h):
+        n = "%d" % h
+        for u in range(2):
+            turn(T.psT1[:, 128 * u:128 * u + 128], T.PU[:, 6 + 8 * h:14 + 8 * h, u:32:2], ["Pa" + n, "Pb" + n, "Pc" + n], ["+psT1"])
+        act(T.R[:, 256 * h:256 * h + 256], T.psT1[:, 0:256], ["psT1"], ["R" + n])
 
-    def spread(t):
-        h = t // 4
-        mm(T[ring[t]][:], selr, T.Z[:, 512 * t:512 * t + 512], ["SELO", "Z"], ["+" + ring[t]], True, False)
-        mm(T[ring[t]][:], T.SEL8[:, 128 * t:128 * t + 128], T.R[:, 512 * h:512 * h + 512], ["SEL8", "R%d" % h], ["+" + ring[t]], False, True)
+    def parts(v):
+        return [(v, 0, 64), (v + pairs, 64, 128)] if v < pairs else [(v + pairs, 0, 128)]
 
-    def lit(c0, n):
-        bank = ring[c0 // 512]
-        tt(T.LIT[:, c0:c0 + n], T[bank][:, c0 % 512:c0 % 512 + n], T.BAS[:, c0:c0 + n], OP.mult, [bank, "BAS"], ["+LIT"])
+    def spread_r(v):
+        for t, lo, hi in parts(v):
+            for e in range(2):
+                p0, h = 32 * (t % 4), t // 4
+                mm(ps(ring[v], 256 * e, 256 * e + 256, hi, lo), T.SEL2[p0:p0 + 32, 128 * e + lo:128 * e + hi],
+                   T.R[p0:p0 + 32, 256 * h:256 * h + 256], ["SELa", "SELb", "R%d" % h], ["+" + ring[v]], e == lo == h == 0, e == h == 1)
 
-    done = [0]
+    def spread_z(v):
+        for t, lo, hi in parts(v):
+            mm(ps(ring[v], 0, 512, hi, lo), T.SELO[:, 384 + lo:384 + hi], T.Z[:, 512 * t:512 * t + 512], ["SELR", "Z"], ["+" + ring[v]],
+               t >= 4, t < 4 and hi == 128)
+
+    def lit(v, lo, hi):
+        if v >= pairs:
+            c = 512 * (v + pairs)
+            tt(T.LIT[:, c + lo:c + hi], ps(ring[v], lo, hi), T.BAS[:, c + lo:c + hi], OP.mult, [ring[v], "BAS"], ["+LIT"])
+            return
+        c = 512 * v
+        tt(T.TMP[:, c + lo:c + hi], ps(ring[v], lo, hi), T.BAS2[:, c + lo:c + hi], OP.mult, [ring[v], "BAS2"], ["+TMP%d" % v])
+        for t, p0, p1 in parts(v) if hi == 512 else ():
+            for half in range(2):
+                dma("S", "dsw", T.LIT[64 * half:64 * half + 64, 512 * t:512 * t + 512], T.TMP[p0:p1, c:c + 512], ["TMP%d" % v], ["+LIT"])
+
+    done, order, held, hold = [0], list(PAR["order"]), [], [False]
+    chain, lits = [pieces(0, 224, "0"), pieces(224, 352, "1")], [x for x in PAR["lits"] if x[0] < 4 - pairs]
 
     def step(c):
         if c.isdigit():
             t, n = done[0], int(c)
-            dots(128 * t, 128 * n, T.OU[:, 8 * t:8 * t + 8 * n], T.BAS[:, 128 * t:128 * t + 128 * n], ["OU", "BAS"],
-                 ("psA", "ps3")[t // 16], 8 * (t % 16))
+            tt(T.T1[:, 128 * t:128 * (t + n)], T.WD[:, 0:4096].indirect(T.OU[:, 8 * t:8 * (t + n)]), T.BAS[:, 128 * t:128 * (t + n)],
+               OP.mult, ["WD", "OU", "BAS"], ["T1%d" % (128 * t)])
+            held.append((128 * t, 128 * n, ("psA", "psB")[t // 16], 48 + 8 * (t % 16)))
             done[0] = t + n
-        if c == "G":
-            dots(S, NG, T.OG[:, 0:48], T.BG[:], ["OG", "BG"], "psD", 256)
+        if c in "()":
+            hold[0] = c == "("
+        while held and not hold[0]:
+            sums(*held.pop(0))
         if c == "x":
-            tt(T.XD[:], T.XS[:, 0:114], T.XY[:], OP.subtract, ["XS", "XY"], ["XD"])
-            act(T.FF[:, 114:228], T.XD[:], ["XD"], ["F1"], FN.Abs)
-            act(T.EC[:, 4:5], T.GS[:, 0:1], ["GS"], ["Ea"], bias=T.GS[:, 2:3])
-            act(T.FF[:, 0:114], T.FF[:, 114:228], ["F1"], ["F0"], bias=1.0, scale=-1.0)
-            act(T.RET[:, :, 16:32], T.psD[:, 256:304], ["psD"], ["+RET"])
-            act(T.EC[:, 8:9], T.GS[:, 4:5], ["GS", "Ea"], ["Eb"], bias=T.EC[:, 4:5])
-        if c == "F":
-            for lo, hi in ((0, 4), (4, 6)):
-                dots(S + NG + 128 * lo, 128 * (hi - lo), T.OF[:, 8 * lo:8 * hi], T.BFO[:, 128 * lo:128 * hi], ["OF", "BFO"], "psB", 8 * lo)
-            act(T.DF[:], T.psB[:, 0:48], ["psB"], ["DF"])
-            send("2", "DF", "RET", 16)
+            tt(T.XD[:], T.XS[:, 0:3, :], ps("C", 200, 314), OP.subtract, ["XS", "psC"], ["XD"])
+            act(ps("C", 396, 472), T.XD[:, 0:76], ["XD"], ["+psC"], FN.Abs)
+            act(T.FS[:, 38:76], T.XD[:, 76:114], ["XD"], ["F1"], FN.Abs, scale=0.125)
+            act(ps("C", 320, 396), ps("C", 396, 472), ["psC"], ["+psC"], bias=1.0, scale=-1.0)
+            act(T.FS[:, 0:38], T.FS[:, 38:76], ["F1"], ["F0"], bias=0.125, scale=-1.0)
+        if c == "C":
+            hop2()
+        if c == "O":
+            act(T.GO[:], T.WD[:, 0:4096].indirect(T.OG[:, 0:48]), ["WD", "OG"], ["GO"])
+        if c == "B":
+            act(T.BG[:], T.BAS[:, 0:S].indirect(go_u), ["BAS", "CU"], ["BG"])
+        if c == "S":
+            wait("G", ("sent2", None, "D"))
+            send("b", "BG", "BFO", CAP)
+            fill(T.Z[:, zq:zp], zp - zq, 0, ["+Z"])
+            fill(T.LIT[:, S + CAP * r:S + CAP * r + CAP], CAP, 0, ["+LIT"])
             sel(T.IDF[:], T.ONE[:, 0:128], [[-1, 128]], OP.is_equal, 0, 1, ["ONE"], ["IDF"])
-            zero(T.LIT[:, S + CAP * r:S + CAP * r + CAP], CAP, ["+LIT"])
-            act(selr, T.ONE[:, 0:128], ["ONE", "Eb"], ["+SELO"], scale=T.EC[:, 8:9])
-            for j in range(3):
-                act(T.SELO[:, 128 * j:128 * j + 128], T.ONE[:, 0:128], ["ONE", "GS", "Eb"], ["+SELO"],
-                    scale=T.GS[:, 2 * there[j] + 1:2 * there[j] + 2], bias=T.EC[:, 8:9])
+        if c == "A":
+            act(T.GOA[:], T.GO[:], ["GO"], ["GOA"], FN.Abs)
+            zero(T.ZIN[96:128, :], 256, ["+ZIN"], 96, 128)
+        if c == "n":
+            for c6 in range(6):
+                mm(ps("D", 304 + 8 * c6, 312 + 8 * c6), T.GOA[:, 128 * c6:128 * c6 + 128], T.GSB[:], ["GOA", "GSB"], ["+psD"])
+            act(T.FL[:], ps("D", 304, 352), ["psD"], ["FL"], FN.Sign)
+            act(T.Z[:, zp:S], T.BAS[:, zp:S], ["BAS"], ["+Z"], scale=0.0)
+            act(T.EC[:, 16:19], T.GS[:, 0:3], ["GS", "E1"], ["Ea"], scale=-1.0, accum_out=T.EC[:, 4:5])
+            act(T.EC[:, 20:23], T.GS[:, 3:6], ["GS"], ["Eb"], accum_out=T.EC[:, 5:6])
+            act(T.EC[:, 8:9], T.EC[:, 4:5], ["Ea", "Eb"], ["Ec"], bias=T.EC[:, 5:6])
+            act(T.SEL2[:, 128:256], T.ONE[:, 0:128], ["ONE", "E1"], ["SELb"], scale=T.EC[:, 0:1])
+            act(selr, T.ONE[:, 0:128], ["ONE", "Ec"], ["SELR"], scale=T.EC[:, 8:9])
+            act(T.SEL2[:, 0:128], T.SEL2[:, 128:256], ["SELb"], ["SELa"], scale=-1.0, bias=1.0)
         if c == "w":
-            for x in range(4):
-                tt(T.WXY[:, 38 * x:38 * x + 38], f(0, x & 1), f(1, x >> 1), OP.mult, ["F0", "F1"], ["+WXY"])
             for e in range(2):
-                tt(T.FZ[:, 38 * e:38 * e + 38], f(2, e), T.XS[:, 114:152], OP.mult, ["F0", "F1", "AL"], ["+FZ"])
-            for p in range(8):
-                act(T.EB[:, p:304:8], T.WXY[:, 38 * (p & 3):38 * (p & 3) + 38], ["WXY"], ["+EB"])
-            for p in range(8):
-                act(T.EA[:, p:304:8], T.FZ[:, 38 * (p >> 2):38 * (p >> 2) + 38], ["FZ"], ["+EA"])
+                tt(T.FY[:, 38 * e:38 * e + 38], ps("C", 358 + 76 * e, 396 + 76 * e), T.XS[:, 3, :], OP.mult, ["psC", "XS"], ["+FY"])
+            for x in range(4):
+                tt(T.WXZ[:, 38 * x:38 * x + 38], ps("C", 320 + 76 * (x & 1), 358 + 76 * (x & 1)), T.FS[:, 38 * (x >> 1):38 * (x >> 1) + 38],
+                   OP.mult, ["psC", "F0", "F1"], ["+WXZ"])
         if c == "W":
-            tt(T.WT[:], T.EA[:], T.EB[:], OP.mult, ["EA", "EB"], ["WT"])
-            for x in range(2):
-                act(T.WG[:, :, 16 * x:16 * x + 16], T.WT[:, 256:304], ["WT"], ["+WG"])
-            for t in range(8):
-                act(T.SEL8[:, 128 * t:128 * t + 128], T.ONE[0:48, 0:128], ["ONE", "ID16"], ["+SEL8"], scale=T.ID16[0:48, t:t + 1])
+            for p in range(8):
+                x, y = (p & 1) + 2 * (p >> 2), p >> 1 & 1
+                tt(T.WT[:, p:304:8], T.WXZ[:, 38 * x:38 * x + 38], T.FY[:, 38 * y:38 * y + 38], OP.mult, ["WXZ", "FY"], ["+WT"])
+        if c in "tu":
+            src, st = ("GO", True) if c == "t" else ("RC", False)
+            for bank, lo, hi in (("psE", 0, 512), ("psF", 512, NG)):
+                mm(ps(bank, 0, hi - lo), T.IDB[:], T[src][:, lo:hi], ["IDB", src], ["+" + bank], st, not st)
+        if c == "U":
+            lo = 0
+            for n in PAR["us"]:
+                banks = ["psE", "psF"][lo // 512:(lo + n - 1) // 512 + 1]
+                tt(T.T1[:, S + lo:S + lo + n], ps("E", lo, lo + n), T.BG[:, lo:lo + n], OP.mult, banks + ["BG"], ["T1%d" % (S + lo)])
+                sums(S + lo, n, "psA", lo // 16)
+                lo += n
+        if c == "k":
+            tt(T.WO[:], T.FL[:], T.WT[:, 0:48], OP.mult, ["FL", "WT"], ["WO"])
+        if c == "d":
+            tt(T.DW[:, 48:224], ps("A", 0, 176), T.WT[:, 0:176], OP.mult, ["psA", "WT"], ["+DW0"])
+            tt(T.DW[:, 0:48], ps("A", 0, 48), T.WO[:], OP.mult, ["psA", "WO"], ["+DW0"])
+        if c == "D":
+            tt(T.DW[:, 224:352], ps("B", 48, 176), T.WT[:, 176:304], OP.mult, ["psB", "WT"], ["DW1"])
+        if c in "hi":
+            lo = 256 * "hi".index(c)
+            copy(T.HU[:, lo:lo + 256], T.HB[:, lo:lo + 256], ["HB"], ["+HU"])
+        if c == "H":
+            copy(T.HU[:], T.HB[:], ["HB"], ["+HU"])
+        if c == "a":
+            chain[0].pop(0)()
+            if not chain[0]:
+                for t2 in range(2):
+                    turn(T.psT0[0:96, 128 * t2:128 * t2 + 128], T.PU[:, 0:6, t2:32:2], ["Pa0", "Pb0", "Pc0"], ["+psT0"])
+                if not PAR["zv"]:
+                    act(T.ZIN[0:96, :], T.psT0[0:96, 0:256], ["psT0"], ["+ZIN"])
+                rows(0)
         if c == "b":
-            v, hi, mid, lo = T.SG[:, 7:96:8], T.PG[:, :, 0:2], T.PG[:, :, 2:4], T.PG[:, :, 4:6]
-            steps = [lambda: scan(T.SG[:], T.KEEP[:, 0:96], T.DG[:], ["KEEP", "DG"], ["SG"]),
-                     lambda: copy(hi, v, ["SG"], ["+PG"]),
-                     lambda: tt(T.RG[:], v, hi, OP.subtract, ["SG", "PG"], ["RG"]),
-                     lambda: copy(mid, T.RG[:], ["RG"], ["+PGm"]),
-                     lambda: (tt(lo, T.RG[:], mid, OP.subtract, ["RG", "PGm"], ["+PGl"]), step("z"))]
-            tt(T.DG[:], T.RET[:], T.WG[:], OP.mult, ["RET", "WG"], ["DG"])
-            rad(0, lambda: steps.pop(0)())
-        if c == "z":
-            for t2 in range(2):
-                mm(T.psD[0:96, 128 * t2:128 * t2 + 128], T.PG[:, :, t2:32:2], T.IDB[:], ["PG", "PGm", "PGl", "IDB"], ["+psD"])
-            act(T.ZIN[0:96, :], T.psD[0:96, 0:256], ["psD"], ["+ZIN"])
+            chain[1].pop(0)()
+            if not chain[1]:
+                rows(1)
+        if c == "r":
+            for v in range(4 - pairs):
+                spread_r(v)
+        if c == "y" and PAR["zv"]:
+            copy(T.ZIN[0:96, :], T.psT0[0:96, 0:256], ["psT0"], ["+ZIN"])
         if c == "s":
             copy(T.Z[:, 0:S].indirect(T.ZL[:, 0:16]), T.ZIN[:], ["ZL", "ZIN"], ["Z"])
-            act(T.ZG[:], T.Z[:, 0:S].indirect(T.GU[:, 0:48]), ["Z", "GU"], ["ZG"])
+            act(T.ZG[:], T.Z[:, 0:S].indirect(go_u), ["Z", "CU"], ["ZG"])
             send("3", "ZG", "ZF", CAP)
+            for v in range(4 - pairs):
+                spread_z(v)
+        if c == "z":
+            for v in range(4 - pairs, min(6, 8 - pairs)):
+                spread_z(v)
+        if c == "L" and lits:
+            lit(*lits.pop(0))
 
-    for c in PAR["order"]:
-        step(c)
-    for t in range(4):
-        spread(t)
-    todo = [None, None, (0, 256), (256, 256), (512, 256), (768, 256), (1024, 512), (1536, 512)]
-    rad(1, lambda: lit(*todo.pop(0)) if todo[0] else todo.pop(0))
-    for x in todo:
-        lit(*x)
-    copy(T.HU[:], T.HB[:], ["HB"], ["HU"])
-    for t in range(4, 8):
-        spread(t)
-        lit(512 * t, 512)
-    for j, q in enumerate(others):
-        bank = ("psD", "ps3", "psC")[j]
-        mm(T[bank][:, 0:256], T.SELO[:, 128 * j:128 * j + 128], T.ZF[:, 256 * j:256 * j + 256], ["SELO", "ZF"], ["+" + bank])
-        tt(T.LIT[:, S + CAP * q:S + CAP * q + CAP], T[bank][:, 0:256], T.BFO[:, 256 * j:256 * j + 256], OP.mult, [bank, "BFO"], ["+LIT"])
+    while order:
+        step(order.pop(0))
+    assert done[0] == 32
+
+    calls, first, p0, col = [], [], P - na, 0
+    for i, u in enumerate(sets):
+        first.append(col)
+        for c in u:
+            calls.append([])
+            for nb in c:
+                calls[-1].append((i, col, nb, p0))
+                col, p0 = col + 16 * nb, p0 + 128 * nb
+        col = -(-col // 128) * 128
+    units = [u for c in calls for u in c]
+    wait("S", ("sentb", None, "D"))
+    for k in range(8):
+        dma("S", "dprg", T.PRG[16 * k:16 * k + 16, 0:nv], T.pro[:, nv * k:nv * k + nv], [], ["+PRG"])
+    for i, c, nb, p0 in units:
+        dma("S", "dprg", T.PRA[c % 128:c % 128 + 16 * nb, c - c % 128:c - c % 128 + 128], T.pro[:, p0:p0 + 128 * nb], [], ["+PRA"])
+
+    for j in range(3):
+        act(T.SELO[:, 128 * j:128 * j + 128], T.ONE[:, 0:128], ["ONE", "GS", "Ec"], ["+SELO"],
+            scale=T.GS[:, there[j]:there[j] + 1], bias=T.EC[:, 8:9])
+    zero(T.E4[:], 68, ["E4"])
+    act(T.E4[:, 3:67:4], T.ID16[:], ["ID16"], ["+E4"])
+    while lits:
+        step("L")
+    for v in range(4 - pairs, 8 - pairs):
+        if v >= 6:
+            spread_z(v)
+        spread_r(v)
+    for v in range(4 - pairs, 8 - pairs):
+        lit(v, 0, 512)
+    cut, (b0, b1) = min(max(r, 1), 2), (("psE", "psF") if pairs == 2 else ("psC", "psD"))
+    for j in range(3):
+        at = 512 + CAP * (j - cut)
+        mm(ps(b0, at, at + CAP), T.SELO[:, 128 * j:128 * j + 128], T.ZF[:, CAP * j:CAP * j + CAP], ["SELO", "ZF"], ["+" + (b0 if j < cut else b1)])
+    for lo, hi, bank in ((0, cut, b0), (cut, 3, b1)):
+        tt(T.LIT[:, S + CAP * others[lo]:S + CAP * (others[lo] + hi - lo)], ps(b0, 512 + CAP * (lo - cut), 512 + CAP * (hi - cut)),
+           T.BFO[:, CAP * lo:CAP * hi], OP.mult, [bank, "BFO"], ["+LIT"])
 
     win = T.LIT[:, 0:S + N * CAP]
-    nc, v1, v2 = PAR["na"], PAR["v1"], PAR["v2"]
-    c0, m = 1024 - 16 * nc, 64 - nc + PAR["n2"]
+    v1, v2 = PAR["v1"], PAR["v2"]
 
     def on_vector(k, a, b, key):
         src = T.PRG if k == 0 else T.ACC
-        tt(T.ACC[:, 16 * a:16 * b], win.indirect(T.HU[:, 64 * k + a:64 * k + b]), src[:, 16 * a:16 * b], OP.add,
+        tt(T.ACC[:, 16 * a:16 * b], win.indirect(T.HU[:, cw * k + a:cw * k + b]), src[:, 16 * a:16 * b], OP.add,
            ["LIT", "HU", "PRG"] + ([key] if k else []), [key])
-
-    def on_scalar(a, b, bank, key):
-        n, g0 = 16 * (b - a), 128 * (a - 64 + nc)
-        mm(T[bank][:, 0:n], T.IDB[:], T.PRG[:, 16 * a:16 * b], ["IDB", "PRG"], ["+" + bank], True, False)
-        for k in range(8):
-            out = T.GA[:, g0 + n * k:g0 + n * k + n]
-            act(out, win.indirect(T.HU[:, 64 * k + a:64 * k + b]), ["LIT", "HU"], ["GA%d%s" % (k, key)])
-            mm(T[bank][:, 0:n], T.IDF[:], out, ["IDF", "GA%d%s" % (k, key)], ["+" + bank], False, k == 7)
-            if k == 7 and key == "d":
-                act(T.ACC[:, 16 * b:1024], T.psB[:, 0:1024 - 16 * b], ["psB"], ["ACCc"])
 
     def store(lo, hi, keys, queues):
         for k in range(8):
-            dma(queues[k % len(queues)], "dy", T.y[:, 1024 * k + lo:1024 * k + hi], T.ACC[16 * k:16 * k + 16, lo:hi], keys, [])
+            dma(queues[k % len(queues)], "dy", T.y[:, nv * k + lo:nv * k + hi], T.ACC[16 * k:16 * k + 16, lo:hi], keys, [])
 
-    on_scalar(m, 64, "psB", "c")
-    on_scalar(64 - nc, m, "ps0", "d")
-    act(T.ACC[:, c0:16 * m], T.ps0[:, 0:16 * m - c0], ["ps0"], ["ACCd"])
-    x, y, z = (0, v1, "ACCa"), (v1, v2, "ACCz"), (v2, 64 - nc, "ACCb")
-    for k in range(4):
-        on_vector(k, *x)
-        on_vector(k, *y)
-    for k in range(4):
-        on_vector(k + 4, *x)
-        on_vector(k, *z)
-    for k in range(4, 8):
-        on_vector(k, *y)
-        on_vector(k, *z)
-    store(0, 16 * v1, ["ACCa"], "S")
-    store(16 * m, 1024, ["ACCc"], "S")
-    store(16 * v1, 16 * m, ["ACCz", "ACCb", "ACCd"], "SA")
+    def gather(call):
+        p0, n = call[0][3], 128 * sum(u[2] for u in call)
+        key = "GA%d" % p0
+        act(T.GA[:, p0 - (P - na):p0 - (P - na) + n], win.indirect(T.HU[:, p0 // 16:(p0 + n) // 16]), ["LIT", "HU"], [key])
+        for i, c, nb, p in call:
+            bank, c0, st = ("psE", "psF")[i % 2], p - (P - na), 4 // nb
+            for b in range(nb):
+                mm(ps(bank, c - first[i], c - first[i] + 16 * nb), T.GA[:, c0 + 128 * b:c0 + 128 * b + 128],
+                   T.E4[:, 3 - st * b:67 - st * b:st], ["E4", key], ["+" + bank], b == 0, b == nb - 1)
+
+    def width(i):
+        return 16 * sum(sum(c) for c in sets[i])
+
+    def back(i):
+        m, bank, src, c = width(i), ("psD", "psB")[i % 2], ("psE", "psF")[i % 2], first[i]
+        act(T.SUM[:, c:c + m], ps(src, 0, m), [src], ["SUM%d" % i])
+        for x in range(0, m, 128):
+            n = min(128, m - x)
+            mm(ps(bank, x, x + 128, n), T.IDB[0:n, 0:n], T.PRA[0:n, c + x:c + x + 128], ["IDB", "PRA"], ["+" + bank], True, False)
+            mm(ps(bank, x, x + 128, n), T.SUM[:, c + x:c + x + n], T.IDF[:], ["IDF", "SUM%d" % i], ["+" + bank], False, True)
+
+    def out(i):
+        m, bank, c = width(i), ("psD", "psB")[i % 2], first[i]
+        n, w = min(m, 128), -(-m // 128) * 128
+        act(T.OUT[0:n, c:c + w], ps(bank, 0, w, n), [bank], ["OUT%d" % i])
+
+    def store_set(i):
+        for j, c, nb, p0 in units:
+            if j == i:
+                dma("S", "dy", T.y[:, p0:p0 + 128 * nb], T.OUT[c % 128:c % 128 + 16 * nb, c - c % 128:c - c % 128 + 128], ["OUT%d" % i], [])
+
+    n2 = PAR["n2"]
+
+    def last(k):
+        n, c0 = 16 * n2, na + 16 * n2 * k
+        if k == 0:
+            mm(ps("A", 0, n), T.IDB[:], T.PRG[:, nv - n:nv], ["IDB", "PRG"], ["+psA"], True, False)
+        act(T.GA[:, c0:c0 + n], win.indirect(T.HU[:, cw * k + cw - n2:cw * k + cw]), ["LIT", "HU"], ["GL%d" % k])
+        mm(ps("A", 0, n), T.IDF[:], T.GA[:, c0:c0 + n], ["IDF", "GL%d" % k], ["+psA"], False, k == 7)
+
+    if PAR.get("probe") == 2:
+        act(T.T1[:, 0:900], T.LIT[:, 0:900], ["LIT"], ["T10"])
+    flow = [lambda c=c: gather(c) for c in calls] + [lambda k=k: last(k) for k in range(8)]
+    ends = [n for n, c in enumerate(calls) if n + 1 == len(calls) or calls[n + 1][0][0] != c[0][0]]
+    for n, f in enumerate(flow):
+        f()
+        for i, e in enumerate(ends):
+            if n == e + PAR["lag"][i][0]:
+                back(i)
+            if n == e + PAR["lag"][i][1]:
+                out(i)
+    act(T.ACC[:, nv - 16 * n2:nv], ps("A", 0, 16 * n2), ["psA"], ["ACCc"])
+    x, y, z = (0, v1, "ACCa"), (v1, v2, "ACCz"), (v2, cw - n2, "ACCb")
+    if v2 == cw - n2:
+        for k in range(8):
+            on_vector(k, *x)
+            on_vector(k, *y)
+        for i in range(len(sets)):
+            store_set(i)
+        store(0, nv, ["ACCa", "ACCz", "ACCc"], "SA")
+    else:
+        for k in range(4):
+            on_vector(k, *x)
+            on_vector(k, *y)
+        for k in range(4):
+            on_vector(k + 4, *x)
+            on_vector(k, *z)
+        for k in range(4, 8):
+            on_vector(k, *y)
+            on_vector(k, *z)
+        store(0, 16 * v1, ["ACCa"], "S")
+        for i in range(len(sets)):
+            store_set(i)
+        store(16 * v1, nv, ["ACCz", "ACCb", "ACCc"], "SA")
 
     for s in SEMAPHORES:
         wait("G" if s.startswith("sent") else "S", (s, None, "D"))

@@ -5,38 +5,40 @@ F32, BF, I32, U16 = "float32", "bfloat16", "int32", "uint16"
 N, S, P, CAP = 4, 4096, 8192, 256
 NG = (N - 1) * CAP
 MAGIC = 25165824.0
-PAR = {"dense_v": 112, "sets": (((4,), (4,), (4,), (4,)),), "n2": 10, "lag": ((2, 5),), "v1": 22, "v2": 32,
-       "pre": "bkBlLyQYmfnFwdVOHMDogxeEpX", "mid": "P", "order": "C6xOBAS43w3t5nW(4ukU)4da1a1a1aarDybszhbibLbLb", "early": 6, "zp": 2048, "zq": 768, "zv": 1, "fcv": 0,
-       "us": (384, 384), "pairs": 0, "lits": ((0, 0, 256), (0, 256, 512), (1, 0, 512), (2, 0, 512), (3, 0, 512))}
+RW = 1056
+PAR = {"sets": (((4,), (4,), (4,), (4,)),), "n2": 12, "flow": "LLLLSSLSSLbLLo", "v1": 16, "v2": 26, "sums": "xy" * 4 + "xz" * 4 + "yz" * 4,
+       "early": (0, 8, 9, 0), "hopb": "sent2", "late": 0, "round": "", "bas": (0, 0, 4096, 4096), "fcv": 0, "zv": 1056, "zg": (768, 1024, 1536), "za": 768, "hu": 4, "pair": 2, "via": "psB psD psB psD psB",
+       "us": (512, 256), "named": "psD", "pool": "ID", "tabq": "SA", "z0": 256,
+       "queues": ("SSASSA", "SSSASSSA", "SS"), "alb": 0, "ring": "psE psF psC psD psA psB", "wide": (2, 4), "seen": "psE psF", "hop2": 0, "hop3": ("AVA",),
+       "order": "k0 b Ba z1 tab k yv l Yv q0 d K0 q1 wv q2 L Wv Q E7 f2 O m H M g F x D3 X D13 o p E9 G1 h1 G2 h2 v5 v9 P rv t1 c G3 v1 z h3 t2 v5 R q w "
+                "B S K t3 W U a U a a n K2 a n a n a n K3 e Ra0 Ra1 n n i j Zv i Z j j J i J i N j j"}
 
 SB = {
-    "X": ([128, 1024], BF), "Y": ([128, 1024], BF), "W": ([128, 1056], BF), "WD": ([128, 4096], BF),
+    "X": ([128, 1024], BF), "Y": ([128, 8, 16, 8], BF), "W": ([128, 1056], BF), "WD": ([128, 4096], BF),
     "BAS": ([128, S], BF), "BG": ([128, NG], BF), "BFO": ([128, NG], BF), "OG": ([128, 48], U16), "OF": ([128, 48], U16),
-    "FC": ([128, NG], BF), "RC": ([128, NG], BF), "GO": ([128, NG], BF), "GOA": ([128, NG], BF),
-    "POS": ([128, 256], F32), "P3": ([16, 1024], F32), "GBI": ([16, 48], I32), "GBF": ([16, 72], F32), "BM": ([128, 256], I32),
-    "DU": ([128, 256], U16), "CR": ([128, 216], I32), "CU": ([128, 216], U16),
+    "FC": ([128, NG], BF), "RC": ([128, NG], BF), "CG": ([128, S], BF),
+    "POS": ([128, 256], F32), "P3": ([16, 768], F32), "GBI": ([16, 48], I32), "GBF": ([16, 48], F32), "BM": ([128, 256], I32),
+    "DU": ([128, 256], U16), "CR": ([128, 120], I32), "CU": ([128, 120], U16), "QF": ([128, 48], F32), "QU": ([128, 24], U16),
     "ZL": ([128, 16], U16), "BU": ([128, 256], F32), "B2": ([128, 256], BF), "OU": ([128, 256], U16),
-    "MASK": ([128, NG + 384], BF), "MX": ([128, 384], F32), "MB": ([128, NG], BF),
-    "T1": ([128, S + NG], F32), "XS": ([128, 4, 38], F32), "XT": ([128, 114], F32), "XD": ([128, 114], F32),
-    "FS": ([128, 76], F32), "FY": ([128, 76], F32), "WXZ": ([128, 152], F32), "WT": ([128, 304], F32),
-    "FL": ([128, 48], F32), "WO": ([128, 48], F32),
-    "DW": ([128, 352], F32), "SC": ([128, 352], F32), "R1": ([128, 44], F32), "PU": ([128, 22, 32], BF), "R": ([128, 512], BF),
-    "ZIN": ([128, 256], BF), "Z": ([128, S], BF), "ZG": ([128, NG], BF), "ZF": ([128, NG], BF), "LIT": ([128, S + N * CAP], F32),
+    "MASK": ([128, 384], BF), "MX": ([128, 384], F32), "MB": ([128, 384], BF), "SK": ([128, 128], BF), "FG": ([128, 142], BF),
+    "T1": ([128, S + NG], F32), "XS": ([128, 4, 38], F32), "XD": ([128, 114], F32), "EIG": ([128, 34], F32),
+    "FS": ([128, 76], F32), "WXZ": ([128, 152], F32), "WT": ([128, 304], F32),
+    "DW": ([128, 304], F32), "SC": ([128, 304], F32), "R1": ([128, 38], F32), "PU": ([128, 4, 16, 8], BF), "PN": ([128, 8, 16, 2], BF),
+    "GZ": ([128, 48], U16), "ZIN": ([128, 256], BF), "Z": ([128, RW + S], BF), "ZG": ([128, NG], BF), "ZF": ([128, NG], BF), "LIT": ([128, S + N * CAP], F32),
     "HA": ([128, 512], I32), "HB": ([128, 512], I32), "HU": ([128, 512], U16),
     "PRG": ([128, 1024], BF), "ACC": ([128, 1024], F32), "GA": ([128, 5120], F32),
     "PRA": ([128, 768], BF), "SUM": ([128, 768], F32), "OUT": ([128, 768], F32), "E4": ([128, 68], F32),
-    "ONE": ([128, 256], F32), "SL": ([16, 240], F32), "SL2": ([16, 34], F32),
-    "REP": ([16, 128], F32), "REPB": ([16, 128], F32), "I16": ([128, 32], I32), "I16B": ([128, 32], I32),
-    "ID16": ([128, 16], F32), "GS": ([128, 8], F32), "GSB": ([128, 8], BF), "GS3": ([128, 26], F32), "EC": ([128, 24], F32),
-    "FGO": ([128, 144], BF), "WB": ([128, 128], BF), "IDF": ([128, 128], F32), "IDB": ([128, 128], BF),
-    "SEL2": ([128, 256], BF), "SELO": ([128, 512], BF), "KEEP": ([128, 224], F32),
-    "TMP": ([128, 1536], F32), "BAS2": ([128, 1536], BF),
+    "ONE": ([128, 256], F32), "SL": ([16, 240], F32), "SL2": ([128, 34], F32),
+    "REP": ([16, 128], F32), "REPB": ([16, 136], F32), "I16": ([128, 32], I32), "I16B": ([128, 32], I32),
+    "ID16": ([128, 16], F32), "GS": ([128, 8], F32), "GS3": ([128, 28], F32), "EC": ([128, 24], F32),
+    "WB": ([128, 128], BF), "IDF": ([128, 128], F32), "IDB": ([128, 128], BF),
+    "SEL2": ([128, 256], BF), "ONEB": ([128, 128], BF), "KEEP": ([128, 256], F32),
 }
 SCRATCH = {k: ("sbuf", v[0], v[1]) for k, v in SB.items()}
 SCRATCH["PS"] = ("psum", [128, 6 * 512], F32)
 for _b in ("psT0", "psT1"):
     SCRATCH[_b] = ("psum", [128, 1024], BF)
-SEMAPHORES = ["V", "A", "P", "G", "dpro", "dgo", "dgb", "dpos", "dalb", "dbas", "dp3", "dha", "dhb", "dprg", "dzl", "db2", "dsw", "dy",
+SEMAPHORES = ["V", "A", "P", "G", "dpro0", "dpro1", "dgo", "dgb", "dpos", "dalb", "dbas0", "dbas1", "dbas2", "dp3", "dha", "dhb", "dprg", "dzl", "dtab", "dy",
               "hop1", "hop2", "hop3", "hopb", "sent1", "sent2", "sent3", "sentb"]
 
 
@@ -80,6 +82,7 @@ def rank_program(g, core, T, topo):
         toks = []
         for k in reads:
             st = state.setdefault(k, {"w": [], "base": [], "r": []})
+            assert st["w"], k
             toks += st["w"]
             if k.startswith("ps"):
                 toks += [t for t in st["r"] if t[2] != q]
@@ -113,18 +116,22 @@ def rank_program(g, core, T, topo):
         cnt[sem] += 16
         after((sem, None, "D"), reads, writes)
 
-    def send(hop, src, dst, width):
-        before("G", [src], [])
+    def send(hop, src, dst, width, js=range(N - 1), key=None):
+        before("G", [key or src], [])
         tr = []
-        for j, q in enumerate(others):
+        for j in js:
+            q = others[j]
             rid, pid, _ = topo.addr(cores[q])
             tr.append(RemoteDMATransfer(dst_ids=[DstId(rid=rid, pnc=pid)], dma_engine_mask=masks[cores[q]], remote_sem=T.sem["hop" + hop],
                                         src=T[src][:, width * j:width * j + width],
                                         dst=T[dst][:, width * there[j]:width * there[j] + width]))
         g.remote_dma_fused(tr, local_sem=T.sem["sent" + hop])
-        cnt["sent" + hop] += neng * len(others)
-        cnt["hop" + hop] += neng * len(others)
+        cnt["sent" + hop] += neng * len(tr)
+        cnt["hop" + hop] += neng * len(tr)
         state.setdefault(dst, {"w": [], "base": [], "r": []})["w"].append(("hop" + hop, None, "D"))
+
+    far = [j for j, q in enumerate(others) if topo.chip(cores[q]) != topo.chip(core)]
+    near = [j for j in range(N - 1) if j not in far]
 
     V, A, PE = g.vector, g.scalar, g.tensor
 
@@ -134,6 +141,9 @@ def rank_program(g, core, T, topo):
 
     def copy(out, in_, rd, w):
         op("V", lambda: V.tensor_copy(out, in_), rd, w)
+
+    def mset(out, c, w):
+        op("V", lambda: V.memset(out, c), [], w)
 
     def tt(out, a, b, o, rd, w):
         op("V", lambda: V.tensor_tensor(out, a, b, o), rd, w)
@@ -154,8 +164,8 @@ def rank_program(g, core, T, topo):
     def mm(out, lhsT, rhs, rd, w, start=True, stop=True):
         op("P", lambda: PE.matmul(out, lhsT, rhs, start, stop), rd, w)
 
-    def turn(out, in_, rd, w):
-        op("P", lambda: PE.transpose(out, in_, T.IDB[:]), rd + ["IDB"], w)
+    def turn(out, in_, rd, w, rows=slice(0, 128)):
+        op("P", lambda: PE.transpose(out, in_, T.IDB[rows, rows]), rd + ["IDB"], w)
 
     start = [0]
 
@@ -177,111 +187,171 @@ def rank_program(g, core, T, topo):
     def zero(out, n, w, lo=0, hi=128):
         act(out, T.ONE[lo:hi, 0:n], ["ONE"], w, scale=0.0)
 
+    qs = PAR["queues"]
     if r > 0:
         dma("A", "dgo", T.GBI[:, 0:16 * r], T.go[:, 0:16 * r], [], ["+GOI"])
     if r < N - 1:
         dma("A", "dgo", T.GBI[:, 16 * r:48], T.go[:, 16 * r + 16:64], [], ["+GOI"])
     for k in range(6):
-        dma("SSA"[k % 3], "dpos", T.POS[16 * k:16 * k + 16, :], T.pos[16 * (k // 2):16 * (k // 2) + 16, :], [], ["+POS"])
-    dma("S", "dpro", T.X[:], T.pro[:], [], ["X"])
+        dma(qs[0][k], "dpos", T.POS[16 * k:16 * k + 16, :], T.pos[16 * (k // 2):16 * (k // 2) + 16, :], [], ["+POS"])
+    for h in range(2):
+        dma("S", "dpro%d" % h, T.X[64 * h:64 * h + 64, :], T.pro[8 * h:8 * h + 8, :], [], ["X%d" % h])
     for p in range(8):
-        dma("S", "dgb", T.BM[16 * p:16 * p + 16, :], T.bmap[:], [], ["+BM"])
-    for e in range(2):
-        dma("S", "dalb", T.POS[96 + 16 * e:112 + 16 * e, :], T.alb[:], [], ["+ALB"])
-    for a in range(3):
-        dma("S", "dp3", T.P3[:, 256 * a:256 * a + 256], T.pos[16 * a:16 * a + 16, :], [], ["+P3"])
-    dma("S", "dp3", T.P3[:, 768:1024], T.alb[:], [], ["+P3"])
-    for p in range(8):
-        dma("S", "dbas", T.BAS[16 * p:16 * p + 16, :], T.bas[:], [], ["+BAS"])
+        dma(qs[1][p], "dgb", T.BM[16 * p:16 * p + 16, :], T.bmap[:], [], ["+BM"])
 
-    op("V", lambda: V.memset(T.ONE[:], 1.0), [], ["ONE"])
+    def albedo():
+        for e in range(2):
+            dma(qs[2][e], "dalb", T.POS[96 + 16 * e:112 + 16 * e, :], T.alb[:], [], ["+ALB"])
+
+    def places():
+        for a in range(3):
+            dma("S", "dp3", T.P3[:, 256 * a:256 * a + 256], T.pos[16 * a:16 * a + 16, :], [], ["+P3"])
+
+    if PAR["alb"] == 0:
+        albedo()
+
+    cuts = PAR["bas"]
+
+    def basis(n):
+        lo, hi = cuts[n], cuts[n + 1]
+        for p in range(8 * (lo < hi)):
+            dma("S", "dbas%d" % n, T.BAS[16 * p:16 * p + 16, lo:hi], T.bas[:, lo:hi], [], ["+BAS%d" % n])
+
+    def bas(lo, hi):
+        return ["BAS%d" % n for n in range(3) if max(lo, cuts[n]) < min(hi, cuts[n + 1])]
+
+    basis(0)
+
+    zv = PAR["zv"]
+    mset(T.ONE[:], 1.0, ["ONE"])
+    mset(T.REPB[:, 0:8], 0.0, ["+REPB"])
     iota(T.I16[:, 0:16], [[-1, 16]], 16, 1, ["I16"])
     iota(T.I16[:, 16:24], [[-16, 8]], 0, 1, ["I8"])
+    sel(T.REPB[:, 8:136], T.ONE[0:16, 0:128], [[0, 4], [-1, 2], [-2, 16]], OP.is_equal, 0, 1, ["ONE"], ["+REPB"])
     sel(T.REP[:], T.ONE[0:16, 0:128], [[0, 8], [-1, 16]], OP.is_equal, 0, 1, ["ONE"], ["REP"])
-    sel(T.REPB[:], T.ONE[0:16, 0:128], [[0, 4], [-1, 32]], OP.is_equal, 16, 1, ["ONE"], ["REPB"])
     sel(T.IDB[:], T.ONE[:, 0:128], [[-1, 128]], OP.is_equal, 0, 1, ["ONE"], ["IDB"])
-    ts(T.I16B[:, 16:24], T.I16[:, 16:24], 4, OP.arith_shift_right, ["I8"], ["I8B"])
-    ts(T.I16B[:, 0:16], T.I16[:, 0:16], 15, OP.bitwise_and, ["I16"], ["I16B"])
-    ts(T.GS[:], T.I16B[:, 16:24], 0.0, OP.is_equal, ["I8B"], ["GS"])
-    ts(T.ID16[:], T.I16B[:, 0:16], 0.0, OP.is_equal, ["I16B"], ["ID16"])
-    for a, factor in enumerate((16.0, 256.0, 1.0)):
-        act(T.EC[32 * a:32 * a + 32, 1:2], T.ONE[32 * a:32 * a + 32, 0:1], ["ONE"], ["+EF"], scale=0.5 * factor)
-    zero(T.FGO[0:96, :], 144, ["FGO"], 0, 96)
-    act(T.EC[:, 16:20], T.GS[:, 1:8:2], ["GS"], ["E1"], accum_out=T.EC[:, 0:1])
-    if "A" in PAR["pre"]:
-        act(T.EC[0:96, 2:3], T.EC[0:96, 1:2], ["EF"], ["EM"], scale=-MAGIC)
-    zero(T.B2[96:128, :], 256, ["+B2"], 96, 128)
-    zero(T.W[:, 0:16], 16, ["+W"])
-    zero(T.W[:, 1040:1056], 16, ["+W"])
-    zero(T.GS3[:], 26, ["GS3"])
-    act(T.GSB[:], T.GS[:], ["GS"], ["GSB"])
-    act(T.GS3[:, 2:26:3], T.GS[:], ["GS"], ["+GS3"])
-    for a, bit in enumerate(([[0, 4], [16, 2]], [[0, 2], [16, 2], [0, 2]], [[16, 2], [0, 4]])):
+    sel(T.SK[0:96, :], T.ONE[0:96, 0:128], [[0, 8], [-16, 16]], OP.is_equal, 0, 1, ["ONE"], ["SK"])
+    for a, bit in enumerate(([[0, 4], [16, 2]], None, [[16, 2], [0, 4]])):
         rows, p0 = slice(32 * a, 32 * a + 32), 32 * a
-        iota(T.I16[rows, 24:32], bit, 15, -1, ["+IP"], p0)
         if a == 1:
             for h in range(2):
                 sel(T.WB[rows, 64 * h:64 * h + 64], T.ONE[rows, 0:64], [[16, 2], [0, 2], [1, 16]], OP.is_equal, 0, -1, ["ONE"], ["+WB"], p0)
         else:
             sel(T.WB[rows, :], T.ONE[rows, 0:128], bit + [[1, 16]], OP.is_equal, 0, -1, ["ONE"], ["+WB"], p0)
-    sel(T.SL[:], T.ONE[0:16, 0:240], [[-1, 240]], OP.is_equal, 112, 1, ["ONE"], ["SL"])
-    sel(T.SL2[:], T.ONE[0:16, 0:34], [[-1, 34]], OP.is_equal, 1, 2, ["ONE"], ["SL2"])
+    for a, factor in enumerate((16.0, 256.0, 1.0)):
+        mset(T.EC[32 * a:32 * a + 32, 1:2], 0.5 * factor, ["+EF"])
+    ts(T.I16B[:, 16:24], T.I16[:, 16:24], 4, OP.arith_shift_right, ["I8"], ["I8B"])
+    ts(T.I16B[:, 0:16], T.I16[:, 0:16], 15, OP.bitwise_and, ["I16"], ["I16B"])
+    ts(T.GS[:], T.I16B[:, 16:24], 0.0, OP.is_equal, ["I8B"], ["GS"])
+    ts(T.ID16[:], T.I16B[:, 0:16], 0.0, OP.is_equal, ["I16B"], ["ID16"])
+    ts(T.I16B[:, 17:18], T.I16[:, 16:17], 5, OP.arith_shift_right, ["I8", "GS"], ["I4B"])
+    if PAR["z0"]:
+        mset(T.Z[:, 0:PAR["z0"]], 0.0, ["+Z0"])
+    ts(T.EC[:, 5:7], T.I16B[:, 16:18], -1024.0, OP.mult, ["I8B", "I4B"], ["EQ"], 16.0, OP.add)
+    act(T.EC[:, 16:20], T.GS[:, 1:8:2], ["GS"], ["E1"], accum_out=T.EC[:, 0:1])
+    act(T.EC[0:96, 2:3], T.EC[0:96, 1:2], ["EF"], ["EM"], scale=-MAGIC)
+    zero(T.FG[:], 142, ["FG"])
+    zero(T.W[:, 0:16], 16, ["+W"])
+    zero(T.W[:, 1040:1056], 16, ["+W"])
+    act(T.EC[:, 7:8], T.EC[:, 0:1], ["E1"], ["E0"], scale=-1.0, bias=1.0)
+    zero(T.GS3[:], 28, ["GS3"])
 
-    copy(T.GBF[:, 0:48], T.GBI[:], ["GOI"], ["GBG"])
-    tt(T.GBF[:, 48:72], T.GBI[:, 24:48], T.GBI[:, 0:24], OP.subtract, ["GOI"], ["GBD"])
-    mm(ps("D", 0, 48), T.REP[:], T.GBF[:, 0:48], ["REP", "GBG"], ["+psD"])
-    mm(ps("D", 48, 72), T.REP[:], T.GBF[:, 0:24], ["REP", "GBG"], ["+psD"], True, False)
-    mm(ps("D", 48, 72), T.REPB[:], T.GBF[:, 48:72], ["REPB", "GBD"], ["+psD"], False, True)
+    def soon(c):
+        if c == "z1":
+            mset(T.Z[:, PAR["z0"]:zv], 0.0, ["+Z0"])
+        if c == "K0":
+            act(T.EIG[96:112, :], T.ONE[96:112, 0:34], ["ONE"], ["EIG"], scale=0.125)
+            for h in range(2):
+                act(T.GS3[:, 4 + h:22:6], T.GS[:, h:6:2], ["GS"], ["+GS3"])
+            act(T.GS3[:, 22:24], T.GS[:, 6:8], ["GS"], ["+GS3"], scale=0.125)
+            sel(T.SL[:], T.ONE[0:16, 0:240], [[-1, 240]], OP.is_equal, 112, 1, ["ONE"], ["SL"])
+            sel(T.SL2[96:112, :], T.EIG[96:112, :], [[-1, 34]], OP.is_equal, 1, 2, ["EIG"], ["SL2"], 96)
+        if c == "k0":
+            for e in range(2):
+                mm(ps("D", 48, 72), T.REPB[:, 8 - 8 * e:136 - 8 * e], T.GBF[:, e:48:2], ["REPB", "GBG"], ["+psD"], e == 0, e == 1)
+            mm(ps("D", 0, 48), T.REP[:], T.GBF[:], ["REP", "GBG"], ["+psD"])
 
-    d, go_u = PAR["dense_v"], T.CU[:, 0:48]
-    halves = ((0, 24), (24, 48)) if "n" in PAR["pre"] else ((0, 48),)
+    copy(T.GBF[:], T.GBI[:], ["GOI"], ["GBG"])
+
+    go_u = T.CU[:, 0:48]
+    sets = PAR["sets"]
+    na = 128 * sum(sum(sum(c) for c in u) for u in sets)
+    cw = (P - na) // 128
+    nv = 16 * cw
+    pair = PAR["pair"]
+    jobs = [(v, v + 2) for v in range(pair)]
+    jobs += [(t,) for t in range(8) if not any(t in j for j in jobs)]
+
+    turns = [(T.HA[:, cw * k:cw * k + cw], T.hit[16 * k:16 * k + 16, 0:8 * cw], "dha", [], "+HA") for k in range(8)]
+    turns += [(T.HB[:, 8 * cw:512], T.hit[:, 8 * cw:512], "dhb", [], "+HB")]
+    turns += [(T.HB[16 * k:16 * k + 16, 0:8 * cw], T.HA[k:128:8, 0:8 * cw], "dhb", ["HA"], "+HB") for k in range(8)]
+
+    def lists(n):
+        for _ in range(PAR["early"][n]):
+            out, in_, sem, rd, w = turns.pop(0)
+            dma("S", sem, out, in_, rd, [w])
+
+    lists(0)
+
+    def zeros(n):
+        at = zv + sum(PAR["zg"][:n])
+        if PAR["zg"][n]:
+            fill(T.Z[:, at:at + PAR["zg"][n]], PAR["zg"][n], 0, ["+ZS"])
 
     def ready(c):
         if c == "k":
             copy(T.CR[:, 0:72], ps("D", 0, 72), ["psD"], ["GI"])
         if c == "l":
-            ts(T.CR[0:96, 144:216], T.CR[0:96, 0:72], 15, OP.bitwise_and, ["GI"], ["+CR"])
-            ts(T.CR[96:128, 144:216], T.CR[96:128, 0:72], 8, OP.arith_shift_right, ["GI"], ["+CR"])
-            ts(T.CR[0:96, 72:144], T.CR[0:96, 0:72], 4, OP.arith_shift_right, ["GI"], ["+CR"])
-            ts(T.CR[96:128, 72:144], T.CR[96:128, 0:72], 255, OP.bitwise_and, ["GI"], ["+CR"])
+            ts(T.CR[:, 96:120], T.CR[:, 48:72], 15, OP.bitwise_and, ["GI"], ["CR2"])
+            ts(T.CR[:, 72:96], T.CR[:, 48:72], 4, OP.arith_shift_right, ["GI"], ["CR1"])
         if c == "L":
-            lo = 144 * ("Q" in PAR["pre"])
-            copy(T.CU[:, lo:216], T.CR[:, lo:216], ["CR", "GI"], ["CL", "+CU"])
-            for a, b in halves:
-                act(T.MASK[:, 16 * a:16 * b], T.ID16[:, 0:16].indirect(T.CU[:, 144 + a:144 + b]), ["ID16", "CL"], ["MASK%d" % a])
+            ts(T.CR[96:128, 72:96], T.CR[96:128, 48:72], 255, OP.bitwise_and, ["GI"], ["CR1"])
+            ts(T.CR[96:128, 96:120], T.CR[96:128, 48:72], 8, OP.arith_shift_right, ["GI"], ["CR2"])
         if c == "Q":
-            copy(T.CU[:, 0:144], T.CR[:, 0:144], ["CR", "GI"], ["+CU"])
+            copy(T.CU[:], T.CR[:], ["CR1", "CR2", "GI"], ["CU"])
         if c == "H":
-            act(T.MASK[:, NG:NG + 384], T.ID16[:, 0:16].indirect(T.CU[:, 192:216]), ["ID16", "CL"], ["MASKH"])
+            act(T.MASK[:], T.ID16[:, 0:16].indirect(T.CU[:, 96:120]), ["ID16", "CU"], ["MASK"])
+        if c == "q0":
+            ts(T.QF[:, 0:24], T.CR[:, 96:120], 256.0, OP.mult, ["CR2", "EQ"], ["QF0"], T.EC[:, 6:7], OP.add)
+        if c == "q1":
+            tt(T.QF[:, 24:48], T.QF[:, 0:24], T.CR[:, 72:96], OP.add, ["QF0", "CR1"], ["QF1"])
+        if c == "q2":
+            ts(T.QU[:], T.QF[:, 24:48], 1040.0, OP.min, ["QF1"], ["QU"])
+        if c == "tab":
+            for k in range(12):
+                dma(PAR["tabq"][k % len(PAR["tabq"])], "dtab", T.Z[16 * (k // 6) + k % 6:128:32, 16:1040], T.B2[16 * (k % 6):16 * (k % 6) + 16, :], ["B2", "Z0"], ["+TAB"])
+            if PAR["alb"] == 1:
+                albedo()
+            basis(1)
+            places()
         if c == "b":
             ts(T.BU[0:96, :], T.POS[0:96, :], T.EC[0:96, 0:1], OP.subtract, ["POS", "E1"], ["BU"], MAGIC, OP.add)
-        if c == "B":
+        if c == "Bv":
             ts(T.B2[0:96, :], T.BU[0:96, :], MAGIC, OP.subtract, ["BU", "EF"], ["+B2"], T.EC[0:96, 1:2], OP.mult)
-        if c == "A":
+        if c == "Ba":
             act(T.B2[0:96, :], T.BU[0:96, :], ["BU", "EF", "EM"], ["+B2"], scale=T.EC[0:96, 1:2], bias=T.EC[0:96, 2:3])
-        if c in "yz":
+        if c in ("yv", "ya", "Yv", "Ya"):
+            h = "yY".index(c[0])
+            rows = slice(64 * h, 64 * h + 64)
             for p in range(8):
-                turn(T["psT%d" % (p // 4)][:, 128 * (p % 4):128 * (p % 4) + 128], T.X[:, p:1024:8], ["X"], ["+psT%d" % (p // 4)])
-            (copy if c == "y" else act)(T.Y[:, 0:512], T.psT0[:, 0:512], ["psT0"], ["+Y"])
-        if c == "Y":
-            copy(T.Y[:, 512:1024], T.psT1[:, 0:512], ["psT1"], ["+Y"])
-            for p in range(8):
-                turn(T["psT%d" % (p // 4)][:, 128 * (p % 4):128 * (p % 4) + 128], T.Y[:, p:1024:8], ["Y"], ["+psT%d" % (p // 4)])
-        if c in "wW":
-            (act if c == "w" else copy)(T.W[:, 16:528], T.psT0[:, 0:512], ["psT0"], ["+W"])
-        if c in "vV":
-            (act if c == "v" else copy)(T.W[:, 528:1040], T.psT1[:, 0:512], ["psT1"], ["+W"])
-        if c in "mn":
-            a, b = halves[c == "n"]
-            tt(T.MB[:, 16 * a:16 * b], T.B2[:, 0:256].indirect(T.CU[:, 72 + a:72 + b]), T.MASK[:, 16 * a:16 * b], OP.mult,
-               ["B2", "CU", "MASK%d" % a], ["+MB"])
-        if c == "f":
-            ts(T.I16B[0:96, 24:32], T.I16[0:96, 24:32], 4, OP.arith_shift_right, ["IP"], ["IPB"])
-        if c == "F":
-            ts(T.FGO[0:96, 15:128:16], T.I16B[0:96, 24:32], 0.0, OP.is_equal, ["IPB"], ["+FGO"])
+                turn(T["psT%d" % h][:, 64 * p:64 * p + 64], T.X[rows, p:1024:8], ["X%d" % h], ["+psT%d" % h], rows)
+            (copy if c[1] == "v" else act)(T.Y[:, :, 8 * h:8 * h + 8, :], T["psT%d" % h][:, 0:512], ["psT%d" % h], ["+Y"])
+        if c in ("Yv", "Ya"):
+            for b in range(8):
+                turn(T["psT%d" % (b // 4)][:, 128 * (b % 4):128 * (b % 4) + 128], T.Y[:, :, :, b], ["Y"], ["+psT%d" % (b // 4)])
+        if c in ("wa", "wv"):
+            (act if c == "wa" else copy)(T.W[:, 16:528], T.psT0[:, 0:512], ["psT0"], ["+W"])
+        if c in ("Wa", "Wv"):
+            (act if c == "Wa" else copy)(T.W[:, 528:1040], T.psT1[:, 0:512], ["psT1"], ["+W"])
+        if c == "m":
+            act(T.MB[:], T.Z[:, 0:RW].indirect(T.QU[:]), ["Z0", "TAB", "QU"], ["MB"])
+        if c == "f2":
+            mm(ps("F", 256, 264), T.SK[0:96, :], T.WB[0:96, 0:128:16], ["SK", "WB"], ["+psF"])
+            for h in range(2):
+                act(T.FG[:, 14 + h:142:16], ps("F", 256, 264), ["psF", "E0", "E1"], ["+FG"], scale=T.EC[:, 7 - 7 * h:8 - 7 * h])
         if c == "M":
-            for rho in range(16):
-                mm(ps("E", 256, 304), T.FGO[0:96, 15 - rho:143 - rho], T.MB[0:96, rho:NG:16], ["FGO", "MB"], ["+psE"], rho == 0, rho == 15)
+            for i in range(8):
+                mm(ps("E", 256, 304), T.FG[:, 14 - 2 * i:142 - 2 * i], T.MB[:, i:384:8], ["FG", "MB"], ["+psE"], i == 0, i == 7)
         if c == "g":
             copy(T.OG[:], ps("E", 256, 304), ["psE"], ["OG"])
         if c == "O":
@@ -290,230 +360,245 @@ def rank_program(g, core, T, topo):
             copy(T.OU[:], ps("F", 0, 256), ["psF"], ["OU"])
         if c == "d":
             ts(T.DU[:], T.BM[:], float(16 - 1024 * r), OP.add, ["BM"], ["DU"], 1040.0, OP.min)
-        if c == "D":
-            act(T.WD[:, 16 * d:4096], T.W[:, 0:1056].indirect(T.DU[:, d:256]), ["W", "DU"], ["+WD"])
-        if c == "e":
-            copy(T.WD[:, 0:256], T.W[:, 0:1056].indirect(T.DU[:, 0:16]), ["W", "DU"], ["+WD"])
-        if c == "E":
-            lo = 16 * ("e" in PAR["pre"])
-            copy(T.WD[:, 16 * lo:16 * d], T.W[:, 0:1056].indirect(T.DU[:, lo:d]), ["W", "DU"], ["+WD"])
         if c == "p":
             for c8 in range(8):
                 mm(ps("C", 0, 96), T.SL[:, 112 - 16 * c8:240 - 16 * c8], T.P3[:, c8:768:8], ["SL", "P3"], ["+psC"], c8 == 0, c8 == 7)
+            wait("P", ("P", None, "X"))
             for h in range(2):
-                mm(ps("C", 96, 128), T.P3[:, 768 + 128 * h:896 + 128 * h], T.SL2[:, 1 - h:33 - h], ["SL2", "P3"], ["+psC"], h == 0, h == 1)
+                mm(ps("C", 96, 128), T.POS[96:112, 128 * h:128 * h + 128], T.SL2[96:112, 1 - h:33 - h], ["SL2", "ALB"], ["+psC"], h == 0, h == 1)
         if c == "x":
-            tt(T.MX[:], T.POS[:, 0:256].indirect(T.CU[:, 120:144]), T.MASK[:, NG:NG + 384], OP.mult, ["POS", "ALB", "CU", "MASKH"], ["MX"])
+            tt(T.MX[:], T.POS[:, 0:256].indirect(T.CU[:, 72:96]), T.MASK[:], OP.mult, ["POS", "ALB", "CU", "MASK"], ["MX"])
         if c == "X":
             for b in range(3):
-                mm(ps("C", 128, 152), T.MX[:, 128 * b:128 * b + 128], T.GS3[:, 2 - b:26 - b], ["MX", "GS3"], ["+psC"], b == 0, b == 2)
+                mm(ps("C", 128, 152), T.MX[:, 128 * b:128 * b + 128], T.GS3[:, 4 - 2 * b:28 - 2 * b], ["MX", "GS3"], ["+psC"], b == 0, b == 2)
+        if c == "F":
+            send("1", "OG", "OF", 16)
+            fill(T.PU[:], 512, 0, ["+PU"])
+            fill(T.PN[:], 256, 0, ["+PU"])
+            zeros(0)
+            wait("S", ("sent1", None, "D"))
+            basis(2)
+            for j, lo, hi in ((0, 0, 80), (1, 80, 96), (2, 96, 128)):
+                dma("S", "dzl", T.ZL[lo:hi, :], T.CU[lo:hi, 16 * j:16 * j + 16], ["CU"], ["+ZL"])
+            lists(1)
 
-    for c in PAR["pre"]:
-        ready(c)
+    held, hold, nb = [], [False], PAR["named"]
 
-    zp, zq = PAR["zp"], PAR["zq"]
-    if PAR.get("probe") == 1:
-        before("G", ["OG"], [])
-        fill(T.GA[:, 0:448], 448, 0, [])
-    send("1", "OG", "OF", 16)
-    fill(T.PU[:], 704, 0, ["PU"])
-    sel(T.KEEP[:], T.ONE[:, 0:224], [[0, 28], [1, 8]], OP.not_equal, 0, 0, ["ONE"], ["KEEP"])
-    for c in PAR["mid"]:
-        if c == "P":
-            act(T.XS[:, :, 6:38], ps("C", 0, 128), ["psC"], ["+XS"])
-            act(T.XS[:, :, 0:6], ps("C", 128, 152), ["psC"], ["+XS"])
-            act(T.XT[:], T.XS[:, 0:3, :], ["XS"], ["XT"], bias=MAGIC)
-            act(ps("C", 200, 314), T.XT[:], ["XT"], ["+psC"], bias=-MAGIC)
-        if c == "B":
-            act(T.BG[:], T.BAS[:, 0:S].indirect(go_u), ["BAS", "CU"], ["BG"])
+    def sums(col, n):
+        for c in range(col, col + n, 128):
+            if c < S:
+                mm(ps("A", c // 16, c // 16 + 8), T.T1[:, c:c + 128], T.GS[:], ["T1%d" % col, "GS"], ["+psA"])
+            else:
+                at, c0 = (c - S) // 16, c - c % 256
+                mm(ps(nb, at, at + 8), T.T1[:, c0 + c % 256 // 128:c0 + 256:2], T.GS[:], ["T1%d" % col, "GS"], ["+" + nb])
 
-    sets = PAR["sets"]
-    na = 128 * sum(sum(sum(c) for c in u) for u in sets)
-    cw = (P - na) // 128
-    nv = 16 * cw
-    early = PAR["early"]
-    for k, (lo, hi) in enumerate(((0, 16), (16, 32), (32, 48), (48, 64), (64, 80), (80, 128))):
-        dma("S", "dzl", T.ZL[lo:hi, :], T.CU[lo:hi, 16 * (k % 3):16 * (k % 3) + 16], ["CU"], ["+ZL"])
-    wait("S", ("sent1", None, "D"))
-    for e in range(2 if PAR["pairs"] else 0):
-        n = 512 * PAR["pairs"]
-        dma("S", "db2", T.BAS2[64 * e:64 * e + 64, 0:n], T.BAS[64 * e:64 * e + 64, n * e:n * e + n], ["BAS"], ["+BAS2"])
-    for k in range(early):
-        dma("S", "dha", T.HA[:, cw * k:cw * k + cw], T.hit[16 * k:16 * k + 16, 0:8 * cw], [], ["+HA"])
-
-    def hop2():
-        n = PAR["fcv"]
-        act(T.FC[:, 16 * n:NG], T.WD[:, 0:4096].indirect(T.OF[:, n:48]), ["WD", "OF"], ["+FC"])
-        if n:
-            copy(T.FC[:, 0:16 * n], T.WD[:, 0:4096].indirect(T.OF[:, 0:n]), ["WD", "OF"], ["+FC"])
-        send("2", "FC", "RC", CAP)
-        fill(T.Z[:, 0:zq], zq, 0, ["+Z"])
-        wait("S", ("sent2", None, "D"))
-        for k in range(early, 8):
-            dma("S", "dha", T.HA[:, cw * k:cw * k + cw], T.hit[16 * k:16 * k + 16, 0:8 * cw], [], ["+HA"])
-        dma("S", "dhb", T.HB[:, 8 * cw:512], T.hit[:, 8 * cw:512], [], ["+HB"])
-        for k in range(8):
-            dma("S", "dhb", T.HB[16 * k:16 * k + 16, 0:8 * cw], T.HA[k:128:8, 0:8 * cw], ["HA"], ["+HB"])
-
-    def sums(col, n, bank, pcol):
-        for c in range(n // 128):
-            mm(ps(bank, pcol + 8 * c, pcol + 8 * c + 8), T.T1[:, col + 128 * c:col + 128 * c + 128], T.GS[:], ["T1%d" % col, "GS"], ["+" + bank])
-
-    selr = T.SELO[:, 384:512]
-    ring, pairs = ["psE", "psF", "psC", "psD", "psA", "psB", "psE", "psF"], PAR["pairs"]
-
-    def pieces(lo, hi, n):
-        v, rest = T.SC[:, lo + 7:hi:8], T.R1[:, lo // 8:hi // 8]
-        top, mid, low = (T.PU[:, lo // 16:hi // 16, 2 * x:2 * x + 2] for x in range(3))
-        return [lambda: scan(T.SC[:, lo:hi], T.KEEP[:, 0:hi - lo], T.DW[:, lo:hi], ["KEEP", "DW" + n], ["SC" + n]),
-                lambda: copy(top, v, ["SC" + n, "PU"], ["Pa" + n]),
-                lambda: tt(rest, v, top, OP.subtract, ["SC" + n, "Pa" + n], ["R1" + n]),
-                lambda: copy(mid, rest, ["R1" + n], ["Pb" + n]),
-                lambda: tt(low, rest, mid, OP.subtract, ["R1" + n, "Pb" + n], ["Pc" + n])]
-
-    def rows(h):
-        n = "%d" % h
-        for u in range(2):
-            turn(T.psT1[:, 128 * u:128 * u + 128], T.PU[:, 6 + 8 * h:14 + 8 * h, u:32:2], ["Pa" + n, "Pb" + n, "Pc" + n], ["+psT1"])
-        act(T.R[:, 256 * h:256 * h + 256], T.psT1[:, 0:256], ["psT1"], ["R" + n])
-
-    def parts(v):
-        return [(v, 0, 64), (v + pairs, 64, 128)] if v < pairs else [(v + pairs, 0, 128)]
-
-    def spread_r(v):
-        for t, lo, hi in parts(v):
-            for e in range(2):
-                p0, h = 32 * (t % 4), t // 4
-                mm(ps(ring[v], 256 * e, 256 * e + 256, hi, lo), T.SEL2[p0:p0 + 32, 128 * e + lo:128 * e + hi],
-                   T.R[p0:p0 + 32, 256 * h:256 * h + 256], ["SELa", "SELb", "R%d" % h], ["+" + ring[v]], e == lo == h == 0, e == h == 1)
-
-    def spread_z(v):
-        for t, lo, hi in parts(v):
-            mm(ps(ring[v], 0, 512, hi, lo), T.SELO[:, 384 + lo:384 + hi], T.Z[:, 512 * t:512 * t + 512], ["SELR", "Z"], ["+" + ring[v]],
-               t >= 4, t < 4 and hi == 128)
-
-    def lit(v, lo, hi):
-        if v >= pairs:
-            c = 512 * (v + pairs)
-            tt(T.LIT[:, c + lo:c + hi], ps(ring[v], lo, hi), T.BAS[:, c + lo:c + hi], OP.mult, [ring[v], "BAS"], ["+LIT"])
-            return
-        c = 512 * v
-        tt(T.TMP[:, c + lo:c + hi], ps(ring[v], lo, hi), T.BAS2[:, c + lo:c + hi], OP.mult, [ring[v], "BAS2"], ["+TMP%d" % v])
-        for t, p0, p1 in parts(v) if hi == 512 else ():
-            for half in range(2):
-                dma("S", "dsw", T.LIT[64 * half:64 * half + 64, 512 * t:512 * t + 512], T.TMP[p0:p1, c:c + 512], ["TMP%d" % v], ["+LIT"])
-
-    done, order, held, hold = [0], list(PAR["order"]), [], [False]
-    chain, lits = [pieces(0, 224, "0"), pieces(224, 352, "1")], [x for x in PAR["lits"] if x[0] < 4 - pairs]
+    done, tiles, dense, named, via = [0], {}, [0], [0], PAR["via"].split()
 
     def step(c):
-        if c.isdigit():
-            t, n = done[0], int(c)
-            tt(T.T1[:, 128 * t:128 * (t + n)], T.WD[:, 0:4096].indirect(T.OU[:, 8 * t:8 * (t + n)]), T.BAS[:, 128 * t:128 * (t + n)],
-               OP.mult, ["WD", "OU", "BAS"], ["T1%d" % (128 * t)])
-            held.append((128 * t, 128 * n, ("psA", "psB")[t // 16], 48 + 8 * (t % 16)))
-            done[0] = t + n
-        if c in "()":
+        if c[0] in "DE":
+            lo, hi = 8 * dense[0], 8 * (dense[0] + int(c[1:]))
+            (act if c[0] == "D" else copy)(T.WD[:, 16 * lo:16 * hi], T.W[:, 0:1056].indirect(T.DU[:, lo:hi]), ["W", "DU"], ["+WD"])
+            dense[0] = hi // 8
+        if c[0] == "v":
+            lo, hi = 128 * done[0], 128 * (done[0] + int(c[1:]))
+            tt(T.T1[:, lo:hi], T.WD[:, 0:4096].indirect(T.OU[:, lo // 16:hi // 16]), T.BAS[:, lo:hi], OP.mult, ["WD", "OU"] + bas(lo, hi), ["T1%d" % lo])
+            held.append((lo, hi - lo))
+            done[0] = hi // 128
+        if c[0] in "Ght" and c[1:].isdigit():
+            n = int(c[1:])
+            if c[0] == "G":
+                tiles[n] = 128 * done[0]
+                done[0] += 4
+            lo, bank = tiles[n], via[n - 1]
+            if c[0] == "G":
+                act(T.CG[:, lo:lo + 512], T.WD[:, 0:4096].indirect(T.OU[:, lo // 16:lo // 16 + 32]), ["WD", "OU"], ["CG%d" % n])
+            elif c[0] == "h":
+                mm(ps(bank, 0, 512), T.IDB[:], T.CG[:, lo:lo + 512], ["IDB", "CG%d" % n], ["+" + bank])
+            else:
+                tt(T.T1[:, lo:lo + 512], ps(bank, 0, 512), T.BAS[:, lo:lo + 512], OP.mult, [bank] + bas(lo, lo + 512), ["T1%d" % lo])
+                held.append((lo, 512))
+        if c in ("(", ")", "a"):
             hold[0] = c == "("
         while held and not hold[0]:
             sums(*held.pop(0))
-        if c == "x":
-            tt(T.XD[:], T.XS[:, 0:3, :], ps("C", 200, 314), OP.subtract, ["XS", "psC"], ["XD"])
-            act(ps("C", 396, 472), T.XD[:, 0:76], ["XD"], ["+psC"], FN.Abs)
-            act(T.FS[:, 38:76], T.XD[:, 76:114], ["XD"], ["F1"], FN.Abs, scale=0.125)
-            act(ps("C", 320, 396), ps("C", 396, 472), ["psC"], ["+psC"], bias=1.0, scale=-1.0)
-            act(T.FS[:, 0:38], T.FS[:, 38:76], ["F1"], ["F0"], bias=0.125, scale=-1.0)
-        if c == "C":
-            hop2()
-        if c == "O":
-            act(T.GO[:], T.WD[:, 0:4096].indirect(T.OG[:, 0:48]), ["WD", "OG"], ["GO"])
-        if c == "B":
-            act(T.BG[:], T.BAS[:, 0:S].indirect(go_u), ["BAS", "CU"], ["BG"])
-        if c == "S":
-            wait("G", ("sent2", None, "D"))
-            send("b", "BG", "BFO", CAP)
-            fill(T.Z[:, zq:zp], zp - zq, 0, ["+Z"])
-            fill(T.LIT[:, S + CAP * r:S + CAP * r + CAP], CAP, 0, ["+LIT"])
-            sel(T.IDF[:], T.ONE[:, 0:128], [[-1, 128]], OP.is_equal, 0, 1, ["ONE"], ["IDF"])
-        if c == "A":
-            act(T.GOA[:], T.GO[:], ["GO"], ["GOA"], FN.Abs)
-            zero(T.ZIN[96:128, :], 256, ["+ZIN"], 96, 128)
-        if c == "n":
-            for c6 in range(6):
-                mm(ps("D", 304 + 8 * c6, 312 + 8 * c6), T.GOA[:, 128 * c6:128 * c6 + 128], T.GSB[:], ["GOA", "GSB"], ["+psD"])
-            act(T.FL[:], ps("D", 304, 352), ["psD"], ["FL"], FN.Sign)
-            act(T.Z[:, zp:S], T.BAS[:, zp:S], ["BAS"], ["+Z"], scale=0.0)
-            act(T.EC[:, 16:19], T.GS[:, 0:3], ["GS", "E1"], ["Ea"], scale=-1.0, accum_out=T.EC[:, 4:5])
-            act(T.EC[:, 20:23], T.GS[:, 3:6], ["GS"], ["Eb"], accum_out=T.EC[:, 5:6])
-            act(T.EC[:, 8:9], T.EC[:, 4:5], ["Ea", "Eb"], ["Ec"], bias=T.EC[:, 5:6])
-            act(T.SEL2[:, 128:256], T.ONE[:, 0:128], ["ONE", "E1"], ["SELb"], scale=T.EC[:, 0:1])
-            act(selr, T.ONE[:, 0:128], ["ONE", "Ec"], ["SELR"], scale=T.EC[:, 8:9])
-            act(T.SEL2[:, 0:128], T.SEL2[:, 128:256], ["SELb"], ["SELa"], scale=-1.0, bias=1.0)
+        if c == "P":
+            act(T.XS[:, :, 6:38], ps("C", 0, 128), ["psC"], ["+XS"])
+            act(T.XS[:, :, 0:6], ps("C", 128, 152), ["psC"], ["+XS"])
+        if c == "rv":
+            ts(ps("C", 152, 266), T.XS[:, 0:3, :], MAGIC, OP.add, ["XS"], ["+psC"], MAGIC, OP.subtract)
+        if c == "ra":
+            act(T.XD[:], T.XS[:, 0:3, :], ["XS"], ["XD"], bias=MAGIC)
+            act(ps("C", 152, 266), T.XD[:], ["XD"], ["+psC"], bias=-MAGIC)
+        if c == "z":
+            tt(T.XD[:], T.XS[:, 0:3, :], ps("C", 152, 266), OP.subtract, ["XS", "psC"], ["XD"])
+            act(ps("C", 348, 424), T.XD[:, 0:76], ["XD"], ["+psC"], FN.Abs)
+            act(T.FS[:, 38:76], T.XD[:, 76:114], ["XD"], ["F1"], FN.Abs)
+        if c == "q":
+            act(ps("C", 272, 348), ps("C", 348, 424), ["psC"], ["+psC"], bias=1.0, scale=-1.0)
+            act(T.FS[:, 0:38], T.FS[:, 38:76], ["F1"], ["F0"], bias=1.0, scale=-1.0)
         if c == "w":
-            for e in range(2):
-                tt(T.FY[:, 38 * e:38 * e + 38], ps("C", 358 + 76 * e, 396 + 76 * e), T.XS[:, 3, :], OP.mult, ["psC", "XS"], ["+FY"])
             for x in range(4):
-                tt(T.WXZ[:, 38 * x:38 * x + 38], ps("C", 320 + 76 * (x & 1), 358 + 76 * (x & 1)), T.FS[:, 38 * (x >> 1):38 * (x >> 1) + 38],
+                tt(T.WXZ[:, 38 * x:38 * x + 38], ps("C", 272 + 76 * (x & 1), 310 + 76 * (x & 1)), T.FS[:, 38 * (x >> 1):38 * (x >> 1) + 38],
                    OP.mult, ["psC", "F0", "F1"], ["+WXZ"])
+            for e in range(2):
+                tt(ps("C", 424 + 38 * e, 462 + 38 * e), ps("C", 310 + 76 * e, 348 + 76 * e), T.XS[:, 3, :], OP.mult, ["psC", "XS"], ["+FY"])
         if c == "W":
             for p in range(8):
                 x, y = (p & 1) + 2 * (p >> 2), p >> 1 & 1
-                tt(T.WT[:, p:304:8], T.WXZ[:, 38 * x:38 * x + 38], T.FY[:, 38 * y:38 * y + 38], OP.mult, ["WXZ", "FY"], ["+WT"])
-        if c in "tu":
-            src, st = ("GO", True) if c == "t" else ("RC", False)
+                tt(T.WT[:, p:304:8], T.WXZ[:, 38 * x:38 * x + 38], ps("C", 424 + 38 * y, 462 + 38 * y), OP.mult, ["WXZ", "FY", "psC"], ["+WT"])
+        if c == "c":
+            if PAR["hop2"]:
+                for js in (far, near):
+                    lo, hi = min(js), max(js) + 1
+                    act(T.FC[:, CAP * lo:CAP * hi], T.WD[:, 0:4096].indirect(T.OF[:, 16 * lo:16 * hi]), ["WD", "OF"], ["FC%d" % lo])
+                    send("2", "FC", "RC", CAP, js, "FC%d" % lo)
+            else:
+                n = PAR["fcv"]
+                act(T.FC[:, 16 * n:NG], T.WD[:, 0:4096].indirect(T.OF[:, n:48]), ["WD", "OF"], ["+FC"])
+                if n:
+                    copy(T.FC[:, 0:16 * n], T.WD[:, 0:4096].indirect(T.OF[:, 0:n]), ["WD", "OF"], ["+FC"])
+                send("2", "FC", "RC", CAP)
+            sel(T.KEEP[:], T.ONE[:], [[0, 32], [1, 8]], OP.not_equal, 0, 0, ["ONE"], ["KEEP"])
+            zeros(1)
+            wait("S", ("sent2", None, "D"))
+            lists(2)
+        if c == "K3" and pair:
+            act(T.BAS[64:128, 0:512 * pair], T.BAS[64:128, 1024:1024 + 512 * pair], [], ["+" + k for k in bas(0, S)] + ["BASP"])
+        if c == "B":
+            act(T.BG[:], T.BAS[:, 0:S].indirect(go_u), bas(0, S) + ["CU"], ["BG"])
+        if c == "S":
+            wait("G", (PAR["hopb"], None, "D"))
+            send("b", "BG", "BFO", CAP)
+            wait("S", ("sentb", None, "D"))
+            lists(3)
+            zeros(2)
+            fill(T.LIT[:, S + CAP * r:S + CAP * r + CAP], CAP, 0, ["+LIT"])
+            sel(T.IDF[:], T.ONE[:, 0:128], [[-1, 128]], OP.is_equal, 0, 1, ["ONE"], ["IDF"])
+        if c == "R":
             for bank, lo, hi in (("psE", 0, 512), ("psF", 512, NG)):
-                mm(ps(bank, 0, hi - lo), T.IDB[:], T[src][:, lo:hi], ["IDB", src], ["+" + bank], st, not st)
+                mm(ps(bank, 0, hi - lo), T.IDB[:], T.RC[:, lo:hi], ["IDB", "RC"], ["+" + bank])
         if c == "U":
-            lo = 0
-            for n in PAR["us"]:
-                banks = ["psE", "psF"][lo // 512:(lo + n - 1) // 512 + 1]
-                tt(T.T1[:, S + lo:S + lo + n], ps("E", lo, lo + n), T.BG[:, lo:lo + n], OP.mult, banks + ["BG"], ["T1%d" % (S + lo)])
-                sums(S + lo, n, "psA", lo // 16)
-                lo += n
-        if c == "k":
-            tt(T.WO[:], T.FL[:], T.WT[:, 0:48], OP.mult, ["FL", "WT"], ["WO"])
-        if c == "d":
-            tt(T.DW[:, 48:224], ps("A", 0, 176), T.WT[:, 0:176], OP.mult, ["psA", "WT"], ["+DW0"])
-            tt(T.DW[:, 0:48], ps("A", 0, 48), T.WO[:], OP.mult, ["psA", "WO"], ["+DW0"])
-        if c == "D":
-            tt(T.DW[:, 224:352], ps("B", 48, 176), T.WT[:, 176:304], OP.mult, ["psB", "WT"], ["DW1"])
-        if c in "hi":
-            lo = 256 * "hi".index(c)
-            copy(T.HU[:, lo:lo + 256], T.HB[:, lo:lo + 256], ["HB"], ["+HU"])
-        if c == "H":
-            copy(T.HU[:], T.HB[:], ["HB"], ["+HU"])
-        if c == "a":
-            chain[0].pop(0)()
-            if not chain[0]:
-                for t2 in range(2):
-                    turn(T.psT0[0:96, 128 * t2:128 * t2 + 128], T.PU[:, 0:6, t2:32:2], ["Pa0", "Pb0", "Pc0"], ["+psT0"])
-                if not PAR["zv"]:
-                    act(T.ZIN[0:96, :], T.psT0[0:96, 0:256], ["psT0"], ["+ZIN"])
-                rows(0)
-        if c == "b":
-            chain[1].pop(0)()
-            if not chain[1]:
-                rows(1)
-        if c == "r":
-            for v in range(4 - pairs):
-                spread_r(v)
-        if c == "y" and PAR["zv"]:
-            copy(T.ZIN[0:96, :], T.psT0[0:96, 0:256], ["psT0"], ["+ZIN"])
-        if c == "s":
-            copy(T.Z[:, 0:S].indirect(T.ZL[:, 0:16]), T.ZIN[:], ["ZL", "ZIN"], ["Z"])
-            act(T.ZG[:], T.Z[:, 0:S].indirect(go_u), ["Z", "CU"], ["ZG"])
-            send("3", "ZG", "ZF", CAP)
-            for v in range(4 - pairs):
-                spread_z(v)
-        if c == "z":
-            for v in range(4 - pairs, min(6, 8 - pairs)):
-                spread_z(v)
-        if c == "L" and lits:
-            lit(*lits.pop(0))
+            lo = named[0]
+            n = PAR["us"][lo > 0]
+            banks = ["psE", "psF"][lo // 512:(lo + n - 1) // 512 + 1]
+            tt(T.T1[:, S + lo:S + lo + n], ps("E", lo, lo + n), T.BG[:, lo:lo + n], OP.mult, banks + ["BG"], ["T1%d" % (S + lo)])
+            sums(S + lo, n)
+            named[0] += n
+        if c == "e":
+            ts(T.GZ[:], T.CR[:, 0:48], T.EC[:, 4:5], OP.add, ["GI", "EZ"], ["GZ"], T.EC[:, 3:4], OP.min)
 
-    while order:
-        step(order.pop(0))
-    assert done[0] == 32
+    def pieces(lo, hi, dots, bank, buf, n):
+        v, rest = T.SC[:, lo + 7:hi:8], T.R1[:, lo // 8:hi // 8]
+        top, mid, low = (buf[x] for x in range(3))
+        cut = act if n in PAR["round"] else copy
+        return [lambda: tt(T.DW[:, lo:hi], dots, T.WT[:, lo:hi], OP.mult, [bank, "WT"], ["DW" + n]),
+                lambda: scan(T.SC[:, lo:hi], T.KEEP[:, 0:hi - lo], T.DW[:, lo:hi], ["KEEP", "DW" + n], ["SC" + n]),
+                lambda: cut(top, v, ["SC" + n, "PU"], ["Pa" + n]),
+                lambda: tt(rest, v, top, OP.subtract, ["SC" + n, "Pa" + n], ["R1" + n]),
+                lambda: cut(mid, rest, ["R1" + n], ["Pb" + n]),
+                lambda: tt(low, rest, mid, OP.subtract, ["R1" + n, "Pb" + n], ["Pc" + n])]
+
+    chain = {"a": pieces(48, 304, ps("A", 0, 256), "psA", [T.PU[:, :, x, :] for x in range(3)], "a"),
+             "n": pieces(0, 48, ps(nb, 0, 48), nb, [T.PN[:, 4:7, x, :] for x in range(3)], "n")}
+
+    ring, ahead, nh, hu = PAR["ring"].split(), [0, 0, 0], PAR["hu"], [0]
+
+    def parts(v):
+        return [(jobs[v][0], 0, 64), (jobs[v][1], 64, 128)] if v < pair else [(jobs[v][0], 0, 128)]
+
+    def spread_r(v):
+        a, h = jobs[v][0] // 2, jobs[v][0] % 2
+        p0, c = 32 * (a // 2), 64 if len(jobs[v]) == 2 else 128 * (a % 2)
+        mm(ps(ring[v], 0, 512), T.SEL2[p0:p0 + 32, c:c + 128], T.Z[p0:p0 + 32, 16 + 512 * h:528 + 512 * h],
+           ["SELa", "SELb", "RH%d" % h], ["+" + ring[v]], True, False)
+        ahead[0] = v + 1
+
+    def spread_z(v):
+        if v >= ahead[0]:
+            spread_r(v)
+        for t, lo, hi in parts(v):
+            c = RW + 512 * t
+            mm(ps(ring[v], 0, 512, hi, lo), T.ONEB[64:128, lo:hi], T.Z[64:128, c:c + 512], ["ONEB", "ZS"], ["+" + ring[v]], False, True)
+        ahead[1] = v + 1
+
+    def spread(v):
+        if ahead[1] == v < len(jobs) and ring[v] not in ring[ahead[2]:v]:
+            spread_z(v)
+
+    halves = []
+
+    def lit():
+        v = ahead[2]
+        c = 512 * jobs[v][0]
+        spread(v)
+        if v < pair:
+            d, key = 512 * jobs[v][1], "LP%d" % v
+            tt(T.LIT[:, c:c + 512], ps(ring[v], 0, 512), T.BAS[:, c:c + 512], OP.mult, [ring[v], "BASP"], ["+LIT", key])
+            act(T.LIT[0:64, d:d + 512], T.LIT[64:128, c:c + 512], [key], ["+LIT"])
+            act(T.LIT[64:128, d:d + 512], T.LIT[64:128, c:c + 512], [key], ["+LIT"])
+            halves.append(lambda: act(T.LIT[64:128, c:c + 512], T.LIT[0:64, c:c + 512], [], ["+LIT", key]))
+        else:
+            n = 1 + (v in PAR["wide"])
+            spread(v + n - 1)
+            tt(T.LIT[:, c:c + 512 * n], ps(ring[v], 0, 512 * n), T.BAS[:, c:c + 512 * n], OP.mult, ring[v:v + n] + bas(0, S), ["+LIT"])
+            v += n - 1
+        ahead[2] = v + 1
+
+    def close(c):
+        if c in chain:
+            chain[c].pop(0)()
+        if c == "a" and not chain[c]:
+            for u in range(8):
+                turn(T["psT%d" % (u // 4)][0:64, 128 * (u % 4):128 * (u % 4) + 128], T.PU[:, :, :, u], ["Paa", "Pba", "Pca"], ["+psT%d" % (u // 4)])
+        if c == "n" and not chain[c]:
+            for t2 in range(2):
+                mm(T.PS[:, 512 + t2:768:2], T.PN[:, :, :, t2], T.IDB[:], ["Pan", "Pbn", "Pcn", "IDB"], ["+psB"])
+        if c[:2] in ("Rv", "Ra"):
+            h = int(c[2])
+            (copy if c[1] == "v" else act)(T.Z[0:64, 16 + 512 * h:528 + 512 * h], T["psT%d" % h][0:64, 0:512], ["psT%d" % h, "MB"], ["RH%d" % h])
+        if c == "cp":
+            halves.pop(0)()
+        if c == "i":
+            lo, hi = 512 * hu[0] // nh, 512 * (hu[0] + 1) // nh
+            copy(T.HU[:, lo:hi], T.HB[:, lo:hi], ["HB"], ["+HU"])
+            hu[0] += 1
+        if c in ("Zv", "Za"):
+            (copy if c == "Zv" else act)(T.ZIN[:], ps("B", 0, 256), ["psB"], ["ZIN"])
+        if c == "j":
+            spread_r(ahead[0])
+        if c == "J":
+            spread_z(ahead[1])
+        if c == "Z":
+            copy(T.Z[:, RW:RW + S].indirect(T.ZL[:, 0:16]), T.ZIN[:], ["ZL", "ZIN", "Z0"], ["ZS"])
+        if c == "N":
+            for js, by in zip((far, near) if len(PAR["hop3"]) == 2 else (far + near,), PAR["hop3"]):
+                for j, e in zip(js, by):
+                    (act if e == "A" else copy)(T.ZG[:, CAP * j:CAP * j + CAP], T.Z[:, 0:RW + S].indirect(T.GZ[:, 16 * j:16 * j + 16]),
+                                                ["Z0", "ZS", "RH0", "RH1", "GZ"], ["+ZG%d" % len(js)])
+                send("3", "ZG", "ZF", CAP, js, "ZG%d" % len(js))
+        if c == "li":
+            lit()
+        if c == "K":
+            act(T.EC[0:64, 3:4], T.ONE[0:64, 0:1], ["ONE"], ["+EZ"], scale=1040.0)
+            act(T.EC[64:128, 3:4], T.ONE[64:128, 0:1], ["ONE"], ["+EZ"], scale=65535.0)
+            act(T.EC[64:128, 4:5], T.ONE[64:128, 0:1], ["ONE"], ["+EZ"], scale=float(RW))
+            act(T.EC[0:64, 4:5], T.EC[0:64, 5:6], ["EQ"], ["+EZ"])
+            if PAR["za"]:
+                act(T.Z[:, RW + S - PAR["za"]:RW + S], T.BAS[:, 0:PAR["za"]], bas(0, S), ["+ZS"], scale=0.0)
+        if c == "K2":
+            act(T.SEL2[:, 128:256], T.ONE[:, 0:128], ["ONE", "E1"], ["SELb"], scale=T.EC[:, 0:1])
+            act(T.ONEB[:], T.ONE[:, 0:128], ["ONE"], ["ONEB"])
+            act(T.SEL2[:, 0:128], T.SEL2[:, 128:256], ["SELb"], ["SELa"], scale=-1.0, bias=1.0)
+            zero(T.E4[:], 68, ["E4"])
+            act(T.E4[:, 3:67:4], T.ID16[:], ["ID16"], ["+E4"])
+
+    for c in PAR["order"].split():
+        soon(c)
+        ready(c)
+        step(c)
+        close(c)
+    assert done[0] == 32 == dense[0] and not chain["a"] and not chain["n"] and not held
+    assert zv + sum(PAR["zg"]) + PAR["za"] == RW + S
 
     calls, first, p0, col = [], [], P - na, 0
     for i, u in enumerate(sets):
@@ -525,31 +610,29 @@ def rank_program(g, core, T, topo):
                 col, p0 = col + 16 * nb, p0 + 128 * nb
         col = -(-col // 128) * 128
     units = [u for c in calls for u in c]
-    wait("S", ("sentb", None, "D"))
+    if PAR["late"]:
+        wait("S", ("sent3", None, "D"))
     for k in range(8):
         dma("S", "dprg", T.PRG[16 * k:16 * k + 16, 0:nv], T.pro[:, nv * k:nv * k + nv], [], ["+PRG"])
     for i, c, nb, p0 in units:
         dma("S", "dprg", T.PRA[c % 128:c % 128 + 16 * nb, c - c % 128:c - c % 128 + 128], T.pro[:, p0:p0 + 128 * nb], [], ["+PRA"])
 
-    for j in range(3):
-        act(T.SELO[:, 128 * j:128 * j + 128], T.ONE[:, 0:128], ["ONE", "GS", "Ec"], ["+SELO"],
-            scale=T.GS[:, there[j]:there[j] + 1], bias=T.EC[:, 8:9])
-    zero(T.E4[:], 68, ["E4"])
-    act(T.E4[:, 3:67:4], T.ID16[:], ["ID16"], ["+E4"])
-    while lits:
-        step("L")
-    for v in range(4 - pairs, 8 - pairs):
-        if v >= 6:
-            spread_z(v)
-        spread_r(v)
-    for v in range(4 - pairs, 8 - pairs):
-        lit(v, 0, 512)
-    cut, (b0, b1) = min(max(r, 1), 2), (("psE", "psF") if pairs == 2 else ("psC", "psD"))
+    for v in range(ahead[2], ahead[2] + 6):
+        spread(v)
+    while ahead[2] < len(jobs):
+        lit()
+        while halves and ahead[2] >= pair:
+            halves.pop(0)()
+        for v in range(ahead[2], ahead[2] + 6):
+            spread(v)
+    while hu[0] < nh:
+        close("i")
+    cut, (ba, bb) = min(max(r, 1), 2), PAR["seen"].split()
     for j in range(3):
         at = 512 + CAP * (j - cut)
-        mm(ps(b0, at, at + CAP), T.SELO[:, 128 * j:128 * j + 128], T.ZF[:, CAP * j:CAP * j + CAP], ["SELO", "ZF"], ["+" + (b0 if j < cut else b1)])
-    for lo, hi, bank in ((0, cut, b0), (cut, 3, b1)):
-        tt(T.LIT[:, S + CAP * others[lo]:S + CAP * (others[lo] + hi - lo)], ps(b0, 512 + CAP * (lo - cut), 512 + CAP * (hi - cut)),
+        mm(ps(ba, at, at + CAP), T.ONEB[:], T.ZF[:, CAP * j:CAP * j + CAP], ["ONEB", "ZF"], ["+" + (ba if j < cut else bb)])
+    for lo, hi, bank in ((0, cut, ba), (cut, 3, bb)):
+        tt(T.LIT[:, S + CAP * others[lo]:S + CAP * (others[lo] + hi - lo)], ps(ba, 512 + CAP * (lo - cut), 512 + CAP * (hi - cut)),
            T.BFO[:, CAP * lo:CAP * hi], OP.mult, [bank, "BFO"], ["+LIT"])
 
     win = T.LIT[:, 0:S + N * CAP]
@@ -604,40 +687,23 @@ def rank_program(g, core, T, topo):
         act(T.GA[:, c0:c0 + n], win.indirect(T.HU[:, cw * k + cw - n2:cw * k + cw]), ["LIT", "HU"], ["GL%d" % k])
         mm(ps("A", 0, n), T.IDF[:], T.GA[:, c0:c0 + n], ["IDF", "GL%d" % k], ["+psA"], False, k == 7)
 
-    if PAR.get("probe") == 2:
-        act(T.T1[:, 0:900], T.LIT[:, 0:900], ["LIT"], ["T10"])
-    flow = [lambda c=c: gather(c) for c in calls] + [lambda k=k: last(k) for k in range(8)]
-    ends = [n for n, c in enumerate(calls) if n + 1 == len(calls) or calls[n + 1][0][0] != c[0][0]]
-    for n, f in enumerate(flow):
-        f()
-        for i, e in enumerate(ends):
-            if n == e + PAR["lag"][i][0]:
-                back(i)
-            if n == e + PAR["lag"][i][1]:
-                out(i)
+    at = {"S": 0, "L": 0, "b": 0, "o": 0}
+    for c in PAR["flow"]:
+        {"S": lambda n: gather(calls[n]), "L": last, "b": back, "o": out}[c](at[c])
+        at[c] += 1
+    assert at == {"S": len(calls), "L": 8, "b": len(sets), "o": len(sets)}
     act(T.ACC[:, nv - 16 * n2:nv], ps("A", 0, 16 * n2), ["psA"], ["ACCc"])
     x, y, z = (0, v1, "ACCa"), (v1, v2, "ACCz"), (v2, cw - n2, "ACCb")
-    if v2 == cw - n2:
-        for k in range(8):
-            on_vector(k, *x)
-            on_vector(k, *y)
-        for i in range(len(sets)):
-            store_set(i)
-        store(0, nv, ["ACCa", "ACCz", "ACCc"], "SA")
-    else:
-        for k in range(4):
-            on_vector(k, *x)
-            on_vector(k, *y)
-        for k in range(4):
-            on_vector(k + 4, *x)
-            on_vector(k, *z)
-        for k in range(4, 8):
-            on_vector(k, *y)
-            on_vector(k, *z)
+    nxt = {"x": 0, "y": 0, "z": 0}
+    for c in PAR["sums"]:
+        on_vector(nxt[c], *{"x": x, "y": y, "z": z}[c])
+        nxt[c] += 1
+    two = not nxt["z"]
+    if not two:
         store(0, 16 * v1, ["ACCa"], "S")
-        for i in range(len(sets)):
-            store_set(i)
-        store(16 * v1, nv, ["ACCz", "ACCb", "ACCc"], "SA")
+    for i in range(len(sets)):
+        store_set(i)
+    store(16 * v1 * (not two), nv, ["ACCa", "ACCz", "ACCc"] + ["ACCb"] * (not two), "SA")
 
     for s in SEMAPHORES:
         wait("G" if s.startswith("sent") else "S", (s, None, "D"))

@@ -6,40 +6,42 @@ N, S, P, CAP = 4, 4096, 8192, 256
 NG = (N - 1) * CAP
 MAGIC = 25165824.0
 RW = 1056
-PAR = {"sets": (((4,), (4,), (4,), (4,)),), "n2": 12, "flow": "LLLLSSLSSLbLLo", "v1": 16, "v2": 26, "sums": "xy" * 4 + "xz" * 4 + "yz" * 4,
-       "early": (0, 8, 9, 0), "hopb": "sent2", "late": 0, "round": "", "bas": (0, 0, 4096, 4096), "fcv": 0, "zv": 1056, "zg": (768, 1024, 1536), "za": 768, "hu": 4, "pair": 2, "via": "psB psD psB psD psB",
-       "us": (512, 256), "named": "psD", "pool": "ID", "tabq": "SA", "z0": 256,
-       "queues": ("SSASSA", "SSSASSSA", "SS"), "alb": 0, "ring": "psE psF psC psD psA psB", "wide": (2, 4), "seen": "psE psF", "hop2": 0, "hop3": ("AVA",),
-       "order": "k0 b Ba z1 tab k yv l Yv q0 d K0 q1 wv q2 L Wv Q E7 f2 O m H M g F x D3 X D13 o p E9 G1 h1 G2 h2 v5 v9 P rv t1 c G3 v1 z h3 t2 v5 R q w "
-                "B S K t3 W U a U a a n K2 a n a n a n K3 e Ra0 Ra1 n n i j Zv i Z j j J i J i N j j"}
+PAR = {"sets": (((4,), (4,), (4,), (4,)),), "n2": 12, "flow": "1111SS1SS1b11oc", "widths": (16, 10, 10), "sums": "xy" * 4 + "xz" * 4 + "yz" * 4,
+       "stores": (("x", "S"), ("s", "S"), ("yzc", "SA")), "zg": 12,
+       "first": "x0S m0A m1A x1A", "copies": "AAA AAA AAA AAA", "share": "hybrid", "u0": 4, "jobs": "01 23 4 5 6 7", "bas": (0, 512, 1536, 4096),
+       "tz": (1024, 2560), "tabq": "S", "posq": "SSSSSS", "look": "psA psB", "dots": "psA psB", "via": "psD psE psF", "quad": "psC", "ring": "psC psF psD psE psA psB", "seen": "psE psF",
+       "order": "pos p3 b16 bas0 c2 E tz WB PK x0 x1 d0 e0 d1 e1 tab gi y0v b y1v w0v s0 Ba K0 w1v s1 rp O K1 p o "
+                "c0 c3 D9 z0 c1 E7 c4 E7 m0 s2 KG k5 sents1 bas1 bas2 ha hb bp prg P D9 rv g0v z gz0 gz1 zb q M0 m1 n0 gu w K g1a h2 h3 M1 h5 W "
+                "G2 G3 v0 u0 t2 n1 G6 G5 G7 K2 B S t3 v1 v4 t5 u2 u3 h6 u1 u4 h7 a t6 a t7a a u5 u6 t7b a u7a a u7b a R0a "
+                "c j i c i c i c i c c j l R1v N l cp cp cp cp cq cq j j j j l l l l"}
 
+U0 = PAR["u0"]
+CW = 64 - sum(sum(sum(c) for c in u) for u in PAR["sets"])
 SB = {
-    "X": ([128, 1024], BF), "Y": ([128, 8, 16, 8], BF), "W": ([128, 1056], BF), "WD": ([128, 4096], BF),
-    "BAS": ([128, S], BF), "BG": ([128, NG], BF), "BFO": ([128, NG], BF), "OG": ([128, 48], U16), "OF": ([128, 48], U16),
-    "FC": ([128, NG], BF), "RC": ([128, NG], BF), "CG": ([128, S], BF),
-    "POS": ([128, 256], F32), "P3": ([16, 768], F32), "GBI": ([16, 48], I32), "GBF": ([16, 48], F32), "BM": ([128, 256], I32),
-    "DU": ([128, 256], U16), "CR": ([128, 120], I32), "CU": ([128, 120], U16), "QF": ([128, 48], F32), "QU": ([128, 24], U16),
-    "ZL": ([128, 16], U16), "BU": ([128, 256], F32), "B2": ([128, 256], BF), "OU": ([128, 256], U16),
-    "MASK": ([128, 384], BF), "MX": ([128, 384], F32), "MB": ([128, 384], BF), "SK": ([128, 128], BF), "FG": ([128, 142], BF),
-    "T1": ([128, S + NG], F32), "XS": ([128, 4, 38], F32), "XD": ([128, 114], F32), "EIG": ([128, 34], F32),
-    "FS": ([128, 76], F32), "WXZ": ([128, 152], F32), "WT": ([128, 304], F32),
-    "DW": ([128, 304], F32), "SC": ([128, 304], F32), "R1": ([128, 38], F32), "PU": ([128, 4, 16, 8], BF), "PN": ([128, 8, 16, 2], BF),
-    "GZ": ([128, 48], U16), "ZIN": ([128, 256], BF), "Z": ([128, RW + S], BF), "ZG": ([128, NG], BF), "ZF": ([128, NG], BF), "LIT": ([128, S + N * CAP], F32),
-    "HA": ([128, 512], I32), "HB": ([128, 512], I32), "HU": ([128, 512], U16),
+    "X": ([128, 1024], BF), "Y0": ([128, 8, 16, 4], BF), "Y1": ([128, 8, 16, 4], BF), "W": ([128, 4096], BF), "WD": ([128, 4096], BF),
+    "BAS": ([128, S], BF), "BQ": ([128, 128 * U0], BF), "BP": ([128, 2048], BF), "BG": ([128, NG], BF), "BFO": ([128, NG], BF), "CG": ([128, S], BF),
+    "POS": ([128, 256], F32), "P3": ([16, 768], F32), "BM": ([64, 128], I32), "GI": ([128, 3, 2, 8], I32), "GU": ([128, 48], U16), "GZ": ([128, 24], U16),
+    "BH": ([64, 128], BF), "TAB": ([128, 4096], BF), "PICK": ([128, 16], BF), "REP": ([16, 128], BF), "GT0": ([128, 256], BF), "GT1": ([128, 256], BF),
+    "OW": ([128, 256], U16), "BU": ([128, 4, 2, 32], F32), "B2": ([128, 256], BF), "OU": ([128, 256], U16),
+    "T1": ([128, S], F32), "XS": ([128, 128], F32), "XD": ([128, 96], F32), "EIG": ([128, 34], F32),
+    "FS": ([128, 64], F32), "WXZ": ([128, 128], F32), "WT": ([128, 4, 64], F32),
+    "DW": ([128, 256], F32), "SC": ([128, 256], F32), "R1": ([128, 32], F32), "PU": ([128, 4, 16, 8], BF),
+    "Z": ([128, RW], BF), "ZG": ([128, NG // 2], BF), "ZF": ([128, NG // 2], BF), "LQ": ([128, 128 * U0], F32), "LIT": ([128, S + N * CAP], F32),
+    "HA": ([128, 512], I32), "HB": ([128, 8, CW], I32), "HN": ([128, 512 - 8 * CW], I32), "HU": ([128, 512], U16),
     "PRG": ([128, 1024], BF), "ACC": ([128, 1024], F32), "GA": ([128, 5120], F32),
     "PRA": ([128, 768], BF), "SUM": ([128, 768], F32), "OUT": ([128, 768], F32), "E4": ([128, 68], F32),
-    "ONE": ([128, 256], F32), "SL": ([16, 240], F32), "SL2": ([128, 34], F32),
-    "REP": ([16, 128], F32), "REPB": ([16, 136], F32), "I16": ([128, 32], I32), "I16B": ([128, 32], I32),
-    "ID16": ([128, 16], F32), "GS": ([128, 8], F32), "GS3": ([128, 28], F32), "EC": ([128, 24], F32),
+    "ONE": ([128, 256], F32), "SL": ([16, 240], F32), "SL2": ([128, 34], F32), "I16": ([128, 32], I32), "I16B": ([128, 32], I32),
+    "ID16": ([128, 16], F32), "GS": ([128, 8], F32), "EC": ([128, 24], F32),
     "WB": ([128, 128], BF), "IDF": ([128, 128], F32), "IDB": ([128, 128], BF),
-    "SEL2": ([128, 256], BF), "ONEB": ([128, 128], BF), "KEEP": ([128, 256], F32),
+    "SEL2": ([128, 256], BF), "SELQ": ([128, 128], BF), "HS": ([128, 256], BF), "KEEP": ([128, 256], F32),
 }
 SCRATCH = {k: ("sbuf", v[0], v[1]) for k, v in SB.items()}
 SCRATCH["PS"] = ("psum", [128, 6 * 512], F32)
 for _b in ("psT0", "psT1"):
     SCRATCH[_b] = ("psum", [128, 1024], BF)
-SEMAPHORES = ["V", "A", "P", "G", "dpro0", "dpro1", "dgo", "dgb", "dpos", "dalb", "dbas0", "dbas1", "dbas2", "dp3", "dha", "dhb", "dprg", "dzl", "dtab", "dy",
-              "hop1", "hop2", "hop3", "hopb", "sent1", "sent2", "sent3", "sentb"]
+SEMAPHORES = ["V", "A", "P", "G", "dpro0", "dpro1", "dgo", "dgb", "dtab", "dpos", "dalb", "db16", "dbas0", "dbas1", "dbas2", "dbas3", "dbq", "dbp", "dp3", "dha", "dhb", "dprg", "dlq", "dy",
+              "dcp00", "dcp01", "dcp10", "dcp11", "dcp20", "dcp21", "dcp30", "dcp31",
+              "hopw", "hopf0", "hopf1", "hop3", "hopb", "sents0", "sents1", "sents2", "sents3", "sent3", "sentb"]
 
 
 def split_engines(topo, core, dsts):
@@ -55,6 +57,22 @@ def split_engines(topo, core, dsts):
         used.update(mine)
         masks[d] = sum(1 << e for e in mine)
     return masks, n
+
+
+def share_plan(topo, cores, r):
+    me = cores[r]
+    near = [q for q in range(N) if q != r and topo.chip(cores[q]) == topo.chip(me)][0]
+    far = [q for q in range(N) if topo.chip(cores[q]) != topo.chip(me)]
+    mate = [q for q in far if topo.die(cores[q]) == topo.die(me)][0]
+    cross = [q for q in far if q != mate][0]
+    out = topo.engines(me, cores[mate])
+    on = [e for e in topo.engines(me, cores[near]) if e not in out]
+    a, b = out[:len(out) // 2], out[len(out) // 2:]
+    both = [[(mate, r, h, a, "hopw"), (cross, r, h, b, "hopw"), (near, r, h, on, "hopw")] for h in range(2)]
+    first = [[(mate, r, h, out, "hopf%d" % h), (near, r, h, on, "hopw")] for h in range(2)]
+    onward = [[(near, mate, h, on, "hopw")] for h in range(2)]
+    return {"direct": both, "hybrid": [first[0], both[1], onward[0]], "relay": first + onward,
+            "apart": [first[0][:1], both[1], onward[0], first[0][1:]]}[PAR["share"]]
 
 
 def rank_program(g, core, T, topo):
@@ -78,16 +96,19 @@ def rank_program(g, core, T, topo):
             Q[q].wait_ge(T.sem[sem], val)
             seen[(q, sem)] = val
 
+    def at(k):
+        return state.setdefault(k, {"w": [], "base": [], "r": []})
+
     def before(q, reads, writes):
         toks = []
         for k in reads:
-            st = state.setdefault(k, {"w": [], "base": [], "r": []})
+            st = at(k)
             assert st["w"], k
             toks += st["w"]
             if k.startswith("ps"):
                 toks += [t for t in st["r"] if t[2] != q]
         for k in writes:
-            st = state.setdefault(k.lstrip("+"), {"w": [], "base": [], "r": []})
+            st = at(k.lstrip("+"))
             toks += (st["base"] if k[0] == "+" else st["w"]) + st["r"]
             if k.startswith("+ps"):
                 toks += [t for t in st["w"] if t[2] != q]
@@ -116,28 +137,43 @@ def rank_program(g, core, T, topo):
         cnt[sem] += 16
         after((sem, None, "D"), reads, writes)
 
-    def send(hop, src, dst, width, js=range(N - 1), key=None):
-        before("G", [key or src], [])
-        tr = []
-        for j in js:
-            q = others[j]
-            rid, pid, _ = topo.addr(cores[q])
-            tr.append(RemoteDMATransfer(dst_ids=[DstId(rid=rid, pnc=pid)], dma_engine_mask=masks[cores[q]], remote_sem=T.sem["hop" + hop],
-                                        src=T[src][:, width * j:width * j + width],
-                                        dst=T[dst][:, width * there[j]:width * there[j] + width]))
-        g.remote_dma_fused(tr, local_sem=T.sem["sent" + hop])
-        cnt["sent" + hop] += neng * len(tr)
-        cnt["hop" + hop] += neng * len(tr)
-        state.setdefault(dst, {"w": [], "base": [], "r": []})["w"].append(("hop" + hop, None, "D"))
+    def transfer(q, mask, sem, src, dst):
+        rid, pid, _ = topo.addr(cores[q])
+        return RemoteDMATransfer(dst_ids=[DstId(rid=rid, pnc=pid)], dma_engine_mask=mask, remote_sem=T.sem[sem], src=src, dst=dst)
 
-    far = [j for j, q in enumerate(others) if topo.chip(cores[q]) != topo.chip(core)]
-    near = [j for j in range(N - 1) if j not in far]
+    def send(hop, src, dst, width):
+        before("G", [src], [])
+        g.remote_dma_fused([transfer(q, masks[cores[q]], "hop" + hop, T[src][:, width * j:width * j + width],
+                                     T[dst][:, width * there[j]:width * there[j] + width]) for j, q in enumerate(others)], local_sem=T.sem["sent" + hop])
+        cnt["sent" + hop] += neng * len(others)
+        cnt["hop" + hop] += neng * len(others)
+        at(dst)["w"].append(("hop" + hop, None, "D"))
+
+    plan = share_plan(topo, cores, r)
+    for q in others:
+        for call in share_plan(topo, cores, q):
+            for to, owner, h, engines, sem in call:
+                if to == r:
+                    cnt[sem] += len(engines)
+                    at("W%d%d" % (owner, h))["w"].append((sem, None, "D"))
+    every = ["W%d%d" % (q, h) for q in range(N) for h in range(2)]
+
+    def share(n):
+        if n < len(plan):
+            before("G", ["W%d%d" % (owner, h) for _, owner, h, _, _ in plan[n]], [])
+            cols = [T.W[:, 1024 * owner + 512 * h:1024 * owner + 512 * h + 512] for _, owner, h, _, _ in plan[n]]
+            g.remote_dma_fused([transfer(t[0], sum(1 << e for e in t[3]), t[4], c, c) for t, c in zip(plan[n], cols)], local_sem=T.sem["sents%d" % n])
+            cnt["sents%d" % n] += sum(len(t[3]) for t in plan[n])
 
     V, A, PE = g.vector, g.scalar, g.tensor
 
-    def ps(bank, lo, hi, rows=128, row0=0):
-        at = 512 * "ABCDEF".index(bank[-1])
-        return T.PS[row0:rows, at + lo:at + hi]
+    def ps(bank, lo, hi, rows=128, row0=0, step=1):
+        c = 512 * "ABCDEF".index(bank[-1])
+        return T.PS[row0:rows, c + lo:c + hi:step]
+
+    def banks(bank, n):
+        b = "ABCDEF".index(bank[-1])
+        return ["ps" + x for x in "ABCDEF"[b:b - (-n // 512)]]
 
     def copy(out, in_, rd, w):
         op("V", lambda: V.tensor_copy(out, in_), rd, w)
@@ -160,6 +196,8 @@ def rank_program(g, core, T, topo):
     def act(out, in_, rd, w, func=None, **kw):
         plain = FN.Identity if kw else FN.Copy
         op("A", lambda: A.activation(out, in_, plain if func is None else func, **kw), rd, w)
+
+    by = {"v": copy, "a": act, "V": copy, "A": act}
 
     def mm(out, lhsT, rhs, rd, w, start=True, stop=True):
         op("P", lambda: PE.matmul(out, lhsT, rhs, start, stop), rd, w)
@@ -187,418 +225,23 @@ def rank_program(g, core, T, topo):
     def zero(out, n, w, lo=0, hi=128):
         act(out, T.ONE[lo:hi, 0:n], ["ONE"], w, scale=0.0)
 
-    qs = PAR["queues"]
-    if r > 0:
-        dma("A", "dgo", T.GBI[:, 0:16 * r], T.go[:, 0:16 * r], [], ["+GOI"])
-    if r < N - 1:
-        dma("A", "dgo", T.GBI[:, 16 * r:48], T.go[:, 16 * r + 16:64], [], ["+GOI"])
-    for k in range(6):
-        dma(qs[0][k], "dpos", T.POS[16 * k:16 * k + 16, :], T.pos[16 * (k // 2):16 * (k // 2) + 16, :], [], ["+POS"])
-    for h in range(2):
-        dma("S", "dpro%d" % h, T.X[64 * h:64 * h + 64, :], T.pro[8 * h:8 * h + 8, :], [], ["X%d" % h])
-    for p in range(8):
-        dma(qs[1][p], "dgb", T.BM[16 * p:16 * p + 16, :], T.bmap[:], [], ["+BM"])
-
-    def albedo():
-        for e in range(2):
-            dma(qs[2][e], "dalb", T.POS[96 + 16 * e:112 + 16 * e, :], T.alb[:], [], ["+ALB"])
-
-    def places():
-        for a in range(3):
-            dma("S", "dp3", T.P3[:, 256 * a:256 * a + 256], T.pos[16 * a:16 * a + 16, :], [], ["+P3"])
-
-    if PAR["alb"] == 0:
-        albedo()
-
-    cuts = PAR["bas"]
-
-    def basis(n):
-        lo, hi = cuts[n], cuts[n + 1]
-        for p in range(8 * (lo < hi)):
-            dma("S", "dbas%d" % n, T.BAS[16 * p:16 * p + 16, lo:hi], T.bas[:, lo:hi], [], ["+BAS%d" % n])
-
-    def bas(lo, hi):
-        return ["BAS%d" % n for n in range(3) if max(lo, cuts[n]) < min(hi, cuts[n + 1])]
-
-    basis(0)
-
-    zv = PAR["zv"]
-    mset(T.ONE[:], 1.0, ["ONE"])
-    mset(T.REPB[:, 0:8], 0.0, ["+REPB"])
-    iota(T.I16[:, 0:16], [[-1, 16]], 16, 1, ["I16"])
-    iota(T.I16[:, 16:24], [[-16, 8]], 0, 1, ["I8"])
-    sel(T.REPB[:, 8:136], T.ONE[0:16, 0:128], [[0, 4], [-1, 2], [-2, 16]], OP.is_equal, 0, 1, ["ONE"], ["+REPB"])
-    sel(T.REP[:], T.ONE[0:16, 0:128], [[0, 8], [-1, 16]], OP.is_equal, 0, 1, ["ONE"], ["REP"])
-    sel(T.IDB[:], T.ONE[:, 0:128], [[-1, 128]], OP.is_equal, 0, 1, ["ONE"], ["IDB"])
-    sel(T.SK[0:96, :], T.ONE[0:96, 0:128], [[0, 8], [-16, 16]], OP.is_equal, 0, 1, ["ONE"], ["SK"])
-    for a, bit in enumerate(([[0, 4], [16, 2]], None, [[16, 2], [0, 4]])):
-        rows, p0 = slice(32 * a, 32 * a + 32), 32 * a
-        if a == 1:
-            for h in range(2):
-                sel(T.WB[rows, 64 * h:64 * h + 64], T.ONE[rows, 0:64], [[16, 2], [0, 2], [1, 16]], OP.is_equal, 0, -1, ["ONE"], ["+WB"], p0)
-        else:
-            sel(T.WB[rows, :], T.ONE[rows, 0:128], bit + [[1, 16]], OP.is_equal, 0, -1, ["ONE"], ["+WB"], p0)
-    for a, factor in enumerate((16.0, 256.0, 1.0)):
-        mset(T.EC[32 * a:32 * a + 32, 1:2], 0.5 * factor, ["+EF"])
-    ts(T.I16B[:, 16:24], T.I16[:, 16:24], 4, OP.arith_shift_right, ["I8"], ["I8B"])
-    ts(T.I16B[:, 0:16], T.I16[:, 0:16], 15, OP.bitwise_and, ["I16"], ["I16B"])
-    ts(T.GS[:], T.I16B[:, 16:24], 0.0, OP.is_equal, ["I8B"], ["GS"])
-    ts(T.ID16[:], T.I16B[:, 0:16], 0.0, OP.is_equal, ["I16B"], ["ID16"])
-    ts(T.I16B[:, 17:18], T.I16[:, 16:17], 5, OP.arith_shift_right, ["I8", "GS"], ["I4B"])
-    if PAR["z0"]:
-        mset(T.Z[:, 0:PAR["z0"]], 0.0, ["+Z0"])
-    ts(T.EC[:, 5:7], T.I16B[:, 16:18], -1024.0, OP.mult, ["I8B", "I4B"], ["EQ"], 16.0, OP.add)
-    act(T.EC[:, 16:20], T.GS[:, 1:8:2], ["GS"], ["E1"], accum_out=T.EC[:, 0:1])
-    act(T.EC[0:96, 2:3], T.EC[0:96, 1:2], ["EF"], ["EM"], scale=-MAGIC)
-    zero(T.FG[:], 142, ["FG"])
-    zero(T.W[:, 0:16], 16, ["+W"])
-    zero(T.W[:, 1040:1056], 16, ["+W"])
-    act(T.EC[:, 7:8], T.EC[:, 0:1], ["E1"], ["E0"], scale=-1.0, bias=1.0)
-    zero(T.GS3[:], 28, ["GS3"])
-
-    def soon(c):
-        if c == "z1":
-            mset(T.Z[:, PAR["z0"]:zv], 0.0, ["+Z0"])
-        if c == "K0":
-            act(T.EIG[96:112, :], T.ONE[96:112, 0:34], ["ONE"], ["EIG"], scale=0.125)
-            for h in range(2):
-                act(T.GS3[:, 4 + h:22:6], T.GS[:, h:6:2], ["GS"], ["+GS3"])
-            act(T.GS3[:, 22:24], T.GS[:, 6:8], ["GS"], ["+GS3"], scale=0.125)
-            sel(T.SL[:], T.ONE[0:16, 0:240], [[-1, 240]], OP.is_equal, 112, 1, ["ONE"], ["SL"])
-            sel(T.SL2[96:112, :], T.EIG[96:112, :], [[-1, 34]], OP.is_equal, 1, 2, ["EIG"], ["SL2"], 96)
-        if c == "k0":
-            for e in range(2):
-                mm(ps("D", 48, 72), T.REPB[:, 8 - 8 * e:136 - 8 * e], T.GBF[:, e:48:2], ["REPB", "GBG"], ["+psD"], e == 0, e == 1)
-            mm(ps("D", 0, 48), T.REP[:], T.GBF[:], ["REP", "GBG"], ["+psD"])
-
-    copy(T.GBF[:], T.GBI[:], ["GOI"], ["GBG"])
-
-    go_u = T.CU[:, 0:48]
     sets = PAR["sets"]
     na = 128 * sum(sum(sum(c) for c in u) for u in sets)
     cw = (P - na) // 128
     nv = 16 * cw
-    pair = PAR["pair"]
-    jobs = [(v, v + 2) for v in range(pair)]
-    jobs += [(t,) for t in range(8) if not any(t in j for j in jobs)]
+    w0 = 128 * U0
 
-    turns = [(T.HA[:, cw * k:cw * k + cw], T.hit[16 * k:16 * k + 16, 0:8 * cw], "dha", [], "+HA") for k in range(8)]
-    turns += [(T.HB[:, 8 * cw:512], T.hit[:, 8 * cw:512], "dhb", [], "+HB")]
-    turns += [(T.HB[16 * k:16 * k + 16, 0:8 * cw], T.HA[k:128:8, 0:8 * cw], "dhb", ["HA"], "+HB") for k in range(8)]
+    def run(n):
+        return (1024 * n, 1024 * n + w0) if n < 4 else (1024 * (n - 4) + w0, 1024 * (n - 3))
 
-    def lists(n):
-        for _ in range(PAR["early"][n]):
-            out, in_, sem, rd, w = turns.pop(0)
-            dma("S", sem, out, in_, rd, [w])
+    jobs, paired, col = [tuple(int(x) for x in j) for j in PAR["jobs"].split()], {}, 0
+    for j in jobs:
+        if len(j) == 2:
+            paired[j], col = col, col + run(j[0])[1] - run(j[0])[0]
+    cuts = PAR["bas"]
 
-    lists(0)
-
-    def zeros(n):
-        at = zv + sum(PAR["zg"][:n])
-        if PAR["zg"][n]:
-            fill(T.Z[:, at:at + PAR["zg"][n]], PAR["zg"][n], 0, ["+ZS"])
-
-    def ready(c):
-        if c == "k":
-            copy(T.CR[:, 0:72], ps("D", 0, 72), ["psD"], ["GI"])
-        if c == "l":
-            ts(T.CR[:, 96:120], T.CR[:, 48:72], 15, OP.bitwise_and, ["GI"], ["CR2"])
-            ts(T.CR[:, 72:96], T.CR[:, 48:72], 4, OP.arith_shift_right, ["GI"], ["CR1"])
-        if c == "L":
-            ts(T.CR[96:128, 72:96], T.CR[96:128, 48:72], 255, OP.bitwise_and, ["GI"], ["CR1"])
-            ts(T.CR[96:128, 96:120], T.CR[96:128, 48:72], 8, OP.arith_shift_right, ["GI"], ["CR2"])
-        if c == "Q":
-            copy(T.CU[:], T.CR[:], ["CR1", "CR2", "GI"], ["CU"])
-        if c == "H":
-            act(T.MASK[:], T.ID16[:, 0:16].indirect(T.CU[:, 96:120]), ["ID16", "CU"], ["MASK"])
-        if c == "q0":
-            ts(T.QF[:, 0:24], T.CR[:, 96:120], 256.0, OP.mult, ["CR2", "EQ"], ["QF0"], T.EC[:, 6:7], OP.add)
-        if c == "q1":
-            tt(T.QF[:, 24:48], T.QF[:, 0:24], T.CR[:, 72:96], OP.add, ["QF0", "CR1"], ["QF1"])
-        if c == "q2":
-            ts(T.QU[:], T.QF[:, 24:48], 1040.0, OP.min, ["QF1"], ["QU"])
-        if c == "tab":
-            for k in range(12):
-                dma(PAR["tabq"][k % len(PAR["tabq"])], "dtab", T.Z[16 * (k // 6) + k % 6:128:32, 16:1040], T.B2[16 * (k % 6):16 * (k % 6) + 16, :], ["B2", "Z0"], ["+TAB"])
-            if PAR["alb"] == 1:
-                albedo()
-            basis(1)
-            places()
-        if c == "b":
-            ts(T.BU[0:96, :], T.POS[0:96, :], T.EC[0:96, 0:1], OP.subtract, ["POS", "E1"], ["BU"], MAGIC, OP.add)
-        if c == "Bv":
-            ts(T.B2[0:96, :], T.BU[0:96, :], MAGIC, OP.subtract, ["BU", "EF"], ["+B2"], T.EC[0:96, 1:2], OP.mult)
-        if c == "Ba":
-            act(T.B2[0:96, :], T.BU[0:96, :], ["BU", "EF", "EM"], ["+B2"], scale=T.EC[0:96, 1:2], bias=T.EC[0:96, 2:3])
-        if c in ("yv", "ya", "Yv", "Ya"):
-            h = "yY".index(c[0])
-            rows = slice(64 * h, 64 * h + 64)
-            for p in range(8):
-                turn(T["psT%d" % h][:, 64 * p:64 * p + 64], T.X[rows, p:1024:8], ["X%d" % h], ["+psT%d" % h], rows)
-            (copy if c[1] == "v" else act)(T.Y[:, :, 8 * h:8 * h + 8, :], T["psT%d" % h][:, 0:512], ["psT%d" % h], ["+Y"])
-        if c in ("Yv", "Ya"):
-            for b in range(8):
-                turn(T["psT%d" % (b // 4)][:, 128 * (b % 4):128 * (b % 4) + 128], T.Y[:, :, :, b], ["Y"], ["+psT%d" % (b // 4)])
-        if c in ("wa", "wv"):
-            (act if c == "wa" else copy)(T.W[:, 16:528], T.psT0[:, 0:512], ["psT0"], ["+W"])
-        if c in ("Wa", "Wv"):
-            (act if c == "Wa" else copy)(T.W[:, 528:1040], T.psT1[:, 0:512], ["psT1"], ["+W"])
-        if c == "m":
-            act(T.MB[:], T.Z[:, 0:RW].indirect(T.QU[:]), ["Z0", "TAB", "QU"], ["MB"])
-        if c == "f2":
-            mm(ps("F", 256, 264), T.SK[0:96, :], T.WB[0:96, 0:128:16], ["SK", "WB"], ["+psF"])
-            for h in range(2):
-                act(T.FG[:, 14 + h:142:16], ps("F", 256, 264), ["psF", "E0", "E1"], ["+FG"], scale=T.EC[:, 7 - 7 * h:8 - 7 * h])
-        if c == "M":
-            for i in range(8):
-                mm(ps("E", 256, 304), T.FG[:, 14 - 2 * i:142 - 2 * i], T.MB[:, i:384:8], ["FG", "MB"], ["+psE"], i == 0, i == 7)
-        if c == "g":
-            copy(T.OG[:], ps("E", 256, 304), ["psE"], ["OG"])
-        if c == "O":
-            mm(ps("F", 0, 256), T.WB[0:96, :], T.B2[0:96, :], ["WB", "B2"], ["+psF"])
-        if c == "o":
-            copy(T.OU[:], ps("F", 0, 256), ["psF"], ["OU"])
-        if c == "d":
-            ts(T.DU[:], T.BM[:], float(16 - 1024 * r), OP.add, ["BM"], ["DU"], 1040.0, OP.min)
-        if c == "p":
-            for c8 in range(8):
-                mm(ps("C", 0, 96), T.SL[:, 112 - 16 * c8:240 - 16 * c8], T.P3[:, c8:768:8], ["SL", "P3"], ["+psC"], c8 == 0, c8 == 7)
-            wait("P", ("P", None, "X"))
-            for h in range(2):
-                mm(ps("C", 96, 128), T.POS[96:112, 128 * h:128 * h + 128], T.SL2[96:112, 1 - h:33 - h], ["SL2", "ALB"], ["+psC"], h == 0, h == 1)
-        if c == "x":
-            tt(T.MX[:], T.POS[:, 0:256].indirect(T.CU[:, 72:96]), T.MASK[:], OP.mult, ["POS", "ALB", "CU", "MASK"], ["MX"])
-        if c == "X":
-            for b in range(3):
-                mm(ps("C", 128, 152), T.MX[:, 128 * b:128 * b + 128], T.GS3[:, 4 - 2 * b:28 - 2 * b], ["MX", "GS3"], ["+psC"], b == 0, b == 2)
-        if c == "F":
-            send("1", "OG", "OF", 16)
-            fill(T.PU[:], 512, 0, ["+PU"])
-            fill(T.PN[:], 256, 0, ["+PU"])
-            zeros(0)
-            wait("S", ("sent1", None, "D"))
-            basis(2)
-            for j, lo, hi in ((0, 0, 80), (1, 80, 96), (2, 96, 128)):
-                dma("S", "dzl", T.ZL[lo:hi, :], T.CU[lo:hi, 16 * j:16 * j + 16], ["CU"], ["+ZL"])
-            lists(1)
-
-    held, hold, nb = [], [False], PAR["named"]
-
-    def sums(col, n):
-        for c in range(col, col + n, 128):
-            if c < S:
-                mm(ps("A", c // 16, c // 16 + 8), T.T1[:, c:c + 128], T.GS[:], ["T1%d" % col, "GS"], ["+psA"])
-            else:
-                at, c0 = (c - S) // 16, c - c % 256
-                mm(ps(nb, at, at + 8), T.T1[:, c0 + c % 256 // 128:c0 + 256:2], T.GS[:], ["T1%d" % col, "GS"], ["+" + nb])
-
-    done, tiles, dense, named, via = [0], {}, [0], [0], PAR["via"].split()
-
-    def step(c):
-        if c[0] in "DE":
-            lo, hi = 8 * dense[0], 8 * (dense[0] + int(c[1:]))
-            (act if c[0] == "D" else copy)(T.WD[:, 16 * lo:16 * hi], T.W[:, 0:1056].indirect(T.DU[:, lo:hi]), ["W", "DU"], ["+WD"])
-            dense[0] = hi // 8
-        if c[0] == "v":
-            lo, hi = 128 * done[0], 128 * (done[0] + int(c[1:]))
-            tt(T.T1[:, lo:hi], T.WD[:, 0:4096].indirect(T.OU[:, lo // 16:hi // 16]), T.BAS[:, lo:hi], OP.mult, ["WD", "OU"] + bas(lo, hi), ["T1%d" % lo])
-            held.append((lo, hi - lo))
-            done[0] = hi // 128
-        if c[0] in "Ght" and c[1:].isdigit():
-            n = int(c[1:])
-            if c[0] == "G":
-                tiles[n] = 128 * done[0]
-                done[0] += 4
-            lo, bank = tiles[n], via[n - 1]
-            if c[0] == "G":
-                act(T.CG[:, lo:lo + 512], T.WD[:, 0:4096].indirect(T.OU[:, lo // 16:lo // 16 + 32]), ["WD", "OU"], ["CG%d" % n])
-            elif c[0] == "h":
-                mm(ps(bank, 0, 512), T.IDB[:], T.CG[:, lo:lo + 512], ["IDB", "CG%d" % n], ["+" + bank])
-            else:
-                tt(T.T1[:, lo:lo + 512], ps(bank, 0, 512), T.BAS[:, lo:lo + 512], OP.mult, [bank] + bas(lo, lo + 512), ["T1%d" % lo])
-                held.append((lo, 512))
-        if c in ("(", ")", "a"):
-            hold[0] = c == "("
-        while held and not hold[0]:
-            sums(*held.pop(0))
-        if c == "P":
-            act(T.XS[:, :, 6:38], ps("C", 0, 128), ["psC"], ["+XS"])
-            act(T.XS[:, :, 0:6], ps("C", 128, 152), ["psC"], ["+XS"])
-        if c == "rv":
-            ts(ps("C", 152, 266), T.XS[:, 0:3, :], MAGIC, OP.add, ["XS"], ["+psC"], MAGIC, OP.subtract)
-        if c == "ra":
-            act(T.XD[:], T.XS[:, 0:3, :], ["XS"], ["XD"], bias=MAGIC)
-            act(ps("C", 152, 266), T.XD[:], ["XD"], ["+psC"], bias=-MAGIC)
-        if c == "z":
-            tt(T.XD[:], T.XS[:, 0:3, :], ps("C", 152, 266), OP.subtract, ["XS", "psC"], ["XD"])
-            act(ps("C", 348, 424), T.XD[:, 0:76], ["XD"], ["+psC"], FN.Abs)
-            act(T.FS[:, 38:76], T.XD[:, 76:114], ["XD"], ["F1"], FN.Abs)
-        if c == "q":
-            act(ps("C", 272, 348), ps("C", 348, 424), ["psC"], ["+psC"], bias=1.0, scale=-1.0)
-            act(T.FS[:, 0:38], T.FS[:, 38:76], ["F1"], ["F0"], bias=1.0, scale=-1.0)
-        if c == "w":
-            for x in range(4):
-                tt(T.WXZ[:, 38 * x:38 * x + 38], ps("C", 272 + 76 * (x & 1), 310 + 76 * (x & 1)), T.FS[:, 38 * (x >> 1):38 * (x >> 1) + 38],
-                   OP.mult, ["psC", "F0", "F1"], ["+WXZ"])
-            for e in range(2):
-                tt(ps("C", 424 + 38 * e, 462 + 38 * e), ps("C", 310 + 76 * e, 348 + 76 * e), T.XS[:, 3, :], OP.mult, ["psC", "XS"], ["+FY"])
-        if c == "W":
-            for p in range(8):
-                x, y = (p & 1) + 2 * (p >> 2), p >> 1 & 1
-                tt(T.WT[:, p:304:8], T.WXZ[:, 38 * x:38 * x + 38], ps("C", 424 + 38 * y, 462 + 38 * y), OP.mult, ["WXZ", "FY", "psC"], ["+WT"])
-        if c == "c":
-            if PAR["hop2"]:
-                for js in (far, near):
-                    lo, hi = min(js), max(js) + 1
-                    act(T.FC[:, CAP * lo:CAP * hi], T.WD[:, 0:4096].indirect(T.OF[:, 16 * lo:16 * hi]), ["WD", "OF"], ["FC%d" % lo])
-                    send("2", "FC", "RC", CAP, js, "FC%d" % lo)
-            else:
-                n = PAR["fcv"]
-                act(T.FC[:, 16 * n:NG], T.WD[:, 0:4096].indirect(T.OF[:, n:48]), ["WD", "OF"], ["+FC"])
-                if n:
-                    copy(T.FC[:, 0:16 * n], T.WD[:, 0:4096].indirect(T.OF[:, 0:n]), ["WD", "OF"], ["+FC"])
-                send("2", "FC", "RC", CAP)
-            sel(T.KEEP[:], T.ONE[:], [[0, 32], [1, 8]], OP.not_equal, 0, 0, ["ONE"], ["KEEP"])
-            zeros(1)
-            wait("S", ("sent2", None, "D"))
-            lists(2)
-        if c == "K3" and pair:
-            act(T.BAS[64:128, 0:512 * pair], T.BAS[64:128, 1024:1024 + 512 * pair], [], ["+" + k for k in bas(0, S)] + ["BASP"])
-        if c == "B":
-            act(T.BG[:], T.BAS[:, 0:S].indirect(go_u), bas(0, S) + ["CU"], ["BG"])
-        if c == "S":
-            wait("G", (PAR["hopb"], None, "D"))
-            send("b", "BG", "BFO", CAP)
-            wait("S", ("sentb", None, "D"))
-            lists(3)
-            zeros(2)
-            fill(T.LIT[:, S + CAP * r:S + CAP * r + CAP], CAP, 0, ["+LIT"])
-            sel(T.IDF[:], T.ONE[:, 0:128], [[-1, 128]], OP.is_equal, 0, 1, ["ONE"], ["IDF"])
-        if c == "R":
-            for bank, lo, hi in (("psE", 0, 512), ("psF", 512, NG)):
-                mm(ps(bank, 0, hi - lo), T.IDB[:], T.RC[:, lo:hi], ["IDB", "RC"], ["+" + bank])
-        if c == "U":
-            lo = named[0]
-            n = PAR["us"][lo > 0]
-            banks = ["psE", "psF"][lo // 512:(lo + n - 1) // 512 + 1]
-            tt(T.T1[:, S + lo:S + lo + n], ps("E", lo, lo + n), T.BG[:, lo:lo + n], OP.mult, banks + ["BG"], ["T1%d" % (S + lo)])
-            sums(S + lo, n)
-            named[0] += n
-        if c == "e":
-            ts(T.GZ[:], T.CR[:, 0:48], T.EC[:, 4:5], OP.add, ["GI", "EZ"], ["GZ"], T.EC[:, 3:4], OP.min)
-
-    def pieces(lo, hi, dots, bank, buf, n):
-        v, rest = T.SC[:, lo + 7:hi:8], T.R1[:, lo // 8:hi // 8]
-        top, mid, low = (buf[x] for x in range(3))
-        cut = act if n in PAR["round"] else copy
-        return [lambda: tt(T.DW[:, lo:hi], dots, T.WT[:, lo:hi], OP.mult, [bank, "WT"], ["DW" + n]),
-                lambda: scan(T.SC[:, lo:hi], T.KEEP[:, 0:hi - lo], T.DW[:, lo:hi], ["KEEP", "DW" + n], ["SC" + n]),
-                lambda: cut(top, v, ["SC" + n, "PU"], ["Pa" + n]),
-                lambda: tt(rest, v, top, OP.subtract, ["SC" + n, "Pa" + n], ["R1" + n]),
-                lambda: cut(mid, rest, ["R1" + n], ["Pb" + n]),
-                lambda: tt(low, rest, mid, OP.subtract, ["R1" + n, "Pb" + n], ["Pc" + n])]
-
-    chain = {"a": pieces(48, 304, ps("A", 0, 256), "psA", [T.PU[:, :, x, :] for x in range(3)], "a"),
-             "n": pieces(0, 48, ps(nb, 0, 48), nb, [T.PN[:, 4:7, x, :] for x in range(3)], "n")}
-
-    ring, ahead, nh, hu = PAR["ring"].split(), [0, 0, 0], PAR["hu"], [0]
-
-    def parts(v):
-        return [(jobs[v][0], 0, 64), (jobs[v][1], 64, 128)] if v < pair else [(jobs[v][0], 0, 128)]
-
-    def spread_r(v):
-        a, h = jobs[v][0] // 2, jobs[v][0] % 2
-        p0, c = 32 * (a // 2), 64 if len(jobs[v]) == 2 else 128 * (a % 2)
-        mm(ps(ring[v], 0, 512), T.SEL2[p0:p0 + 32, c:c + 128], T.Z[p0:p0 + 32, 16 + 512 * h:528 + 512 * h],
-           ["SELa", "SELb", "RH%d" % h], ["+" + ring[v]], True, False)
-        ahead[0] = v + 1
-
-    def spread_z(v):
-        if v >= ahead[0]:
-            spread_r(v)
-        for t, lo, hi in parts(v):
-            c = RW + 512 * t
-            mm(ps(ring[v], 0, 512, hi, lo), T.ONEB[64:128, lo:hi], T.Z[64:128, c:c + 512], ["ONEB", "ZS"], ["+" + ring[v]], False, True)
-        ahead[1] = v + 1
-
-    def spread(v):
-        if ahead[1] == v < len(jobs) and ring[v] not in ring[ahead[2]:v]:
-            spread_z(v)
-
-    halves = []
-
-    def lit():
-        v = ahead[2]
-        c = 512 * jobs[v][0]
-        spread(v)
-        if v < pair:
-            d, key = 512 * jobs[v][1], "LP%d" % v
-            tt(T.LIT[:, c:c + 512], ps(ring[v], 0, 512), T.BAS[:, c:c + 512], OP.mult, [ring[v], "BASP"], ["+LIT", key])
-            act(T.LIT[0:64, d:d + 512], T.LIT[64:128, c:c + 512], [key], ["+LIT"])
-            act(T.LIT[64:128, d:d + 512], T.LIT[64:128, c:c + 512], [key], ["+LIT"])
-            halves.append(lambda: act(T.LIT[64:128, c:c + 512], T.LIT[0:64, c:c + 512], [], ["+LIT", key]))
-        else:
-            n = 1 + (v in PAR["wide"])
-            spread(v + n - 1)
-            tt(T.LIT[:, c:c + 512 * n], ps(ring[v], 0, 512 * n), T.BAS[:, c:c + 512 * n], OP.mult, ring[v:v + n] + bas(0, S), ["+LIT"])
-            v += n - 1
-        ahead[2] = v + 1
-
-    def close(c):
-        if c in chain:
-            chain[c].pop(0)()
-        if c == "a" and not chain[c]:
-            for u in range(8):
-                turn(T["psT%d" % (u // 4)][0:64, 128 * (u % 4):128 * (u % 4) + 128], T.PU[:, :, :, u], ["Paa", "Pba", "Pca"], ["+psT%d" % (u // 4)])
-        if c == "n" and not chain[c]:
-            for t2 in range(2):
-                mm(T.PS[:, 512 + t2:768:2], T.PN[:, :, :, t2], T.IDB[:], ["Pan", "Pbn", "Pcn", "IDB"], ["+psB"])
-        if c[:2] in ("Rv", "Ra"):
-            h = int(c[2])
-            (copy if c[1] == "v" else act)(T.Z[0:64, 16 + 512 * h:528 + 512 * h], T["psT%d" % h][0:64, 0:512], ["psT%d" % h, "MB"], ["RH%d" % h])
-        if c == "cp":
-            halves.pop(0)()
-        if c == "i":
-            lo, hi = 512 * hu[0] // nh, 512 * (hu[0] + 1) // nh
-            copy(T.HU[:, lo:hi], T.HB[:, lo:hi], ["HB"], ["+HU"])
-            hu[0] += 1
-        if c in ("Zv", "Za"):
-            (copy if c == "Zv" else act)(T.ZIN[:], ps("B", 0, 256), ["psB"], ["ZIN"])
-        if c == "j":
-            spread_r(ahead[0])
-        if c == "J":
-            spread_z(ahead[1])
-        if c == "Z":
-            copy(T.Z[:, RW:RW + S].indirect(T.ZL[:, 0:16]), T.ZIN[:], ["ZL", "ZIN", "Z0"], ["ZS"])
-        if c == "N":
-            for js, by in zip((far, near) if len(PAR["hop3"]) == 2 else (far + near,), PAR["hop3"]):
-                for j, e in zip(js, by):
-                    (act if e == "A" else copy)(T.ZG[:, CAP * j:CAP * j + CAP], T.Z[:, 0:RW + S].indirect(T.GZ[:, 16 * j:16 * j + 16]),
-                                                ["Z0", "ZS", "RH0", "RH1", "GZ"], ["+ZG%d" % len(js)])
-                send("3", "ZG", "ZF", CAP, js, "ZG%d" % len(js))
-        if c == "li":
-            lit()
-        if c == "K":
-            act(T.EC[0:64, 3:4], T.ONE[0:64, 0:1], ["ONE"], ["+EZ"], scale=1040.0)
-            act(T.EC[64:128, 3:4], T.ONE[64:128, 0:1], ["ONE"], ["+EZ"], scale=65535.0)
-            act(T.EC[64:128, 4:5], T.ONE[64:128, 0:1], ["ONE"], ["+EZ"], scale=float(RW))
-            act(T.EC[0:64, 4:5], T.EC[0:64, 5:6], ["EQ"], ["+EZ"])
-            if PAR["za"]:
-                act(T.Z[:, RW + S - PAR["za"]:RW + S], T.BAS[:, 0:PAR["za"]], bas(0, S), ["+ZS"], scale=0.0)
-        if c == "K2":
-            act(T.SEL2[:, 128:256], T.ONE[:, 0:128], ["ONE", "E1"], ["SELb"], scale=T.EC[:, 0:1])
-            act(T.ONEB[:], T.ONE[:, 0:128], ["ONE"], ["ONEB"])
-            act(T.SEL2[:, 0:128], T.SEL2[:, 128:256], ["SELb"], ["SELa"], scale=-1.0, bias=1.0)
-            zero(T.E4[:], 68, ["E4"])
-            act(T.E4[:, 3:67:4], T.ID16[:], ["ID16"], ["+E4"])
-
-    for c in PAR["order"].split():
-        soon(c)
-        ready(c)
-        step(c)
-        close(c)
-    assert done[0] == 32 == dense[0] and not chain["a"] and not chain["n"] and not held
-    assert zv + sum(PAR["zg"]) + PAR["za"] == RW + S
+    def bas(lo, hi):
+        return ["B16"] + ["BAS%d" % n for n in range(len(cuts) - 1) if max(lo, cuts[n]) < min(hi, cuts[n + 1])]
 
     calls, first, p0, col = [], [], P - na, 0
     for i, u in enumerate(sets):
@@ -610,47 +253,401 @@ def rank_program(g, core, T, topo):
                 col, p0 = col + 16 * nb, p0 + 128 * nb
         col = -(-col // 128) * 128
     units = [u for c in calls for u in c]
-    if PAR["late"]:
-        wait("S", ("sent3", None, "D"))
-    for k in range(8):
-        dma("S", "dprg", T.PRG[16 * k:16 * k + 16, 0:nv], T.pro[:, nv * k:nv * k + nv], [], ["+PRG"])
-    for i, c, nb, p0 in units:
-        dma("S", "dprg", T.PRA[c % 128:c % 128 + 16 * nb, c - c % 128:c - c % 128 + 128], T.pro[:, p0:p0 + 128 * nb], [], ["+PRA"])
 
-    for v in range(ahead[2], ahead[2] + 6):
-        spread(v)
-    while ahead[2] < len(jobs):
-        lit()
-        while halves and ahead[2] >= pair:
+    for c in PAR["first"].split():
+        h = int(c[1])
+        if c[0] == "m":
+            dma(c[2], "dgb", T.BM[32 * h:32 * h + 32, :], T.bmap[:], [], ["+BM"])
+        else:
+            dma(c[2], "dpro%d" % h, T.X[64 * h:64 * h + 64, :], T.pro[:, 4096 * h:4096 * h + 4096], [], ["X%d" % h])
+
+    tz = PAR["tz"]
+    mset(T.ONE[:], 1.0, ["ONE"])
+    mset(T.TAB[:, 0:tz[0]], 0.0, ["TZ"])
+    mset(T.TAB[:, tz[0]:tz[1]], 0.0, ["+TZa"])
+    iota(T.I16[:, 0:16], [[-1, 16]], 16, 1, ["I16"])
+    iota(T.I16[:, 16:24], [[-16, 8]], 0, 1, ["I8"])
+    sel(T.IDB[:], T.ONE[:, 0:128], [[-1, 128]], OP.is_equal, 0, 1, ["ONE"], ["IDB"])
+
+    def loads(c):
+        if c == "c0":
+            ts(T.I16B[:, 16:24], T.I16[:, 16:24], 4, OP.arith_shift_right, ["I8"], ["I8B"])
+            ts(T.I16B[:, 0:16], T.I16[:, 0:16], 15, OP.bitwise_and, ["I16"], ["I16B"])
+        if c == "c1":
+            ts(T.GS[:], T.I16B[:, 16:24], 0.0, OP.is_equal, ["I8B"], ["GS"])
+            ts(T.ID16[:], T.I16B[:, 0:16], 0.0, OP.is_equal, ["I16B"], ["ID16"])
+        if c == "c2":
+            for a, factor in enumerate((1.0, 16.0, 256.0)):
+                act(T.EC[32 * a:32 * a + 32, 1:2], T.ONE[32 * a:32 * a + 32, 0:1], ["ONE"], ["+EF"], scale=0.5 * factor)
+        if c == "c3":
+            ts(T.I16B[:, 24:25], T.I16[:, 16:17], 4, OP.arith_shift_right, ["I8"], ["I4B"], 3, OP.bitwise_and)
+        if c == "c4":
+            ts(T.EC[:, 5:6], T.I16B[:, 24:25], -1024.0, OP.mult, ["I4B"], ["EQ"], 16.0, OP.add)
+        if c == "b16":
+            dma("S", "db16", T.BAS[0:16, :], T.bas[:], [], ["B16"])
+        if c == "pos":
+            for k in range(6):
+                dma(PAR["posq"][k], "dpos", T.POS[16 * k:16 * k + 16, :], T.pos[16 * (k // 2):16 * (k // 2) + 16, :], [], ["+POS"])
+        if c == "p3":
+            for a in range(3):
+                dma("S", "dp3", T.P3[:, 256 * a:256 * a + 256], T.pos[16 * a:16 * a + 16, :], [], ["+P3"])
+            dma("S", "dalb", T.POS[96:112, :], T.alb[:], [], ["+ALB"])
+        if c == "gi":
+            for p in range(8):
+                for lo, hi, j in ((0, r, 0), (r + 1, N, r)):
+                    if lo < hi:
+                        dma("S", "dgo", T.GI[16 * p:16 * p + 16, j:j + hi - lo], T.go[:, 16 * lo:16 * hi], [], ["+GI"])
+        if c == "tz":
+            for lo in range(tz[1], 4096, tz[0]):
+                hi = min(lo + tz[0], 4096)
+                act(T.TAB[:, lo:hi], T.TAB[:, 0:hi - lo], ["TZ"], ["+TZa"])
+        if c == "E":
+            act(T.EC[0:96, 2:3], T.EC[0:96, 1:2], ["EF"], ["EM"], scale=-MAGIC)
+        if c == "e0":
+            ts(T.I16B[:, 25:26], T.I16[:, 16:17], 4, OP.arith_shift_right, ["I8"], ["I1B"], 1, OP.bitwise_and)
+        if c == "e1":
+            copy(T.EC[:, 0:1], T.I16B[:, 25:26], ["I1B"], ["E1"])
+        if c == "d0":
+            copy(T.BH[0:64, :], T.BM[0:64, :], ["BM"], ["BH"])
+        if c == "d1":
+            tt(T.BH[0:32, :], T.BM[0:32, :], T.BH[0:32, :], OP.subtract, ["BM", "BH"], ["BH"])
+        if c == "tab":
+            for p in range(8):
+                dma(PAR["tabq"][p % len(PAR["tabq"])], "dtab", T.TAB[16 * p:16 * p + 2, :], T.BH[0:64, :], ["BH", "TZa"], ["+TAB", "+TZ"])
+        if c[:3] == "bas":
+            n = int(c[3])
+            for p in range(1, 8):
+                dma("S", "dbas%d" % n, T.BAS[16 * p:16 * p + 16, cuts[n]:cuts[n + 1]], T.bas[:, cuts[n]:cuts[n + 1]], [], ["+BAS%d" % n])
+        if c[:4] == "sent":
+            wait("S", ("sent" + c[4:], None, "D"))
+        if c == "ha":
+            for k in range(8):
+                dma("S", "dha", T.HA[:, cw * k:cw * k + cw], T.hit[16 * k:16 * k + 16, 0:8 * cw], [], ["+HA"])
+        if c == "bq":
+            for p in range(8):
+                dma("S", "dbq", T.BQ[16 * p:16 * p + 16, :], T.bas[:, 1024 * (p // 2):1024 * (p // 2) + w0], [], ["+BQ"])
+        if c == "hb":
+            dma("S", "dhb", T.HN[:], T.hit[:, 8 * cw:512], [], ["+HB"])
+            for k in range(8):
+                dma("S", "dhb", T.HB[16 * k:16 * k + 16], T.HA[k:128:8, 0:8 * cw], ["HA"], ["+HB"])
+        if c == "bp":
+            for j, b0 in paired.items():
+                for h in range(2):
+                    lo, hi = run(j[h])
+                    dma("S", "dbp", T.BP[64 * h:64 * h + 64, b0:b0 + hi - lo], T.BAS[64 * h:64 * h + 64, lo:hi], bas(lo, hi), ["+BP"])
+        if c == "prg":
+            for k in range(8):
+                dma("S", "dprg", T.PRG[16 * k:16 * k + 16, 0:nv], T.pro[:, nv * k:nv * k + nv], [], ["+PRG"])
+            for i, c1, nb, p1 in units:
+                dma("S", "dprg", T.PRA[c1 % 128:c1 % 128 + 16 * nb, c1 - c1 % 128:c1 - c1 % 128 + 128], T.pro[:, p1:p1 + 128 * nb], [], ["+PRA"])
+
+    def ready(c):
+        if c[0] in "xyw" and c[1:2].isdigit():
+            h = int(c[1])
+            rows, bank, Y = slice(64 * h, 64 * h + 64), "psT%d" % h, T["Y%d" % h]
+            if c[0] == "x":
+                for p in range(8):
+                    turn(T[bank][:, 64 * p:64 * p + 64], T.X[rows, p:1024:8], ["X%d" % h], ["+" + bank], rows)
+            elif c[0] == "y":
+                by[c[2]](Y[:], T[bank][:, 0:512], [bank], ["Y%d" % h])
+                for b in range(4):
+                    turn(T[bank][:, 512 + 128 * b:640 + 128 * b], Y[:, :, :, b], ["Y%d" % h], ["+" + bank])
+            else:
+                by[c[2]](T.W[:, 1024 * r + 512 * h:1024 * r + 512 * h + 512], T[bank][:, 512:1024], [bank], ["W%d%d" % (r, h)])
+        if c[0] == "s" and c[1:].isdigit():
+            share(int(c[1]))
+        if c == "K0":
+            zero(T.SL[:], 240, ["SL"], 0, 16)
+            zero(T.SL2[96:112, :], 34, ["SL2"], 96, 112)
+        if c == "K1":
+            act(T.SL[:, 112:128], T.IDB[0:16, 0:16], ["IDB", "SL"], ["+SL"])
+            act(T.SL2[96:112, 1:33:2], T.IDB[96:112, 96:112], ["IDB", "SL2"], ["+SL2"], scale=0.125)
+        if c == "k0":
+            act(T.EIG[96:112, :], T.ONE[96:112, 0:34], ["ONE"], ["EIG"], scale=0.125)
+        if c == "k1":
+            sel(T.SL[:], T.ONE[0:16, 0:240], [[-1, 240]], OP.is_equal, 112, 1, ["ONE"], ["SL"])
+            sel(T.SL2[96:112, :], T.EIG[96:112, :], [[-1, 34]], OP.is_equal, 1, 2, ["EIG"], ["SL2"], 96)
+        if c == "k2":
+            for p1 in (0, 32):
+                rows, key = slice(p1, p1 + 32), "SEL" + "ab"[p1 // 32]
+                sel(T.SEL2[rows, :], T.ONE[rows, :], [[-16, 2], [0, 128]], OP.is_ge, 0, 1, ["ONE"], [key], p1)
+                sel(T.SEL2[rows, :], T.SEL2[rows, :], [[16, 2], [0, 128]], OP.is_ge, 15, -1, [key], [key], p1)
+        if c == "k3":
+            fill(T.Z[:, 0:16], 16, 0, ["+Z0"])
+            fill(T.Z[:, 1040:1056], 16, 0, ["+Z0"])
+            fill(T.E4[:], 68, 0, ["E4"])
+        if c == "k4":
+            sel(T.E4[:, 3:67:4], T.ID16[:], [[0, 16]], OP.is_ge, 0, 0, ["ID16", "E4"], ["+E4"])
+        if c == "z0":
+            mset(T.Z[:, 0:16], 0.0, ["+Z0"])
+            mset(T.Z[:, 1040:1056], 0.0, ["+Z0"])
+        if c == "PK":
+            sel(T.PICK[:], T.ONE[:, 0:16], [[-1, 2], [-16, 8]], OP.is_equal, 0, 1, ["ONE"], ["PICK"])
+        if c == "rp":
+            sel(T.REP[:], T.ONE[0:16, 0:128], [[0, 8], [-1, 16]], OP.is_equal, 0, 1, ["ONE"], ["REP"])
+        if c[0] in "mgMn" and c[1:2].isdigit():
+            h = int(c[1])
+            bank, GT = PAR["look"].split()[h], T["GT%d" % h]
+            if c[0] == "m":
+                for x in range(16):
+                    mm(ps(bank, x, 256, step=16), T.WD[:, 2048 * h + x:2048 * h + 2048:16], T.PICK[:], ["WD%d" % h, "PICK"], ["+" + bank])
+            if c[0] == "g":
+                by[c[2]](GT[:], ps(bank, 0, 256), [bank], ["GT%d" % h])
+            if c[0] == "M":
+                for x in range(2):
+                    mm(ps(bank, 256, 384), GT[:, 128 * x:128 * x + 128], T.IDB[:], ["GT%d" % h, "IDB"], ["+" + bank], x == 0, x == 1)
+            if c[0] == "n":
+                copy(T.OW[:, 128 * h:128 * h + 128], ps(bank, 256, 384), [bank], ["OW%d" % h])
+        if c == "WB":
+            for a, bit in enumerate(([[0, 4], [16, 2]], None, [[16, 2], [0, 4]])):
+                rows, p1 = slice(32 * a, 32 * a + 32), 32 * a
+                if a == 1:
+                    for h in range(2):
+                        sel(T.WB[rows, 64 * h:64 * h + 64], T.ONE[rows, 0:64], [[16, 2], [0, 2], [1, 16]], OP.is_equal, 0, -1, ["ONE"], ["+WB"], p1)
+                else:
+                    sel(T.WB[rows, :], T.ONE[rows, 0:128], bit + [[1, 16]], OP.is_equal, 0, -1, ["ONE"], ["+WB"], p1)
+        if c == "b":
+            ts(T.BU[0:96], T.POS[0:96, :], T.EC[0:96, 0:1], OP.subtract, ["POS", "E1"], ["BU"], MAGIC, OP.add)
+        if c == "Ba":
+            for h in range(2):
+                act(T.B2[0:96, 128 * h:128 * h + 128], T.BU[0:96, :, h, :], ["BU", "EF", "EM"], ["+B2"], scale=T.EC[0:96, 1:2], bias=T.EC[0:96, 2:3])
+        if c == "O":
+            mm(ps("F", 0, 256), T.WB[0:96, :], T.B2[0:96, :], ["WB", "B2"], ["+psF"])
+        if c == "o":
+            copy(T.OU[:], ps("F", 0, 256), ["psF"], ["OU"])
+        if c == "gu":
+            copy(T.GU[:], T.GI[:], ["GI"], ["GU"])
+        if c in ("gz0", "gz1"):
+            rows = slice(64 * int(c[2]), 64 * int(c[2]) + 64)
+            ts(T.GZ[rows, :], T.GI[rows, :, int(c[2]), :], T.EC[rows, 5:6], OP.add, ["GI", "EQ"], ["+GZ"], 1040.0, OP.min)
+        if c == "p":
+            for c8 in range(8):
+                mm(ps("C", 0, 96), T.SL[:, 112 - 16 * c8:240 - 16 * c8], T.P3[:, c8:768:8], ["SL", "P3"], ["+psC"], c8 == 0, c8 == 7)
+            wait("P", ("P", None, "X"))
+            for h in range(2):
+                mm(ps("C", 96, 128), T.POS[96:112, 128 * h:128 * h + 128], T.SL2[96:112, 1 - h:33 - h], ["SL2", "ALB"], ["+psC"], h == 0, h == 1)
+        if c == "P":
+            act(T.XS[:], ps("C", 0, 128), ["psC"], ["XS"])
+        if c == "rv":
+            ts(ps("C", 128, 224), T.XS[:, 0:96], MAGIC, OP.add, ["XS"], ["+psC"], MAGIC, OP.subtract)
+        if c == "z":
+            tt(T.XD[:], T.XS[:, 0:96], ps("C", 128, 224), OP.subtract, ["XS", "psC"], ["XD"])
+        if c == "zb":
+            act(ps("C", 288, 352), T.XD[:, 0:64], ["XD"], ["+psC"], FN.Abs)
+            act(T.FS[:, 32:64], T.XD[:, 64:96], ["XD"], ["F1"], FN.Abs)
+        if c == "q":
+            act(ps("C", 224, 288), ps("C", 288, 352), ["psC"], ["+psC"], bias=1.0, scale=-1.0)
+            act(T.FS[:, 0:32], T.FS[:, 32:64], ["F1"], ["F0"], bias=1.0, scale=-1.0)
+        if c == "w":
+            for x in range(4):
+                tt(T.WXZ[:, 32 * x:32 * x + 32], ps("C", 224 + 64 * (x & 1), 256 + 64 * (x & 1)), T.FS[:, 32 * (x >> 1):32 * (x >> 1) + 32],
+                   OP.mult, ["psC", "F0", "F1"], ["+WXZ"])
+            for e in range(2):
+                tt(ps("C", 352 + 32 * e, 384 + 32 * e), ps("C", 256 + 64 * e, 288 + 64 * e), T.XS[:, 96:128], OP.mult, ["psC", "XS"], ["+FY"])
+        if c == "W":
+            for p in range(8):
+                x, y = (p & 1) + 2 * (p >> 2), p >> 1 & 1
+                tt(T.WT[:, :, p:64:8], T.WXZ[:, 32 * x:32 * x + 32], ps("C", 352 + 32 * y, 384 + 32 * y), OP.mult, ["WXZ", "FY", "psC"], ["+WT"])
+        if c == "B":
+            act(T.BG[:], T.BAS[:, 0:S].indirect(T.GU[:, 0:48]), bas(0, S) + ["GU"], ["BG"])
+        if c == "K":
+            act(T.SEL2[:, 128:256], T.ONE[:, 0:128], ["ONE", "E1"], ["SELb"], scale=T.EC[:, 0:1])
+            zero(T.E4[:], 68, ["E4"])
+        if c == "K2":
+            act(T.SEL2[:, 0:128], T.SEL2[:, 128:256], ["SELb"], ["SELa"], scale=-1.0, bias=1.0)
+            act(T.E4[:, 3:67:4], T.ID16[:], ["ID16", "E4"], ["+E4"])
+        if c == "za":
+            zero(T.Z[:, 0:16], 16, ["+Z0"])
+            zero(T.Z[:, 1040:1056], 16, ["+Z0"])
+        if c == "S":
+            send("b", "BG", "BFO", CAP)
+        if c == "KG":
+            fill(T.PU[:], 512, 0, ["PU"])
+            sel(T.KEEP[:], T.ONE[:], [[0, 32], [1, 8]], OP.not_equal, 0, 0, ["ONE"], ["KEEP"])
+            if "lq" in PAR["order"]:
+                sel(T.SELQ[0:64, :], T.ONE[0:64, 0:128], [[-16, 4], [0, 32]], OP.is_ge, 0, 1, ["ONE"], ["SELQ"])
+                sel(T.SELQ[0:64, :], T.SELQ[0:64, :], [[16, 4], [0, 32]], OP.is_ge, 15, -1, ["SELQ"], ["SELQ"])
+        if c == "k5":
+            sel(T.HS[:, 0:128], T.ONE[:, 0:128], [[0, 128]], OP.is_ge, 63, -1, ["ONE"], ["+HS"])
+            sel(T.HS[:, 128:256], T.ONE[:, 0:128], [[0, 128]], OP.is_ge, -64, 1, ["ONE"], ["+HS"])
+            fill(T.LIT[:, S + CAP * r:S + CAP * r + CAP], CAP, 0, ["+LIT"])
+            sel(T.IDF[:], T.ONE[:, 0:128], [[-1, 128]], OP.is_equal, 0, 1, ["ONE"], ["IDF"])
+
+    dots, via, dense = PAR["dots"].split(), PAR["via"].split(), [0]
+    used, done, held = {}, [], []
+
+    def part(c):
+        lo, hi = run(int(c[1]))
+        return {"": (lo, hi), "a": (lo, hi - 128), "b": (hi - 128, hi)}[c[2:]]
+
+    def sums(name):
+        n = int(name[1])
+        lo, hi = run(n)
+        for c in range(*part(name), 128):
+            k = 8 * ((hi - lo) // 128 * (n % 4) + (c - lo) // 128)
+            mm(ps(dots[n // 4], k, k + 8), T.T1[:, c:c + 128], T.GS[:], ["T1" + name[1:], "GS"], ["+" + dots[n // 4]])
+        if name[2:] != "a":
+            done.append(n)
+
+    def step(c):
+        if c[0] in "DE" and c[1:].isdigit():
+            lo, hi = 8 * dense[0], 8 * (dense[0] + int(c[1:]))
+            assert lo // 128 == (hi - 1) // 128
+            (act if c[0] == "D" else copy)(T.WD[:, 16 * lo:16 * hi], T.TAB[:, 0:4096].indirect(T.OU[:, lo:hi]), ["TAB", "OU"], ["+WD%d" % (lo // 128)])
+            dense[0] = hi // 8
+        if c[0] in "vGh" and c[1:].isdigit():
+            n = int(c[1:])
+            lo, hi = run(n)
+            corners, need = T.W[:, 0:4096].indirect(T.OW[:, 32 * n:32 * n + 32]), every + ["OW%d" % (n // 4)]
+            if c[0] == "v":
+                tt(T.T1[:, lo:hi], corners, T.BAS[:, lo:hi], OP.mult, need + bas(lo, hi), ["T1%d" % n])
+                held.append(c[1:])
+            elif c[0] == "G":
+                act(T.CG[:, lo:hi], corners, need, ["CG%d" % n])
+            elif c[0] == "h":
+                used[n] = via[len(used) % len(via)]
+                for k, bank in enumerate(banks(used[n], hi - lo)):
+                    m = min(512, hi - lo - 512 * k)
+                    mm(ps(bank, 0, m), T.REP[:], T.BAS[0:16, lo + 512 * k:lo + 512 * k + m], ["REP", "B16"], ["+" + bank])
+        if c[0] == "t" and c[1].isdigit():
+            n = int(c[1])
+            lo, hi = part(c)
+            c0 = run(n)[0]
+            tt(T.T1[:, lo:hi], T.CG[:, lo:hi], ps(used[n], lo - c0, hi - c0), OP.mult, banks(used[n], hi - c0) + ["CG%d" % n], ["T1" + c[1:]])
+            held.append(c[1:])
+        if c[0] == "u":
+            held.remove(c[1:])
+            sums(c)
+
+    def pieces(h):
+        u0, u1 = (0, U0) if h == 0 else (U0, 8)
+        lo, hi, n = 32 * u0, 32 * u1, str(h)
+        v, rest = T.SC[:, lo + 7:hi:8], T.R1[:, lo // 8:hi // 8]
+        top, mid, low = (T.PU[:, :, x, u0:u1] for x in range(3))
+
+        def last_piece():
+            tt(low, rest, mid, OP.subtract, ["R1" + n, "Pb" + n], ["Pc" + n])
+            for u in range(u0, u1):
+                for d in range(2):
+                    turn(T["psT" + n][64 * d:64 * d + 64, 128 * u:128 * u + 128], T.PU[:, :, :, u], ["Pa" + n, "Pb" + n, "Pc" + n], ["+psT" + n])
+        return [lambda: tt(T.DW[:, lo:hi], ps(dots[h], 0, hi - lo), T.WT[:, :, 8 * u0:8 * u1], OP.mult, [dots[h], "WT"], ["DW" + n]),
+                lambda: scan(T.SC[:, lo:hi], T.KEEP[:, 0:hi - lo], T.DW[:, lo:hi], ["KEEP", "DW" + n], ["SC" + n]),
+                lambda: copy(top, v, ["SC" + n, "PU"], ["Pa" + n]),
+                lambda: tt(rest, v, top, OP.subtract, ["SC" + n, "Pa" + n], ["R1" + n]),
+                lambda: copy(mid, rest, ["R1" + n], ["Pb" + n]),
+                last_piece]
+
+    chain = {"a": pieces(0), "c": pieces(1)}
+
+    ring, ahead = PAR["ring"].split(), [0, 0]
+    n2 = PAR["n2"]
+    cv = cw - n2
+    offsets = [(T.HU[:, 0:4 * cv], T.HB[:, 0:4, 0:cv]), (T.HU[:, 4 * cv:8 * cv], T.HB[:, 4:8, 0:cv]),
+               (T.HU[:, 8 * cv:8 * cw], T.HB[:, :, cv:cw]), (T.HU[:, 8 * cw:512], T.HN[:])]
+
+    def spread():
+        v = ahead[0]
+        n = jobs[v][0]
+        a, (lo, hi) = n % 4, run(n)
+        p1, c = 32 * (a // 2), 64 if len(jobs[v]) == 2 else 128 * (a % 2)
+        for k, bank in enumerate(banks(ring[v], hi - lo)):
+            m, z0 = min(512, hi - lo - 512 * k), 16 + lo % 1024 + 512 * k
+            mm(ps(bank, 0, m), T.SEL2[p1:p1 + 32, c:c + 128], T.Z[p1:p1 + 32, z0:z0 + m], ["SELa", "SELb", "RH%d" % (n // 4)], ["+" + bank])
+        ahead[0] = v + 1
+
+    def lit():
+        v = ahead[1]
+        c, e = run(jobs[v][0])
+        m, bs = e - c, banks(ring[v], e - c)
+        if len(jobs[v]) == 2:
+            d, key, b0 = run(jobs[v][1])[0], "LP%d" % v, paired[jobs[v]]
+            tt(T.LIT[:, c:e], ps(ring[v], 0, m), T.BP[:, b0:b0 + m], OP.mult, bs + ["BP"], ["+LIT", key])
+            how = PAR["copies"].split()[b0 // 512]
+
+            def half(x, out, in_, rd, w):
+                if how[x] == "A":
+                    act(out, in_, rd, w)
+                elif how[x] == "G":
+                    sel(out, in_, [[0, m]], OP.is_ge, 0, 0, rd, w, 64)
+                else:
+                    dma("S", "dcp%d%d" % (b0 // 512, x // 2), out, in_, rd, w)
+            halves.append(lambda: half(0, T.LIT[0:64, d:d + m], T.LIT[64:128, c:e], [key], ["+LIT"]))
+            halves.append(lambda: half(1, T.LIT[64:128, d:d + m], T.LIT[64:128, c:e], [key], ["+LIT"]))
+            thirds.append(lambda: half(2, T.LIT[64:128, c:e], T.LIT[0:64, c:e], [], ["+LIT", key]))
+        else:
+            tt(T.LIT[:, c:e], ps(ring[v], 0, m), T.BAS[:, c:e], OP.mult, bs + bas(c, e), ["+LIT"])
+        ahead[1] = v + 1
+
+    halves, thirds = [], []
+
+    def close(c):
+        if c in chain:
+            assert all(n + 4 * (c == "c") in done for n in range(4))
+            chain[c].pop(0)()
+        if c[0] == "R":
+            lo, hi = ((0, w0), (w0, 1024))[int(c[1])]
+            by[c[2]](T.Z[:, 16 + lo:16 + hi], T["psT" + c[1]][:, lo:hi], ["psT" + c[1]], ["RH" + c[1]])
+        if c == "q0":
+            for k, bank in enumerate(banks(PAR["quad"], w0)):
+                m = min(512, w0 - 512 * k)
+                mm(ps(bank, 0, m), T.SELQ[0:64, :], T.Z[0:64, 16 + 512 * k:16 + 512 * k + m], ["SELQ", "RH0"], ["+" + bank])
+        if c == "lq":
+            tt(T.LQ[:], ps(PAR["quad"], 0, w0), T.BQ[:], OP.mult, banks(PAR["quad"], w0) + ["BQ"], ["LQ"])
+            for a in range(4):
+                for q in range(4):
+                    dma("S", "dlq", T.LIT[32 * q:32 * q + 32, 1024 * a:1024 * a + w0], T.LQ[32 * a:32 * a + 32, :], ["LQ"], ["+LIQ"])
+        if c == "i":
+            copy(*offsets.pop(0), ["HB"], ["+HU"])
+        if c == "j":
+            spread()
+        if c == "l":
+            lit()
+        if c == "cp":
             halves.pop(0)()
-        for v in range(ahead[2], ahead[2] + 6):
-            spread(v)
-    while hu[0] < nh:
+        if c == "cq":
+            assert len(halves) <= 2 * (len(thirds) - 1)
+            thirds.pop(0)()
+        if c == "N":
+            for e, lo, hi in (("A", PAR["zg"], 24), ("V", 0, PAR["zg"])):
+                if lo < hi:
+                    by[e](T.ZG[:, 16 * lo:16 * hi], T.Z[:, 0:RW].indirect(T.GZ[:, lo:hi]), ["Z0", "RH0", "RH1", "GZ"], ["+ZG"])
+            send("3", "ZG", "ZF", 128)
+
+    for c in PAR["order"].split():
+        loads(c)
+        ready(c)
+        step(c)
+        close(c)
+    assert len(done) == 8 and dense[0] == 32 and not chain["a"] and not chain["c"]
+
+    assert ahead[1] == len(jobs) and not halves and not thirds and not held
+    while offsets:
         close("i")
     cut, (ba, bb) = min(max(r, 1), 2), PAR["seen"].split()
     for j in range(3):
-        at = 512 + CAP * (j - cut)
-        mm(ps(ba, at, at + CAP), T.ONEB[:], T.ZF[:, CAP * j:CAP * j + CAP], ["ONEB", "ZF"], ["+" + (ba if j < cut else bb)])
+        for h in range(2):
+            c = 512 + CAP * (j - cut) + 128 * h
+            mm(ps(ba, c, c + 128), T.HS[:, 128 * h:128 * h + 128], T.ZF[:, 128 * j:128 * j + 128], ["HS", "ZF"], ["+" + (ba if j < cut else bb)])
     for lo, hi, bank in ((0, cut, ba), (cut, 3, bb)):
         tt(T.LIT[:, S + CAP * others[lo]:S + CAP * (others[lo] + hi - lo)], ps(ba, 512 + CAP * (lo - cut), 512 + CAP * (hi - cut)),
            T.BFO[:, CAP * lo:CAP * hi], OP.mult, [bank, "BFO"], ["+LIT"])
 
     win = T.LIT[:, 0:S + N * CAP]
-    v1, v2 = PAR["v1"], PAR["v2"]
+    at("LIQ")["w"] += at("LIT")["w"][-1:]
 
     def on_vector(k, a, b, key):
         src = T.PRG if k == 0 else T.ACC
-        tt(T.ACC[:, 16 * a:16 * b], win.indirect(T.HU[:, cw * k + a:cw * k + b]), src[:, 16 * a:16 * b], OP.add,
-           ["LIT", "HU", "PRG"] + ([key] if k else []), [key])
+        tt(T.ACC[:, 16 * a:16 * b], win.indirect(T.HU[:, cv * k + a:cv * k + b]), src[:, 16 * a:16 * b], OP.add,
+           ["LIT", "LIQ", "HU", "PRG"] + ([key] if k else []), [key])
 
     def store(lo, hi, keys, queues):
         for k in range(8):
             dma(queues[k % len(queues)], "dy", T.y[:, nv * k + lo:nv * k + hi], T.ACC[16 * k:16 * k + 16, lo:hi], keys, [])
 
     def gather(call):
-        p0, n = call[0][3], 128 * sum(u[2] for u in call)
-        key = "GA%d" % p0
-        act(T.GA[:, p0 - (P - na):p0 - (P - na) + n], win.indirect(T.HU[:, p0 // 16:(p0 + n) // 16]), ["LIT", "HU"], [key])
+        p1, n = call[0][3], 128 * sum(u[2] for u in call)
+        key = "GA%d" % p1
+        act(T.GA[:, p1 - (P - na):p1 - (P - na) + n], win.indirect(T.HU[:, p1 // 16:(p1 + n) // 16]), ["LIT", "LIQ", "HU"], [key])
         for i, c, nb, p in call:
             bank, c0, st = ("psE", "psF")[i % 2], p - (P - na), 4 // nb
             for b in range(nb):
@@ -674,36 +671,43 @@ def rank_program(g, core, T, topo):
         act(T.OUT[0:n, c:c + w], ps(bank, 0, w, n), [bank], ["OUT%d" % i])
 
     def store_set(i):
-        for j, c, nb, p0 in units:
+        for j, c, nb, p1 in units:
             if j == i:
-                dma("S", "dy", T.y[:, p0:p0 + 128 * nb], T.OUT[c % 128:c % 128 + 16 * nb, c - c % 128:c - c % 128 + 128], ["OUT%d" % i], [])
+                dma("S", "dy", T.y[:, p1:p1 + 128 * nb], T.OUT[c % 128:c % 128 + 16 * nb, c - c % 128:c - c % 128 + 128], ["OUT%d" % i], [])
 
-    n2 = PAR["n2"]
-
-    def last(k):
+    def last(k, m):
         n, c0 = 16 * n2, na + 16 * n2 * k
         if k == 0:
             mm(ps("A", 0, n), T.IDB[:], T.PRG[:, nv - n:nv], ["IDB", "PRG"], ["+psA"], True, False)
-        act(T.GA[:, c0:c0 + n], win.indirect(T.HU[:, cw * k + cw - n2:cw * k + cw]), ["LIT", "HU"], ["GL%d" % k])
-        mm(ps("A", 0, n), T.IDF[:], T.GA[:, c0:c0 + n], ["IDF", "GL%d" % k], ["+psA"], False, k == 7)
+        act(T.GA[:, c0:c0 + m * n], win.indirect(T.HU[:, 8 * cv + n2 * k:8 * cv + n2 * (k + m)]), ["LIT", "LIQ", "HU"], ["GL%d" % k])
+        for x in range(m):
+            mm(ps("A", 0, n), T.IDF[:], T.GA[:, c0 + x * n:c0 + x * n + n], ["IDF", "GL%d" % k], ["+psA"], False, k + x == 7)
 
-    at = {"S": 0, "L": 0, "b": 0, "o": 0}
+    nth = {"S": 0, "L": 0, "b": 0, "o": 0}
     for c in PAR["flow"]:
-        {"S": lambda n: gather(calls[n]), "L": last, "b": back, "o": out}[c](at[c])
-        at[c] += 1
-    assert at == {"S": len(calls), "L": 8, "b": len(sets), "o": len(sets)}
-    act(T.ACC[:, nv - 16 * n2:nv], ps("A", 0, 16 * n2), ["psA"], ["ACCc"])
-    x, y, z = (0, v1, "ACCa"), (v1, v2, "ACCz"), (v2, cw - n2, "ACCb")
+        if c.isdigit():
+            last(nth["L"], int(c))
+            nth["L"] += int(c)
+        elif c == "c":
+            act(T.ACC[:, nv - 16 * n2:nv], ps("A", 0, 16 * n2), ["psA"], ["ACCc"])
+        else:
+            {"S": lambda n: gather(calls[n]), "b": back, "o": out}[c](nth[c])
+            nth[c] += 1
+    assert nth == {"S": len(calls), "L": 8, "b": len(sets), "o": len(sets)}
+    cols, col = {}, 0
+    for c, n in zip("xyzc", PAR["widths"] + (n2,)):
+        cols[c], col = (col, col + n), col + n
+    assert col == cw
     nxt = {"x": 0, "y": 0, "z": 0}
     for c in PAR["sums"]:
-        on_vector(nxt[c], *{"x": x, "y": y, "z": z}[c])
+        on_vector(nxt[c], *cols[c], "ACC" + c)
         nxt[c] += 1
-    two = not nxt["z"]
-    if not two:
-        store(0, 16 * v1, ["ACCa"], "S")
-    for i in range(len(sets)):
-        store_set(i)
-    store(16 * v1 * (not two), nv, ["ACCa", "ACCz", "ACCc"] + ["ACCb"] * (not two), "SA")
+    for names, queues in PAR["stores"]:
+        if names == "s":
+            for i in range(len(sets)):
+                store_set(i)
+        else:
+            store(16 * cols[names[0]][0], 16 * cols[names[-1]][1], ["ACC" + c for c in names], queues)
 
     for s in SEMAPHORES:
         wait("G" if s.startswith("sent") else "S", (s, None, "D"))

from concourse.bass import DstId, RemoteDMATransfer
from concourse.mybir import AluOpType, ActivationFunctionType

F32, BF, I32, U16 = "float32", "bfloat16", "int32", "uint16"
N, S, P, CAP = 4, 4096, 8192, 256
NG = (N - 1) * CAP
MAGIC = 25165824.0
RW = 1056
PAR = {"sets": (((4,), (4,), (4,), (4,)),), "n2": 12, "flow": "1111SS1SS1b11oc", "widths": (16, 10, 10), "sums": "xy" * 4 + "xz" * 4 + "yz" * 4,
       "stores": (("x", "S"), ("s", "S"), ("yzc", "SA")), "zg": 12,
       "first": "x0S m0A m1A x1A", "copies": "AAA AAA AAA AAA", "share": "hybrid", "u0": 4, "jobs": "01 23 4 5 6 7", "bas": (0, 512, 1536, 4096),
       "tz": (1024, 2560), "tabq": "S", "posq": "SSSSSS", "look": "psA psB", "dots": "psA psB", "via": "psD psE psF", "quad": "psC", "ring": "psC psF psD psE psA psB", "seen": "psE psF",
       "order": "pos p3 b16 bas0 c2 E tz WB PK x0 x1 d0 e0 d1 e1 tab gi y0v b y1v w0v s0 Ba K0 w1v s1 rp O K1 p o "
                "c0 c3 D9 z0 c1 E7 c4 E7 m0 s2 KG k5 sents1 bas1 bas2 ha hb bp prg P D9 rv g0v z gz0 gz1 zb q M0 m1 n0 gu w K g1a h2 h3 M1 h5 W "
                "G2 G3 v0 u0 t2 n1 G6 G5 G7 K2 B S t3 v1 v4 t5 u2 u3 h6 u1 u4 h7 a t6 a t7a a u5 u6 t7b a u7a a u7b a R0a "
                "c j i c i c i c i c c j l R1v N l cp cp cp cp cq cq j j j j l l l l"}

U0 = PAR["u0"]
CW = 64 - sum(sum(sum(c) for c in u) for u in PAR["sets"])
SB = {
    "X": ([128, 1024], BF), "Y0": ([128, 8, 16, 4], BF), "Y1": ([128, 8, 16, 4], BF), "W": ([128, 4096], BF), "WD": ([128, 4096], BF),
    "BAS": ([128, S], BF), "BQ": ([128, 128 * U0], BF), "BP": ([128, 2048], BF), "BG": ([128, NG], BF), "BFO": ([128, NG], BF), "CG": ([128, S], BF),
    "POS": ([128, 256], F32), "P3": ([16, 768], F32), "BM": ([64, 128], I32), "GI": ([128, 3, 2, 8], I32), "GU": ([128, 48], U16), "GZ": ([128, 24], U16),
    "BH": ([64, 128], BF), "TAB": ([128, 4096], BF), "PICK": ([128, 16], BF), "REP": ([16, 128], BF), "GT0": ([128, 256], BF), "GT1": ([128, 256], BF),
    "OW": ([128, 256], U16), "BU": ([128, 4, 2, 32], F32), "B2": ([128, 256], BF), "OU": ([128, 256], U16),
    "T1": ([128, S], F32), "XS": ([128, 128], F32), "XD": ([128, 96], F32), "EIG": ([128, 34], F32),
    "FS": ([128, 64], F32), "WXZ": ([128, 128], F32), "WT": ([128, 4, 64], F32),
    "DW": ([128, 256], F32), "SC": ([128, 256], F32), "R1": ([128, 32], F32), "PU": ([128, 4, 16, 8], BF),
    "Z": ([128, RW], BF), "ZG": ([128, NG // 2], BF), "ZF": ([128, NG // 2], BF), "LQ": ([128, 128 * U0], F32), "LIT": ([128, S + N * CAP], F32),
    "HA": ([128, 512], I32), "HB": ([128, 8, CW], I32), "HN": ([128, 512 - 8 * CW], I32), "HU": ([128, 512], U16),
    "PRG": ([128, 1024], BF), "ACC": ([128, 1024], F32), "GA": ([128, 5120], F32),
    "PRA": ([128, 768], BF), "SUM": ([128, 768], F32), "OUT": ([128, 768], F32), "E4": ([128, 68], F32),
    "ONE": ([128, 256], F32), "SL": ([16, 240], F32), "SL2": ([128, 34], F32), "I16": ([128, 32], I32), "I16B": ([128, 32], I32),
    "ID16": ([128, 16], F32), "GS": ([128, 8], F32), "EC": ([128, 24], F32),
    "WB": ([128, 128], BF), "IDF": ([128, 128], F32), "IDB": ([128, 128], BF),
    "SEL2": ([128, 256], BF), "SELQ": ([128, 128], BF), "HS": ([128, 256], BF), "KEEP": ([128, 256], F32),
}
SCRATCH = {k: ("sbuf", v[0], v[1]) for k, v in SB.items()}
SCRATCH["PS"] = ("psum", [128, 6 * 512], F32)
for _b in ("psT0", "psT1"):
    SCRATCH[_b] = ("psum", [128, 1024], BF)
SEMAPHORES = ["V", "A", "P", "G", "dpro0", "dpro1", "dgo", "dgb", "dtab", "dpos", "dalb", "db16", "dbas0", "dbas1", "dbas2", "dbas3", "dbq", "dbp", "dp3", "dha", "dhb", "dprg", "dlq", "dy",
              "dcp00", "dcp01", "dcp10", "dcp11", "dcp20", "dcp21", "dcp30", "dcp31",
              "hopw", "hopf0", "hopf1", "hop3", "hopb", "sents0", "sents1", "sents2", "sents3", "sent3", "sentb"]


def split_engines(topo, core, dsts):
    free = {d: list(topo.engines(core, d)) for d in dsts}
    fewest = min(len(v) for v in free.values())
    tight = [d for d in dsts if len(free[d]) == fewest]
    n = 1
    while 2 * n * len(tight) <= fewest:
        n *= 2
    used, masks = set(), {}
    for d in sorted(dsts, key=lambda d: len(free[d])):
        mine = [e for e in free[d] if e not in used][:n]
        used.update(mine)
        masks[d] = sum(1 << e for e in mine)
    return masks, n


def share_plan(topo, cores, r):
    me = cores[r]
    near = [q for q in range(N) if q != r and topo.chip(cores[q]) == topo.chip(me)][0]
    far = [q for q in range(N) if topo.chip(cores[q]) != topo.chip(me)]
    mate = [q for q in far if topo.die(cores[q]) == topo.die(me)][0]
    cross = [q for q in far if q != mate][0]
    out = topo.engines(me, cores[mate])
    on = [e for e in topo.engines(me, cores[near]) if e not in out]
    a, b = out[:len(out) // 2], out[len(out) // 2:]
    both = [[(mate, r, h, a, "hopw"), (cross, r, h, b, "hopw"), (near, r, h, on, "hopw")] for h in range(2)]
    first = [[(mate, r, h, out, "hopf%d" % h), (near, r, h, on, "hopw")] for h in range(2)]
    onward = [[(near, mate, h, on, "hopw")] for h in range(2)]
    return {"direct": both, "hybrid": [first[0], both[1], onward[0]], "relay": first + onward,
            "apart": [first[0][:1], both[1], onward[0], first[0][1:]]}[PAR["share"]]


def rank_program(g, core, T, topo):
    r = T.rank_of(core)
    if r is None:
        return
    others = [q for q in range(N) if q != r]
    there = [[x for x in range(N) if x != q].index(r) for q in others]
    cores = list(T.cores)
    masks, neng = split_engines(topo, core, [cores[q] for q in others])
    Q = {"V": g.vector, "A": g.scalar, "P": g.tensor, "G": g, "S": g.sync}
    OP, FN = AluOpType, ActivationFunctionType
    cnt, seen, state = {s: 0 for s in SEMAPHORES}, {}, {}

    def wait(q, tok):
        sem, val, src = tok
        if q == "P" and src == "P":
            return
        val = cnt[sem] if val is None else val
        if seen.get((q, sem), 0) < val:
            Q[q].wait_ge(T.sem[sem], val)
            seen[(q, sem)] = val

    def at(k):
        return state.setdefault(k, {"w": [], "base": [], "r": []})

    def before(q, reads, writes):
        toks = []
        for k in reads:
            st = at(k)
            assert st["w"], k
            toks += st["w"]
            if k.startswith("ps"):
                toks += [t for t in st["r"] if t[2] != q]
        for k in writes:
            st = at(k.lstrip("+"))
            toks += (st["base"] if k[0] == "+" else st["w"]) + st["r"]
            if k.startswith("+ps"):
                toks += [t for t in st["w"] if t[2] != q]
        for t in sorted(toks, key=lambda t: -(t[1] or 0)):
            wait(q, t)

    def after(tok, reads, writes):
        for k in reads:
            state[k]["r"].append(tok)
        for k in writes:
            st = state[k.lstrip("+")]
            if k[0] == "+":
                st["w"].append(tok)
            else:
                st["w"], st["base"], st["r"] = [tok], [tok], []

    def op(q, call, reads, writes):
        before(q, reads, writes)
        call().then_inc(T.sem[q], 1)
        cnt[q] += 1
        after((q, cnt[q], q), reads, writes)

    def dma(q, sem, out, in_, reads, writes):
        before(q, reads, writes)
        Q[q].dma_start(out, in_).then_inc(T.sem[sem], 16)
        cnt[sem] += 16
        after((sem, None, "D"), reads, writes)

    def transfer(q, mask, sem, src, dst):
        rid, pid, _ = topo.addr(cores[q])
        return RemoteDMATransfer(dst_ids=[DstId(rid=rid, pnc=pid)], dma_engine_mask=mask, remote_sem=T.sem[sem], src=src, dst=dst)

    def send(hop, src, dst, width):
        before("G", [src], [])
        g.remote_dma_fused([transfer(q, masks[cores[q]], "hop" + hop, T[src][:, width * j:width * j + width],
                                     T[dst][:, width * there[j]:width * there[j] + width]) for j, q in enumerate(others)], local_sem=T.sem["sent" + hop])
        cnt["sent" + hop] += neng * len(others)
        cnt["hop" + hop] += neng * len(others)
        at(dst)["w"].append(("hop" + hop, None, "D"))

    plan = share_plan(topo, cores, r)
    for q in others:
        for call in share_plan(topo, cores, q):
            for to, owner, h, engines, sem in call:
                if to == r:
                    cnt[sem] += len(engines)
                    at("W%d%d" % (owner, h))["w"].append((sem, None, "D"))
    every = ["W%d%d" % (q, h) for q in range(N) for h in range(2)]

    def share(n):
        if n < len(plan):
            before("G", ["W%d%d" % (owner, h) for _, owner, h, _, _ in plan[n]], [])
            cols = [T.W[:, 1024 * owner + 512 * h:1024 * owner + 512 * h + 512] for _, owner, h, _, _ in plan[n]]
            g.remote_dma_fused([transfer(t[0], sum(1 << e for e in t[3]), t[4], c, c) for t, c in zip(plan[n], cols)], local_sem=T.sem["sents%d" % n])
            cnt["sents%d" % n] += sum(len(t[3]) for t in plan[n])

    V, A, PE = g.vector, g.scalar, g.tensor

    def ps(bank, lo, hi, rows=128, row0=0, step=1):
        c = 512 * "ABCDEF".index(bank[-1])
        return T.PS[row0:rows, c + lo:c + hi:step]

    def banks(bank, n):
        b = "ABCDEF".index(bank[-1])
        return ["ps" + x for x in "ABCDEF"[b:b - (-n // 512)]]

    def copy(out, in_, rd, w):
        op("V", lambda: V.tensor_copy(out, in_), rd, w)

    def mset(out, c, w):
        op("V", lambda: V.memset(out, c), [], w)

    def tt(out, a, b, o, rd, w):
        op("V", lambda: V.tensor_tensor(out, a, b, o), rd, w)

    def ts(out, a, s1, o0, rd, w, s2=None, o1=None):
        if o1 is None:
            op("V", lambda: V.tensor_scalar(out, a, s1, None, o0), rd, w)
        else:
            op("V", lambda: V.tensor_scalar(out, a, s1, s2, o0, o1), rd, w)

    def scan(out, keep, data, rd, w):
        op("V", lambda: V.tensor_tensor_scan(out, keep, data, 0.0, OP.mult, OP.add), rd, w)

    def act(out, in_, rd, w, func=None, **kw):
        plain = FN.Identity if kw else FN.Copy
        op("A", lambda: A.activation(out, in_, plain if func is None else func, **kw), rd, w)

    by = {"v": copy, "a": act, "V": copy, "A": act}

    def mm(out, lhsT, rhs, rd, w, start=True, stop=True):
        op("P", lambda: PE.matmul(out, lhsT, rhs, start, stop), rd, w)

    def turn(out, in_, rd, w, rows=slice(0, 128)):
        op("P", lambda: PE.transpose(out, in_, T.IDB[rows, rows]), rd + ["IDB"], w)

    start = [0]

    def pool(call, p0, rd, w):
        if p0 != start[0]:
            wait("G", ("G", None, "G"))
            start[0] = p0
        op("G", call, rd, w)

    def sel(out, in_, pat, cmp, base, cm, rd, w, p0=0):
        pool(lambda: g.affine_select(out, in_, pat, cmp, 0.0, base, cm), p0, rd, w)

    def iota(out, pat, base, cm, w, p0=0):
        pool(lambda: g.iota(out, pat, base, cm), p0, [], w)

    def fill(out, n, c, w, p0=0):
        pool(lambda: g.iota(out, [[0, n]], c, 0, allow_small_or_imprecise_dtypes=True), p0, [], w)

    def zero(out, n, w, lo=0, hi=128):
        act(out, T.ONE[lo:hi, 0:n], ["ONE"], w, scale=0.0)

    sets = PAR["sets"]
    na = 128 * sum(sum(sum(c) for c in u) for u in sets)
    cw = (P - na) // 128
    nv = 16 * cw
    w0 = 128 * U0

    def run(n):
        return (1024 * n, 1024 * n + w0) if n < 4 else (1024 * (n - 4) + w0, 1024 * (n - 3))

    jobs, paired, col = [tuple(int(x) for x in j) for j in PAR["jobs"].split()], {}, 0
    for j in jobs:
        if len(j) == 2:
            paired[j], col = col, col + run(j[0])[1] - run(j[0])[0]
    cuts = PAR["bas"]

    def bas(lo, hi):
        return ["B16"] + ["BAS%d" % n for n in range(len(cuts) - 1) if max(lo, cuts[n]) < min(hi, cuts[n + 1])]

    calls, first, p0, col = [], [], P - na, 0
    for i, u in enumerate(sets):
        first.append(col)
        for c in u:
            calls.append([])
            for nb in c:
                calls[-1].append((i, col, nb, p0))
                col, p0 = col + 16 * nb, p0 + 128 * nb
        col = -(-col // 128) * 128
    units = [u for c in calls for u in c]

    for c in PAR["first"].split():
        h = int(c[1])
        if c[0] == "m":
            dma(c[2], "dgb", T.BM[32 * h:32 * h + 32, :], T.bmap[:], [], ["+BM"])
        else:
            dma(c[2], "dpro%d" % h, T.X[64 * h:64 * h + 64, :], T.pro[:, 4096 * h:4096 * h + 4096], [], ["X%d" % h])

    tz = PAR["tz"]
    mset(T.ONE[:], 1.0, ["ONE"])
    mset(T.TAB[:, 0:tz[0]], 0.0, ["TZ"])
    mset(T.TAB[:, tz[0]:tz[1]], 0.0, ["+TZa"])
    iota(T.I16[:, 0:16], [[-1, 16]], 16, 1, ["I16"])
    iota(T.I16[:, 16:24], [[-16, 8]], 0, 1, ["I8"])
    sel(T.IDB[:], T.ONE[:, 0:128], [[-1, 128]], OP.is_equal, 0, 1, ["ONE"], ["IDB"])

    def loads(c):
        if c == "c0":
            ts(T.I16B[:, 16:24], T.I16[:, 16:24], 4, OP.arith_shift_right, ["I8"], ["I8B"])
            ts(T.I16B[:, 0:16], T.I16[:, 0:16], 15, OP.bitwise_and, ["I16"], ["I16B"])
        if c == "c1":
            ts(T.GS[:], T.I16B[:, 16:24], 0.0, OP.is_equal, ["I8B"], ["GS"])
            ts(T.ID16[:], T.I16B[:, 0:16], 0.0, OP.is_equal, ["I16B"], ["ID16"])
        if c == "c2":
            for a, factor in enumerate((1.0, 16.0, 256.0)):
                act(T.EC[32 * a:32 * a + 32, 1:2], T.ONE[32 * a:32 * a + 32, 0:1], ["ONE"], ["+EF"], scale=0.5 * factor)
        if c == "c3":
            ts(T.I16B[:, 24:25], T.I16[:, 16:17], 4, OP.arith_shift_right, ["I8"], ["I4B"], 3, OP.bitwise_and)
        if c == "c4":
            ts(T.EC[:, 5:6], T.I16B[:, 24:25], -1024.0, OP.mult, ["I4B"], ["EQ"], 16.0, OP.add)
        if c == "b16":
            dma("S", "db16", T.BAS[0:16, :], T.bas[:], [], ["B16"])
        if c == "pos":
            for k in range(6):
                dma(PAR["posq"][k], "dpos", T.POS[16 * k:16 * k + 16, :], T.pos[16 * (k // 2):16 * (k // 2) + 16, :], [], ["+POS"])
        if c == "p3":
            for a in range(3):
                dma("S", "dp3", T.P3[:, 256 * a:256 * a + 256], T.pos[16 * a:16 * a + 16, :], [], ["+P3"])
            dma("S", "dalb", T.POS[96:112, :], T.alb[:], [], ["+ALB"])
        if c == "gi":
            for p in range(8):
                for lo, hi, j in ((0, r, 0), (r + 1, N, r)):
                    if lo < hi:
                        dma("S", "dgo", T.GI[16 * p:16 * p + 16, j:j + hi - lo], T.go[:, 16 * lo:16 * hi], [], ["+GI"])
        if c == "tz":
            for lo in range(tz[1], 4096, tz[0]):
                hi = min(lo + tz[0], 4096)
                act(T.TAB[:, lo:hi], T.TAB[:, 0:hi - lo], ["TZ"], ["+TZa"])
        if c == "E":
            act(T.EC[0:96, 2:3], T.EC[0:96, 1:2], ["EF"], ["EM"], scale=-MAGIC)
        if c == "e0":
            ts(T.I16B[:, 25:26], T.I16[:, 16:17], 4, OP.arith_shift_right, ["I8"], ["I1B"], 1, OP.bitwise_and)
        if c == "e1":
            copy(T.EC[:, 0:1], T.I16B[:, 25:26], ["I1B"], ["E1"])
        if c == "d0":
            copy(T.BH[0:64, :], T.BM[0:64, :], ["BM"], ["BH"])
        if c == "d1":
            tt(T.BH[0:32, :], T.BM[0:32, :], T.BH[0:32, :], OP.subtract, ["BM", "BH"], ["BH"])
        if c == "tab":
            for p in range(8):
                dma(PAR["tabq"][p % len(PAR["tabq"])], "dtab", T.TAB[16 * p:16 * p + 2, :], T.BH[0:64, :], ["BH", "TZa"], ["+TAB", "+TZ"])
        if c[:3] == "bas":
            n = int(c[3])
            for p in range(1, 8):
                dma("S", "dbas%d" % n, T.BAS[16 * p:16 * p + 16, cuts[n]:cuts[n + 1]], T.bas[:, cuts[n]:cuts[n + 1]], [], ["+BAS%d" % n])
        if c[:4] == "sent":
            wait("S", ("sent" + c[4:], None, "D"))
        if c == "ha":
            for k in range(8):
                dma("S", "dha", T.HA[:, cw * k:cw * k + cw], T.hit[16 * k:16 * k + 16, 0:8 * cw], [], ["+HA"])
        if c == "bq":
            for p in range(8):
                dma("S", "dbq", T.BQ[16 * p:16 * p + 16, :], T.bas[:, 1024 * (p // 2):1024 * (p // 2) + w0], [], ["+BQ"])
        if c == "hb":
            dma("S", "dhb", T.HN[:], T.hit[:, 8 * cw:512], [], ["+HB"])
            for k in range(8):
                dma("S", "dhb", T.HB[16 * k:16 * k + 16], T.HA[k:128:8, 0:8 * cw], ["HA"], ["+HB"])
        if c == "bp":
            for j, b0 in paired.items():
                for h in range(2):
                    lo, hi = run(j[h])
                    dma("S", "dbp", T.BP[64 * h:64 * h + 64, b0:b0 + hi - lo], T.BAS[64 * h:64 * h + 64, lo:hi], bas(lo, hi), ["+BP"])
        if c == "prg":
            for k in range(8):
                dma("S", "dprg", T.PRG[16 * k:16 * k + 16, 0:nv], T.pro[:, nv * k:nv * k + nv], [], ["+PRG"])
            for i, c1, nb, p1 in units:
                dma("S", "dprg", T.PRA[c1 % 128:c1 % 128 + 16 * nb, c1 - c1 % 128:c1 - c1 % 128 + 128], T.pro[:, p1:p1 + 128 * nb], [], ["+PRA"])

    def ready(c):
        if c[0] in "xyw" and c[1:2].isdigit():
            h = int(c[1])
            rows, bank, Y = slice(64 * h, 64 * h + 64), "psT%d" % h, T["Y%d" % h]
            if c[0] == "x":
                for p in range(8):
                    turn(T[bank][:, 64 * p:64 * p + 64], T.X[rows, p:1024:8], ["X%d" % h], ["+" + bank], rows)
            elif c[0] == "y":
                by[c[2]](Y[:], T[bank][:, 0:512], [bank], ["Y%d" % h])
                for b in range(4):
                    turn(T[bank][:, 512 + 128 * b:640 + 128 * b], Y[:, :, :, b], ["Y%d" % h], ["+" + bank])
            else:
                by[c[2]](T.W[:, 1024 * r + 512 * h:1024 * r + 512 * h + 512], T[bank][:, 512:1024], [bank], ["W%d%d" % (r, h)])
        if c[0] == "s" and c[1:].isdigit():
            share(int(c[1]))
        if c == "K0":
            zero(T.SL[:], 240, ["SL"], 0, 16)
            zero(T.SL2[96:112, :], 34, ["SL2"], 96, 112)
        if c == "K1":
            act(T.SL[:, 112:128], T.IDB[0:16, 0:16], ["IDB", "SL"], ["+SL"])
            act(T.SL2[96:112, 1:33:2], T.IDB[96:112, 96:112], ["IDB", "SL2"], ["+SL2"], scale=0.125)
        if c == "k0":
            act(T.EIG[96:112, :], T.ONE[96:112, 0:34], ["ONE"], ["EIG"], scale=0.125)
        if c == "k1":
            sel(T.SL[:], T.ONE[0:16, 0:240], [[-1, 240]], OP.is_equal, 112, 1, ["ONE"], ["SL"])
            sel(T.SL2[96:112, :], T.EIG[96:112, :], [[-1, 34]], OP.is_equal, 1, 2, ["EIG"], ["SL2"], 96)
        if c == "k2":
            for p1 in (0, 32):
                rows, key = slice(p1, p1 + 32), "SEL" + "ab"[p1 // 32]
                sel(T.SEL2[rows, :], T.ONE[rows, :], [[-16, 2], [0, 128]], OP.is_ge, 0, 1, ["ONE"], [key], p1)
                sel(T.SEL2[rows, :], T.SEL2[rows, :], [[16, 2], [0, 128]], OP.is_ge, 15, -1, [key], [key], p1)
        if c == "k3":
            fill(T.Z[:, 0:16], 16, 0, ["+Z0"])
            fill(T.Z[:, 1040:1056], 16, 0, ["+Z0"])
            fill(T.E4[:], 68, 0, ["E4"])
        if c == "k4":
            sel(T.E4[:, 3:67:4], T.ID16[:], [[0, 16]], OP.is_ge, 0, 0, ["ID16", "E4"], ["+E4"])
        if c == "z0":
            mset(T.Z[:, 0:16], 0.0, ["+Z0"])
            mset(T.Z[:, 1040:1056], 0.0, ["+Z0"])
        if c == "PK":
            sel(T.PICK[:], T.ONE[:, 0:16], [[-1, 2], [-16, 8]], OP.is_equal, 0, 1, ["ONE"], ["PICK"])
        if c == "rp":
            sel(T.REP[:], T.ONE[0:16, 0:128], [[0, 8], [-1, 16]], OP.is_equal, 0, 1, ["ONE"], ["REP"])
        if c[0] in "mgMn" and c[1:2].isdigit():
            h = int(c[1])
            bank, GT = PAR["look"].split()[h], T["GT%d" % h]
            if c[0] == "m":
                for x in range(16):
                    mm(ps(bank, x, 256, step=16), T.WD[:, 2048 * h + x:2048 * h + 2048:16], T.PICK[:], ["WD%d" % h, "PICK"], ["+" + bank])
            if c[0] == "g":
                by[c[2]](GT[:], ps(bank, 0, 256), [bank], ["GT%d" % h])
            if c[0] == "M":
                for x in range(2):
                    mm(ps(bank, 256, 384), GT[:, 128 * x:128 * x + 128], T.IDB[:], ["GT%d" % h, "IDB"], ["+" + bank], x == 0, x == 1)
            if c[0] == "n":
                copy(T.OW[:, 128 * h:128 * h + 128], ps(bank, 256, 384), [bank], ["OW%d" % h])
        if c == "WB":
            for a, bit in enumerate(([[0, 4], [16, 2]], None, [[16, 2], [0, 4]])):
                rows, p1 = slice(32 * a, 32 * a + 32), 32 * a
                if a == 1:
                    for h in range(2):
                        sel(T.WB[rows, 64 * h:64 * h + 64], T.ONE[rows, 0:64], [[16, 2], [0, 2], [1, 16]], OP.is_equal, 0, -1, ["ONE"], ["+WB"], p1)
                else:
                    sel(T.WB[rows, :], T.ONE[rows, 0:128], bit + [[1, 16]], OP.is_equal, 0, -1, ["ONE"], ["+WB"], p1)
        if c == "b":
            ts(T.BU[0:96], T.POS[0:96, :], T.EC[0:96, 0:1], OP.subtract, ["POS", "E1"], ["BU"], MAGIC, OP.add)
        if c == "Ba":
            for h in range(2):
                act(T.B2[0:96, 128 * h:128 * h + 128], T.BU[0:96, :, h, :], ["BU", "EF", "EM"], ["+B2"], scale=T.EC[0:96, 1:2], bias=T.EC[0:96, 2:3])
        if c == "O":
            mm(ps("F", 0, 256), T.WB[0:96, :], T.B2[0:96, :], ["WB", "B2"], ["+psF"])
        if c == "o":
            copy(T.OU[:], ps("F", 0, 256), ["psF"], ["OU"])
        if c == "gu":
            copy(T.GU[:], T.GI[:], ["GI"], ["GU"])
        if c in ("gz0", "gz1"):
            rows = slice(64 * int(c[2]), 64 * int(c[2]) + 64)
            ts(T.GZ[rows, :], T.GI[rows, :, int(c[2]), :], T.EC[rows, 5:6], OP.add, ["GI", "EQ"], ["+GZ"], 1040.0, OP.min)
        if c == "p":
            for c8 in range(8):
                mm(ps("C", 0, 96), T.SL[:, 112 - 16 * c8:240 - 16 * c8], T.P3[:, c8:768:8], ["SL", "P3"], ["+psC"], c8 == 0, c8 == 7)
            wait("P", ("P", None, "X"))
            for h in range(2):
                mm(ps("C", 96, 128), T.POS[96:112, 128 * h:128 * h + 128], T.SL2[96:112, 1 - h:33 - h], ["SL2", "ALB"], ["+psC"], h == 0, h == 1)
        if c == "P":
            act(T.XS[:], ps("C", 0, 128), ["psC"], ["XS"])
        if c == "rv":
            ts(ps("C", 128, 224), T.XS[:, 0:96], MAGIC, OP.add, ["XS"], ["+psC"], MAGIC, OP.subtract)
        if c == "z":
            tt(T.XD[:], T.XS[:, 0:96], ps("C", 128, 224), OP.subtract, ["XS", "psC"], ["XD"])
        if c == "zb":
            act(ps("C", 288, 352), T.XD[:, 0:64], ["XD"], ["+psC"], FN.Abs)
            act(T.FS[:, 32:64], T.XD[:, 64:96], ["XD"], ["F1"], FN.Abs)
        if c == "q":
            act(ps("C", 224, 288), ps("C", 288, 352), ["psC"], ["+psC"], bias=1.0, scale=-1.0)
            act(T.FS[:, 0:32], T.FS[:, 32:64], ["F1"], ["F0"], bias=1.0, scale=-1.0)
        if c == "w":
            for x in range(4):
                tt(T.WXZ[:, 32 * x:32 * x + 32], ps("C", 224 + 64 * (x & 1), 256 + 64 * (x & 1)), T.FS[:, 32 * (x >> 1):32 * (x >> 1) + 32],
                   OP.mult, ["psC", "F0", "F1"], ["+WXZ"])
            for e in range(2):
                tt(ps("C", 352 + 32 * e, 384 + 32 * e), ps("C", 256 + 64 * e, 288 + 64 * e), T.XS[:, 96:128], OP.mult, ["psC", "XS"], ["+FY"])
        if c == "W":
            for p in range(8):
                x, y = (p & 1) + 2 * (p >> 2), p >> 1 & 1
                tt(T.WT[:, :, p:64:8], T.WXZ[:, 32 * x:32 * x + 32], ps("C", 352 + 32 * y, 384 + 32 * y), OP.mult, ["WXZ", "FY", "psC"], ["+WT"])
        if c == "B":
            act(T.BG[:], T.BAS[:, 0:S].indirect(T.GU[:, 0:48]), bas(0, S) + ["GU"], ["BG"])
        if c == "K":
            act(T.SEL2[:, 128:256], T.ONE[:, 0:128], ["ONE", "E1"], ["SELb"], scale=T.EC[:, 0:1])
            zero(T.E4[:], 68, ["E4"])
        if c == "K2":
            act(T.SEL2[:, 0:128], T.SEL2[:, 128:256], ["SELb"], ["SELa"], scale=-1.0, bias=1.0)
            act(T.E4[:, 3:67:4], T.ID16[:], ["ID16", "E4"], ["+E4"])
        if c == "za":
            zero(T.Z[:, 0:16], 16, ["+Z0"])
            zero(T.Z[:, 1040:1056], 16, ["+Z0"])
        if c == "S":
            send("b", "BG", "BFO", CAP)
        if c == "KG":
            fill(T.PU[:], 512, 0, ["PU"])
            sel(T.KEEP[:], T.ONE[:], [[0, 32], [1, 8]], OP.not_equal, 0, 0, ["ONE"], ["KEEP"])
            if "lq" in PAR["order"]:
                sel(T.SELQ[0:64, :], T.ONE[0:64, 0:128], [[-16, 4], [0, 32]], OP.is_ge, 0, 1, ["ONE"], ["SELQ"])
                sel(T.SELQ[0:64, :], T.SELQ[0:64, :], [[16, 4], [0, 32]], OP.is_ge, 15, -1, ["SELQ"], ["SELQ"])
        if c == "k5":
            sel(T.HS[:, 0:128], T.ONE[:, 0:128], [[0, 128]], OP.is_ge, 63, -1, ["ONE"], ["+HS"])
            sel(T.HS[:, 128:256], T.ONE[:, 0:128], [[0, 128]], OP.is_ge, -64, 1, ["ONE"], ["+HS"])
            fill(T.LIT[:, S + CAP * r:S + CAP * r + CAP], CAP, 0, ["+LIT"])
            sel(T.IDF[:], T.ONE[:, 0:128], [[-1, 128]], OP.is_equal, 0, 1, ["ONE"], ["IDF"])

    dots, via, dense = PAR["dots"].split(), PAR["via"].split(), [0]
    used, done, held = {}, [], []

    def part(c):
        lo, hi = run(int(c[1]))
        return {"": (lo, hi), "a": (lo, hi - 128), "b": (hi - 128, hi)}[c[2:]]

    def sums(name):
        n = int(name[1])
        lo, hi = run(n)
        for c in range(*part(name), 128):
            k = 8 * ((hi - lo) // 128 * (n % 4) + (c - lo) // 128)
            mm(ps(dots[n // 4], k, k + 8), T.T1[:, c:c + 128], T.GS[:], ["T1" + name[1:], "GS"], ["+" + dots[n // 4]])
        if name[2:] != "a":
            done.append(n)

    def step(c):
        if c[0] in "DE" and c[1:].isdigit():
            lo, hi = 8 * dense[0], 8 * (dense[0] + int(c[1:]))
            assert lo // 128 == (hi - 1) // 128
            (act if c[0] == "D" else copy)(T.WD[:, 16 * lo:16 * hi], T.TAB[:, 0:4096].indirect(T.OU[:, lo:hi]), ["TAB", "OU"], ["+WD%d" % (lo // 128)])
            dense[0] = hi // 8
        if c[0] in "vGh" and c[1:].isdigit():
            n = int(c[1:])
            lo, hi = run(n)
            corners, need = T.W[:, 0:4096].indirect(T.OW[:, 32 * n:32 * n + 32]), every + ["OW%d" % (n // 4)]
            if c[0] == "v":
                tt(T.T1[:, lo:hi], corners, T.BAS[:, lo:hi], OP.mult, need + bas(lo, hi), ["T1%d" % n])
                held.append(c[1:])
            elif c[0] == "G":
                act(T.CG[:, lo:hi], corners, need, ["CG%d" % n])
            elif c[0] == "h":
                used[n] = via[len(used) % len(via)]
                for k, bank in enumerate(banks(used[n], hi - lo)):
                    m = min(512, hi - lo - 512 * k)
                    mm(ps(bank, 0, m), T.REP[:], T.BAS[0:16, lo + 512 * k:lo + 512 * k + m], ["REP", "B16"], ["+" + bank])
        if c[0] == "t" and c[1].isdigit():
            n = int(c[1])
            lo, hi = part(c)
            c0 = run(n)[0]
            tt(T.T1[:, lo:hi], T.CG[:, lo:hi], ps(used[n], lo - c0, hi - c0), OP.mult, banks(used[n], hi - c0) + ["CG%d" % n], ["T1" + c[1:]])
            held.append(c[1:])
        if c[0] == "u":
            held.remove(c[1:])
            sums(c)

    def pieces(h):
        u0, u1 = (0, U0) if h == 0 else (U0, 8)
        lo, hi, n = 32 * u0, 32 * u1, str(h)
        v, rest = T.SC[:, lo + 7:hi:8], T.R1[:, lo // 8:hi // 8]
        top, mid, low = (T.PU[:, :, x, u0:u1] for x in range(3))

        def last_piece():
            tt(low, rest, mid, OP.subtract, ["R1" + n, "Pb" + n], ["Pc" + n])
            for u in range(u0, u1):
                for d in range(2):
                    turn(T["psT" + n][64 * d:64 * d + 64, 128 * u:128 * u + 128], T.PU[:, :, :, u], ["Pa" + n, "Pb" + n, "Pc" + n], ["+psT" + n])
        return [lambda: tt(T.DW[:, lo:hi], ps(dots[h], 0, hi - lo), T.WT[:, :, 8 * u0:8 * u1], OP.mult, [dots[h], "WT"], ["DW" + n]),
                lambda: scan(T.SC[:, lo:hi], T.KEEP[:, 0:hi - lo], T.DW[:, lo:hi], ["KEEP", "DW" + n], ["SC" + n]),
                lambda: copy(top, v, ["SC" + n, "PU"], ["Pa" + n]),
                lambda: tt(rest, v, top, OP.subtract, ["SC" + n, "Pa" + n], ["R1" + n]),
                lambda: copy(mid, rest, ["R1" + n], ["Pb" + n]),
                last_piece]

    chain = {"a": pieces(0), "c": pieces(1)}

    ring, ahead = PAR["ring"].split(), [0, 0]
    n2 = PAR["n2"]
    cv = cw - n2
    offsets = [(T.HU[:, 0:4 * cv], T.HB[:, 0:4, 0:cv]), (T.HU[:, 4 * cv:8 * cv], T.HB[:, 4:8, 0:cv]),
               (T.HU[:, 8 * cv:8 * cw], T.HB[:, :, cv:cw]), (T.HU[:, 8 * cw:512], T.HN[:])]

    def spread():
        v = ahead[0]
        n = jobs[v][0]
        a, (lo, hi) = n % 4, run(n)
        p1, c = 32 * (a // 2), 64 if len(jobs[v]) == 2 else 128 * (a % 2)
        for k, bank in enumerate(banks(ring[v], hi - lo)):
            m, z0 = min(512, hi - lo - 512 * k), 16 + lo % 1024 + 512 * k
            mm(ps(bank, 0, m), T.SEL2[p1:p1 + 32, c:c + 128], T.Z[p1:p1 + 32, z0:z0 + m], ["SELa", "SELb", "RH%d" % (n // 4)], ["+" + bank])
        ahead[0] = v + 1

    def lit():
        v = ahead[1]
        c, e = run(jobs[v][0])
        m, bs = e - c, banks(ring[v], e - c)
        if len(jobs[v]) == 2:
            d, key, b0 = run(jobs[v][1])[0], "LP%d" % v, paired[jobs[v]]
            tt(T.LIT[:, c:e], ps(ring[v], 0, m), T.BP[:, b0:b0 + m], OP.mult, bs + ["BP"], ["+LIT", key])
            how = PAR["copies"].split()[b0 // 512]

            def half(x, out, in_, rd, w):
                if how[x] == "A":
                    act(out, in_, rd, w)
                elif how[x] == "G":
                    sel(out, in_, [[0, m]], OP.is_ge, 0, 0, rd, w, 64)
                else:
                    dma("S", "dcp%d%d" % (b0 // 512, x // 2), out, in_, rd, w)
            halves.append(lambda: half(0, T.LIT[0:64, d:d + m], T.LIT[64:128, c:e], [key], ["+LIT"]))
            halves.append(lambda: half(1, T.LIT[64:128, d:d + m], T.LIT[64:128, c:e], [key], ["+LIT"]))
            thirds.append(lambda: half(2, T.LIT[64:128, c:e], T.LIT[0:64, c:e], [], ["+LIT", key]))
        else:
            tt(T.LIT[:, c:e], ps(ring[v], 0, m), T.BAS[:, c:e], OP.mult, bs + bas(c, e), ["+LIT"])
        ahead[1] = v + 1

    halves, thirds = [], []

    def close(c):
        if c in chain:
            assert all(n + 4 * (c == "c") in done for n in range(4))
            chain[c].pop(0)()
        if c[0] == "R":
            lo, hi = ((0, w0), (w0, 1024))[int(c[1])]
            by[c[2]](T.Z[:, 16 + lo:16 + hi], T["psT" + c[1]][:, lo:hi], ["psT" + c[1]], ["RH" + c[1]])
        if c == "q0":
            for k, bank in enumerate(banks(PAR["quad"], w0)):
                m = min(512, w0 - 512 * k)
                mm(ps(bank, 0, m), T.SELQ[0:64, :], T.Z[0:64, 16 + 512 * k:16 + 512 * k + m], ["SELQ", "RH0"], ["+" + bank])
        if c == "lq":
            tt(T.LQ[:], ps(PAR["quad"], 0, w0), T.BQ[:], OP.mult, banks(PAR["quad"], w0) + ["BQ"], ["LQ"])
            for a in range(4):
                for q in range(4):
                    dma("S", "dlq", T.LIT[32 * q:32 * q + 32, 1024 * a:1024 * a + w0], T.LQ[32 * a:32 * a + 32, :], ["LQ"], ["+LIQ"])
        if c == "i":
            copy(*offsets.pop(0), ["HB"], ["+HU"])
        if c == "j":
            spread()
        if c == "l":
            lit()
        if c == "cp":
            halves.pop(0)()
        if c == "cq":
            assert len(halves) <= 2 * (len(thirds) - 1)
            thirds.pop(0)()
        if c == "N":
            for e, lo, hi in (("A", PAR["zg"], 24), ("V", 0, PAR["zg"])):
                if lo < hi:
                    by[e](T.ZG[:, 16 * lo:16 * hi], T.Z[:, 0:RW].indirect(T.GZ[:, lo:hi]), ["Z0", "RH0", "RH1", "GZ"], ["+ZG"])
            send("3", "ZG", "ZF", 128)

    for c in PAR["order"].split():
        loads(c)
        ready(c)
        step(c)
        close(c)
    assert len(done) == 8 and dense[0] == 32 and not chain["a"] and not chain["c"]

    assert ahead[1] == len(jobs) and not halves and not thirds and not held
    while offsets:
        close("i")
    cut, (ba, bb) = min(max(r, 1), 2), PAR["seen"].split()
    for j in range(3):
        for h in range(2):
            c = 512 + CAP * (j - cut) + 128 * h
            mm(ps(ba, c, c + 128), T.HS[:, 128 * h:128 * h + 128], T.ZF[:, 128 * j:128 * j + 128], ["HS", "ZF"], ["+" + (ba if j < cut else bb)])
    for lo, hi, bank in ((0, cut, ba), (cut, 3, bb)):
        tt(T.LIT[:, S + CAP * others[lo]:S + CAP * (others[lo] + hi - lo)], ps(ba, 512 + CAP * (lo - cut), 512 + CAP * (hi - cut)),
           T.BFO[:, CAP * lo:CAP * hi], OP.mult, [bank, "BFO"], ["+LIT"])

    win = T.LIT[:, 0:S + N * CAP]
    at("LIQ")["w"] += at("LIT")["w"][-1:]

    def on_vector(k, a, b, key):
        src = T.PRG if k == 0 else T.ACC
        tt(T.ACC[:, 16 * a:16 * b], win.indirect(T.HU[:, cv * k + a:cv * k + b]), src[:, 16 * a:16 * b], OP.add,
           ["LIT", "LIQ", "HU", "PRG"] + ([key] if k else []), [key])

    def store(lo, hi, keys, queues):
        for k in range(8):
            dma(queues[k % len(queues)], "dy", T.y[:, nv * k + lo:nv * k + hi], T.ACC[16 * k:16 * k + 16, lo:hi], keys, [])

    def gather(call):
        p1, n = call[0][3], 128 * sum(u[2] for u in call)
        key = "GA%d" % p1
        act(T.GA[:, p1 - (P - na):p1 - (P - na) + n], win.indirect(T.HU[:, p1 // 16:(p1 + n) // 16]), ["LIT", "LIQ", "HU"], [key])
        for i, c, nb, p in call:
            bank, c0, st = ("psE", "psF")[i % 2], p - (P - na), 4 // nb
            for b in range(nb):
                mm(ps(bank, c - first[i], c - first[i] + 16 * nb), T.GA[:, c0 + 128 * b:c0 + 128 * b + 128],
                   T.E4[:, 3 - st * b:67 - st * b:st], ["E4", key], ["+" + bank], b == 0, b == nb - 1)

    def width(i):
        return 16 * sum(sum(c) for c in sets[i])

    def back(i):
        m, bank, src, c = width(i), ("psD", "psB")[i % 2], ("psE", "psF")[i % 2], first[i]
        act(T.SUM[:, c:c + m], ps(src, 0, m), [src], ["SUM%d" % i])
        for x in range(0, m, 128):
            n = min(128, m - x)
            mm(ps(bank, x, x + 128, n), T.IDB[0:n, 0:n], T.PRA[0:n, c + x:c + x + 128], ["IDB", "PRA"], ["+" + bank], True, False)
            mm(ps(bank, x, x + 128, n), T.SUM[:, c + x:c + x + n], T.IDF[:], ["IDF", "SUM%d" % i], ["+" + bank], False, True)

    def out(i):
        m, bank, c = width(i), ("psD", "psB")[i % 2], first[i]
        n, w = min(m, 128), -(-m // 128) * 128
        act(T.OUT[0:n, c:c + w], ps(bank, 0, w, n), [bank], ["OUT%d" % i])

    def store_set(i):
        for j, c, nb, p1 in units:
            if j == i:
                dma("S", "dy", T.y[:, p1:p1 + 128 * nb], T.OUT[c % 128:c % 128 + 16 * nb, c - c % 128:c - c % 128 + 128], ["OUT%d" % i], [])

    def last(k, m):
        n, c0 = 16 * n2, na + 16 * n2 * k
        if k == 0:
            mm(ps("A", 0, n), T.IDB[:], T.PRG[:, nv - n:nv], ["IDB", "PRG"], ["+psA"], True, False)
        act(T.GA[:, c0:c0 + m * n], win.indirect(T.HU[:, 8 * cv + n2 * k:8 * cv + n2 * (k + m)]), ["LIT", "LIQ", "HU"], ["GL%d" % k])
        for x in range(m):
            mm(ps("A", 0, n), T.IDF[:], T.GA[:, c0 + x * n:c0 + x * n + n], ["IDF", "GL%d" % k], ["+psA"], False, k + x == 7)

    nth = {"S": 0, "L": 0, "b": 0, "o": 0}
    for c in PAR["flow"]:
        if c.isdigit():
            last(nth["L"], int(c))
            nth["L"] += int(c)
        elif c == "c":
            act(T.ACC[:, nv - 16 * n2:nv], ps("A", 0, 16 * n2), ["psA"], ["ACCc"])
        else:
            {"S": lambda n: gather(calls[n]), "b": back, "o": out}[c](nth[c])
            nth[c] += 1
    assert nth == {"S": len(calls), "L": 8, "b": len(sets), "o": len(sets)}
    cols, col = {}, 0
    for c, n in zip("xyzc", PAR["widths"] + (n2,)):
        cols[c], col = (col, col + n), col + n
    assert col == cw
    nxt = {"x": 0, "y": 0, "z": 0}
    for c in PAR["sums"]:
        on_vector(nxt[c], *cols[c], "ACC" + c)
        nxt[c] += 1
    for names, queues in PAR["stores"]:
        if names == "s":
            for i in range(len(sets)):
                store_set(i)
        else:
            store(16 * cols[names[0]][0], 16 * cols[names[-1]][1], ["ACC" + c for c in names], queues)

    for s in SEMAPHORES:
        wait("G" if s.startswith("sent") else "S", (s, None, "D"))
